import numpy as np, ml_dtypes
CORES = [13,21,141,149]
N = 4
BF = ml_dtypes.bfloat16
V, U, H, S, Q, P, ST, RO, NEED = 1280, 640, 128, 128, 2, 256, 128, 4, 9
def noisy(rng, base, part):
    return base[:, :, None, :] * (1 + part * (2 * rng.random((N, 8, 16, V)) - 1))
def detours(rng, m, share):
    hub = rng.integers(0, V, (N, 8, m)); h = np.take_along_axis(hub, rng.integers(0, m, (N, 8, 16 * U)), 2).reshape(N, 8, 16, U)
    p = np.where(rng.random((N, 8, 16, U)) < share, h, rng.integers(0, V, (N, 8, 16, U)))
    return p, rng.integers(0, V, (N, 8, 16, U))
def pack(x, p, q):
    x = x.astype(np.float32); x[..., V - H:] = np.roll(x, -1, axis=0)[..., :H]
    e = np.arange(U); p = np.where(p == e, (p + 1) % V, p)
    for i in range(2): q = np.where((q == e) | (q == p), (q + 1) % V, q)
    return {"dist": np.ascontiguousarray(x.reshape(N, 128, V)), "b1": np.ascontiguousarray(p.reshape(N, 128, U)).astype(np.int32), "b2": np.ascontiguousarray(q.reshape(N, 128, U)).astype(np.int32)}
def plain(rng):
    hot = rng.permuted(np.tile(np.array([0.03, 0.05, 0.07, 0.09, 0.12, 0.16, 0.25, 0.4]), (N, 1)), axis=1)[..., None]
    u, w = rng.random((N, 8, V)), rng.random((N, 8, V)); base = 0.8 + 0.4 * rng.random((N, 8, V))
    base = np.where(u < hot, 2 + 2.5 * w * w, np.where(u > 0.97, 0.25 + 0.25 * w, base))
    p, q = detours(rng, 24, 0.5)
    return noisy(rng, base, 0.15), p, q
def quiet(rng, n):
    x = 1 + 0.03 * (2 * rng.random((N, 16, V)) - 1); mid = U + np.argsort(rng.random((N, V - H - U)), axis=1); h = (V - H - U - n) // 2
    p = np.take_along_axis(mid[:, n:n + h], rng.integers(0, h, (N, 16 * U)), 1).reshape(N, 16, U)
    q = np.take_along_axis(mid[:, n + h:n + 2 * h], rng.integers(0, h, (N, 16 * U)), 1).reshape(N, 16, U)
    return x, p, q, mid[:, :n]
def ties(rng, size):
    n = 32; x, p, q, o = quiet(rng, 2 * n); kind = np.arange(n) % 4
    for r in range(N):
        e = rng.permutation(U)[:n]; one, two = o[r, :n], o[r, n:]
        m = rng.integers(192, 256, (16, n)) * 2 ** 16 + rng.integers(2 ** 10, 2 ** 15 - 2 ** 10, (16, n)) + 2 ** 15 * (kind == 3)
        j = rng.integers(2 ** 21, 2 ** 22, (16, n)); up = np.argsort(rng.random((16, n)), axis=0) < np.array([0, 8, 9, 16])[kind]
        x[r][:, e] = (m + up) * 2.0 ** -23; x[r][:, one] = (m - j - 1) * 2.0 ** -23; x[r][:, two] = (4 * j + 3) * 2.0 ** -25
        p[r][:, e] = one; q[r][:, e] = two
    return x * size, p, q
def still(rng):
    x, p, q, o = quiet(rng, Q + 3); f = 1 + 0.05 * rng.random((16, 1)); turn = int(rng.integers(0, 2))
    for r in range(N):
        if r % 2 != turn: continue
        i = rng.permutation(H)[:2 * Q]; a, b = np.sort(i[:Q]), i[Q:]
        x[r][:, a] = 10 * f; x[r][:, b] = f; x[r][:, o[r, :Q]] = f; p[r][:, a] = b; q[r][:, a] = o[r, :Q]
        x[r][:, o[r, Q:Q + 2]] = 8.0; p[r][:, b] = o[r, Q]; q[r][:, b] = o[r, Q + 1]
        s = (r - 1) % N; m = rng.random(U) < 0.05; m[:P * (RO - 1 - Q)] = False; m[ST * (RO - 1) % U] = True; m[U - 1] = True; e = np.nonzero(m)[0]
        x[s][:, e] = 5 * f; x[s, :, o[s, Q + 2]] = f[:, 0]; p[s][:, e] = V - H + b[(RO - 2) % Q]; q[s][:, e] = o[s, Q + 2]
    return x, p, q
def below(rng):
    n = 20; w = 2 * Q; k = 5 + 2 * (w - 3); x, p, q, o = quiet(rng, n * k); odd = np.arange(16) % 2
    for r in range(N):
        f = 1 + 0.05 * rng.random(16); e = np.sort(rng.permutation(ST)[:n * w]).reshape(n, w); spare = rng.permutation(n); d = o[r].reshape(n, k)
        for i in range(n):
            a, b, far = e[i, 0], e[i, 1], e[i, Q + 1]; c, y1, y2, w1, v = d[i, :5]; late = U - 1 - i
            for edge, size in ((a, 8.0), (b, 1.0), (far, 100.0), (c, 1.0), (y1, 0.25), (y2, 0.25), (w1, 1.0), (v, 8.4), (late, 8.0)): x[r, :, edge] = size * f
            if spare[i] < 16: x[r, spare[i], far] = 1.5 * f[spare[i]]
            p[r, :, a] = b; q[r, :, a] = np.where(odd == 1, v, c); p[r, :, b] = y1; q[r, :, b] = y2
            p[r, :, far] = c; q[r, :, far] = w1; p[r, :, late] = b; q[r, :, late] = v
            for j, edge in enumerate(np.delete(e[i], [0, 1, Q + 1])):
                x[r, :, edge] = 4 * f; p[r, :, edge] = d[i, 5 + 2 * j]; q[r, :, edge] = d[i, 6 + 2 * j]
    return x, p, q
def setup_inputs(rng):
    x, p, q = plain(rng)
    return pack(x, p, q)
def setup_inputs_spread(rng):
    base = np.exp2(6 * rng.random((N, 8, V)) - 3) * (rng.random((N, 8, V)) > 0.03125)
    p, q = detours(rng, 48, 0.3); x = noisy(rng, base, 0.25); gs = rng.permutation(8)
    x[:, gs[0]] *= 64.0; x[:, gs[1]] *= 2.0 ** -24
    for g, size in ((gs[2], 512.0), (gs[3], 2.0 ** -22)):
        x[:, g], p[:, g], q[:, g] = ties(rng, size)
    return pack(x, p, q)
def setup_inputs_ends(rng):
    typ = (np.arange(N)[:, None] + np.arange(8)[None, :]) % 2
    base = np.where(rng.random((N, 8, V)) < 0.35, 8.0, 0.125); base[:, 7, :P] = 8.0; base[:, :, U - 1] = 8.0
    base[:, :, 0] = np.where(typ == 0, 8.0, 0.125); base[:, :, H - 1] = np.where(typ == 1, 8.0, 0.125)
    x = base[:, :, None, :] * (1 - 0.05 * rng.random((N, 8, 16, V)))
    p, q = detours(rng, 24, 0.1)
    m = np.argsort(rng.random((N, 8, 16, U)), axis=2) < 11; a = (V - 1) * rng.integers(0, 2, (N, 8, 16, U))
    return pack(x, np.where(m, a, p), np.where(m, V - 1 - a, q))
def setup_inputs_corners(rng):
    wall = V - H - 1; x = noisy(rng, 0.7 + 0.2 * rng.random((N, 8, V)), 0.05)
    hub = rng.integers(U, wall, (N, 8, 16)); h = np.take_along_axis(hub, rng.integers(0, 16, (N, 8, 16 * U)), 2).reshape(N, 8, 16, U)
    p = np.where(rng.random((N, 8, 16, U)) < 0.5, h, rng.integers(U, wall, (N, 8, 16, U))); q = rng.integers(U, wall, (N, 8, 16, U))
    p = np.where(np.arange(16)[:, None] < rng.integers(0, 16, (N, 8, 1, U)), wall, p)
    m = rng.random((N, 8, U)) < 0.1; m[..., :P] = False; rows = np.ones((N, 8, 16, U), bool); w = rng.random((N, 8, 1, U))
    long = (2.2 + 3 * w * w) * (1 + 0.05 * (2 * rng.random((N, 8, 16, U)) - 1)); pairs = np.arange(32)
    late = int(rng.integers(0, 8)); fr = min(RO - 2, (U - 1) // P); e = slice(P * fr, P * fr + 16 * Q)
    for r in range(N):
        order = rng.permutation(8); i = int(np.argmax(order == 5)); order[i] = order[late]; order[late] = 5
        for g in range(8):
            kind = order[g]
            if kind < 5: m[r, g, rng.permutation(P)[:(S - 1, S, S + 1, P, 1)[kind]]] = True
            elif kind == 5 and r % 2 == 0:
                flip = np.repeat(rng.integers(0, 2, 16), 2); m[r, g, :32] = True
                p[r, g, :, :32] = U + np.repeat(rng.permutation(wall - U)[:16], 2)
                long[r, g, :, :32] = np.where(pairs % 2 == flip, 6.0, 2.2) * (1 + 0.05 * (2 * rng.random((16, 32)) - 1))
            elif kind == 5:
                m[r, g] = False; m[r, g, e] = True; o = U + rng.permutation(wall - U)[:16 + 16 * Q]
                c = o[16:].copy(); c[(RO - 1) % Q::Q] = V - H + 32 + rng.permutation(H - 32)[:16]
                p[r, g, :, e] = np.repeat(o[:16], Q); q[r, g, :, e] = c
                long[r, g, :, e] = np.where(np.arange(16 * Q) % Q == fr % Q, 6.0, 2.2) * (1 + 0.05 * (2 * rng.random((16, 16 * Q)) - 1))
            else:
                m[r, g, :P] = True; c = rng.choice(np.array([8, 9] if kind == 6 else [0, 9, 15, 16]), P)
                rows[r, g, :, :P] = np.argsort(rng.random((16, P)), axis=0) < c
    x[..., :U] = np.where(m[:, :, None, :] & rows, long, x[..., :U]); x[..., wall] = 8.0
    return pack(x, p, q)
def setup_inputs_calm(rng):
    x, p, q = plain(rng); og = rng.permutation(8); gs = og[:4]
    x[:, gs] = noisy(rng, 0.9 + 0.2 * rng.random((N, 8, V)), 0.05)[:, gs]
    for r in range(N):
        for i in range(4):
            c = np.concatenate([rng.permutation(ST)[:(i + r) % 4], U - 1 - rng.permutation(64)[:1]])
            x[r, gs[i], :, c] = 2.6 * (1 + 0.03 * (2 * rng.random((len(c), 16)) - 1))
    x[:, og[4]], p[:, og[4]], q[:, og[4]] = still(rng)
    x[:, og[5]], p[:, og[5]], q[:, og[5]] = below(rng)
    return pack(x, p, q)
def setup_inputs_crowd(rng):
    x = 0.25 * (rng.integers(4, 17, (N, 8, 1, V)) + rng.integers(0, 2, (N, 8, 16, V)))
    p, q = detours(rng, 24, 0.2)
    for r in range(N):
        for g in range(8):
            kind = (g + r) % 4; hs = U + rng.permutation(V - H - U)[:8]
            x[r, g, :, hs] = 0.25 * (1 + rng.integers(0, 2, (8, 16)))
            if kind < 2:
                e = rng.integers(0, P); a, b = p[r, g, :, e].copy(), q[r, g, :, e].copy()
                p[r, g] = hs[0]; q[r, g] = hs[1]
                if kind == 1: p[r, g, :, e] = a; q[r, g, :, e] = b
            elif kind == 2: p[r, g] = hs[0]
            else: p[r, g] = hs[rng.integers(0, 8, (16, U))]; q[r, g] = hs[rng.integers(0, 8, (16, U))]
    return pack(x, p, q)
def check_inputs(d):
    bad = []; x, p, q = np.asarray(d["dist"]), np.asarray(d["b1"]), np.asarray(d["b2"]); e = np.arange(U)
    if not np.all((x >= 0) & (x <= 1024)): bad.append("range of dist")
    if np.min(p) < 0 or np.max(p) > V - 1: bad.append("range of b1")
    if np.min(q) < 0 or np.max(q) > V - 1: bad.append("range of b2")
    if np.any((p == e) | (q == e) | (p == q)): bad.append("the three edges of a triple in b1 and b2 differ")
    if not np.array_equal(np.roll(x, -1, axis=0)[..., :H], x[..., V - H:]): bad.append("shared columns of dist")
    return bad
def reference(dist, b1, b2):
    D = dist.astype(np.float32).reshape(N, 8, 16, V); B1 = b1.astype(np.int64).reshape(N, 8, 16, U); B2 = b2.astype(np.int64).reshape(N, 8, 16, U)
    flag = np.ones((N, 8, U), bool); fill = np.zeros((N, 8, S), bool); tri = np.full((N, 8, 3, S), -1, np.int64); z = np.zeros((N, 8, 16, S), np.float32)
    for t in range(RO):
        corr = np.zeros((N, 8, 16, V), np.float32); touch = np.zeros((N, 8, V), bool); order = (ST * t + np.arange(U)) % U
        for r in range(N):
            for g in range(8):
                x = D[r, g]
                look = order[flag[r, g, order]][:P]; flag[r, g, look] = False
                c1, c2 = B1[r, g][:, look], B2[r, g][:, look]
                n = np.sum(x[:, look][:, None, :] > x[:, c1] + x[:, c2], axis=0)
                k = np.argmax(n, axis=0)
                who = np.nonzero(np.max(n, axis=0) >= NEED)[0]; free = np.nonzero(~fill[r, g])[0]
                m = min(len(who), len(free)); who, s = who[:m], free[:m]
                tri[r, g][0, s] = look[who]; tri[r, g][1, s] = c1[k[who], who]; tri[r, g][2, s] = c2[k[who], who]
                fill[r, g, s] = True; z[r, g][:, s] = 0
                vis = np.arange(t % Q, S, Q); vis = vis[fill[r, g, vis]]; w = tri[r, g][:, vis]
                least = np.full(V, S, np.int64); np.minimum.at(least, w, np.broadcast_to(vis, w.shape))
                st = vis[np.all(least[w] == vis, axis=0)]
                a, b, c = tri[r, g][:, st]; old = z[r, g][:, st]
                theta = ((x[:, a] - x[:, b]) - x[:, c]) * np.float32(0.5)
                delta = np.maximum(theta, -old); new = old + delta
                z[r, g][:, st] = new
                corr[r, g][:, a] = -delta; corr[r, g][:, b] = delta; corr[r, g][:, c] = delta
                touch[r, g, a] = True; touch[r, g, b] = True; touch[r, g, c] = True
                gone = st[np.all(new == 0, axis=0)]; fill[r, g, gone] = False; tri[r, g][:, gone] = -1
        nxt = D + corr
        for r in range(N):
            for q, mine, other in (((r - 1) % N, slice(0, H), slice(V - H, V)), ((r + 1) % N, slice(V - H, V), slice(0, H))):
                own, his = corr[r][..., mine], corr[q][..., other]
                one, two = (own, his) if r < q else (his, own)
                nxt[r][..., mine] = (D[r][..., mine] + one) + two
        D = nxt
        flag = flag | touch[..., :U]
        flag[:, :, :H] = flag[:, :, :H] | np.roll(touch, 1, axis=0)[..., V - H:]
    return {"yd": D.reshape(N, 128, V), "yz": z.reshape(N, 128, S), "yt": tri.reshape(N, 8, 3 * S).astype(np.float32), "yf": flag.astype(np.float32)}

@@ -1,0 +1,599 @@
+import math
+from concourse.bass import DstId, RemoteDMATransfer
+from concourse.mybir import AluOpType as A, AxisListType as AX, ActivationFunctionType as AF
+
+V, U, H, RO = 1280, 640, 128, 4
+NONE = 1280
+JUNK = 1288
+DW = JUNK + 192
+TW_ = 392
+P1 = 192
+CH = 32
+ALPHA = math.log(1.7)
+U0 = -6.0 - 272 * ALPHA
+SLOPE = 32776.0
+
+
+def code(x):
+    return 1 / (1 + math.exp(-(x - 512) / 8192))
+
+
+F32, BF, F16, I32, U16 = "float32", "bfloat16", "float16", "int32", "uint16"
+
+SCRATCH = {
+    "D": ("sbuf", [128, DW], F32), "B1i": ("sbuf", [128, U], I32), "B2i": ("sbuf", [128, U], I32),
+    "B1": ("sbuf", [128, 1032], F32), "B2": ("sbuf", [128, 1032], F32),
+    "O1": ("sbuf", [128, 256], U16), "O2": ("sbuf", [128, 256], U16),
+    "G2": ("sbuf", [128, 4096], F32), "S": ("sbuf", [128, 4096], F32),
+    "CM1": ("sbuf", [128, 16 * P1], BF), "CM2": ("sbuf", [128, 16 * (256 - P1)], BF), "G4": ("sbuf", [128, 4], F32),
+    "DE": ("sbuf", [128, 256], F32), "BF1": ("sbuf", [128, 256], F32), "BF2": ("sbuf", [128, 256], F32),
+    "VV": ("sbuf", [128, 256], BF), "WIN": ("sbuf", [128, 256], BF), "PR": ("sbuf", [128, 256], BF),
+    "WB": ("sbuf", [128, 256], F16), "WC": ("sbuf", [128, 256], F16), "TRASH": ("sbuf", [128, 12 * 256], BF),
+    "TR0": ("sbuf", [128, 3 * TW_], F32), "TR1": ("sbuf", [128, 3 * TW_], F32),
+    "ACC": ("sbuf", [128, 12], F32), "OO": ("sbuf", [128, 8], F32), "LG": ("sbuf", [128, 1024], F32), "OV": ("sbuf", [128, 4], F32),
+    "FB": ("sbuf", [128, 8], F32), "FW": ("sbuf", [128, 8], BF), "SL": ("sbuf", [128, 12], U16),
+    "XM": ("sbuf", [128, 192], F16), "XW": ("sbuf", [128, 192], F32), "XL": ("sbuf", [128, 12], U16),
+    "Z": ("sbuf", [128, 3, 128], F16), "E0": ("sbuf", [128, 144], BF), "E1": ("sbuf", [128, 288], BF),
+    "E2": ("sbuf", [128, 432], BF), "E3": ("sbuf", [128, 576], BF), "CF": ("sbuf", [128, 4], F32),
+    "TB": ("sbuf", [128, 12], F32), "OF": ("sbuf", [128, 12], F32), "OL": ("sbuf", [128, 12], U16),
+    "DV": ("sbuf", [128, 192], F32), "T1": ("sbuf", [128, 64], F32), "T2": ("sbuf", [128, 64], F32),
+    "M": ("sbuf", [128, 64], F32), "N2": ("sbuf", [128, 64], F32), "CO": ("sbuf", [128, 192], F32),
+    "NZ": ("sbuf", [128, 768], F32), "NZF": ("sbuf", [128, 64], BF), "I1": ("sbuf", [128, 4], F32), "I2": ("sbuf", [128, 4], F32),
+    "IL": ("sbuf", [128, 4], U16), "G1": ("sbuf", [128, 4], F32), "G3": ("sbuf", [128, 4], F32),
+    "SR": ("sbuf", [128, 8], F32), "WL": ("sbuf", [128, 8], U16),
+    "F": ("sbuf", [128, 40], BF), "SSa": ("sbuf", [128, 48], BF), "SSb": ("sbuf", [128, 48], BF),
+    "NF": ("sbuf", [128, 40], F32), "NG": ("sbuf", [128, 40], F32), "Q": ("sbuf", [128, 40], F32), "KP": ("sbuf", [128, 40], BF),
+    "PL": ("sbuf", [128, 40], U16), "NN": ("sbuf", [128, 2], F32), "LW": ("sbuf", [128, 256], F32),
+    "VL": ("sbuf", [128, 16], U16), "EA": ("sbuf", [128, 16], F32), "EB": ("sbuf", [128, 16], F32), "EL": ("sbuf", [128, 16], U16),
+    "PI": ("sbuf", [128, 2], I32), "PJ": ("sbuf", [128, 2], I32), "PC": ("sbuf", [128, 4], F32),
+    "J16": ("sbuf", [128, 256], F32), "R": ("sbuf", [128, 256], F32), "ET": ("sbuf", [128, 1032], F32),
+    "M16": ("sbuf", [128, 128], F32), "WD": ("sbuf", [128, 144], BF), "BO": ("sbuf", [128, 128], BF), "BH": ("sbuf", [128, 128], F16),
+    "BT": ("sbuf", [128, 128], BF), "TI": ("sbuf", [128, 128], BF), "TG": ("sbuf", [128, 128], BF), "TX": ("sbuf", [128, 128], BF),
+    "IK": ("sbuf", [128, 128], BF), "UV": ("sbuf", [128, 192], BF), "ONE": ("sbuf", [128, 256], BF), "IM": ("sbuf", [128, 64], F32),
+    "MB": ("sbuf", [128, 256], F32), "RS": ("sbuf", [128, 192], F16), "ZM": ("sbuf", [128, 128], F32), "CR": ("sbuf", [128, 40], F32),
+    "JK": ("sbuf", [128, 40], F32), "J12": ("sbuf", [128, 12], F32), "K1": ("sbuf", [128, 8], F32), "K2": ("sbuf", [128, 8], F32),
+    "QT": ("sbuf", [128, 4], F32), "SEL": ("sbuf", [128, 128], BF), "SE0": ("sbuf", [128, 8], F32),
+    "BIG": ("sbuf", [128, 192], F32), "TS": ("sbuf", [128, RO * H], BF), "TH": ("sbuf", [128, U], BF),
+    "YZ": ("sbuf", [128, 128], F32), "YT": ("sbuf", [128, 384], F32), "YF": ("sbuf", [128, 640], F32),
+    "LL": ("sbuf", [128, RO * H], F32), "LR": ("sbuf", [128, RO * H], F32), "LT": ("sbuf", [128, RO * H], BF),
+}
+for _t in range(RO):
+    SCRATCH["C%d" % _t] = ("sbuf", [128, DW], F32)
+    SCRATCH["TW%d" % _t] = ("sbuf", [128, DW], F32)
+for _t in range(1, RO):
+    SCRATCH["L%d" % _t] = ("sbuf", [128, V], F32)
+for _b in range(8):
+    SCRATCH["P%d" % _b] = ("psum", [128, 512], F32)
+
+SEMAPHORES = (["qv", "qa", "qp", "qg", "ls"] + ["dma%d" % i for i in range(16)]
+              + [n + str(t) for t in range(RO) for n in ("al", "ar", "at")])
+
+
+def relays(T, topo, rank):
+    n = len(T.cores); me = T.cores[rank]; left, right = T.cores[(rank - 1) % n], T.cores[(rank + 1) % n]
+    able = [c for c in topo.cores_of(me) if c != me and topo.may_write(c, left) and topo.may_write(c, right)]
+    near = [c for c in able if topo.die(c) == topo.die(me)]; other = [c for c in able if topo.die(c) != topo.die(me)]
+    return near[0], other[0], near[1]
+
+
+def mask_of(engines):
+    m = 0
+    for e in engines:
+        m |= 1 << e
+    return m
+
+
+def relay_program(g, core, T, topo):
+    n = len(T.cores)
+    for rank in range(n):
+        roles = relays(T, topo, rank)
+        if core not in roles:
+            continue
+        role = roles.index(core)
+        dst = T.cores[(rank - 1) % n] if role == 0 else T.cores[(rank + 1) % n]
+        buf, sem = (("LR", "ar"), ("LL", "al"), ("LT", "at"))[role]
+        rid, pid = topo.addr(dst, core); m = topo.mask(core, dst); k = len(topo.engines(core, dst))
+        for t in range(RO):
+            piece = T[buf][:, t * H:(t + 1) * H]
+            g.wait_ge(T.sem[sem + str(t)], len(topo.engines(T.cores[rank], core)) // 2)
+            g.remote_dma(piece, piece, T.sem[sem + str(t)], T.sem.ls, pid, rid, m)
+        g.wait_ge(T.sem.ls, k * RO)
+
+
+def emit(g, T, ops):
+    queue = {"v": g.vector, "a": g.scalar, "p": g.tensor, "g": g, "s": g.sync}
+    last_w, readers, deps = {}, {}, []
+    for i, (eng, fn, rd, wr, sem) in enumerate(ops):
+        d = set()
+        own = lambda j: ops[j][0] == eng and ops[j][4] is None and sem is None
+        for k in rd:
+            if k in last_w: d.add(last_w[k])
+            if k[0] == "#":
+                d.update(j for j in readers.get(k, ()) if not own(j))
+        for k in wr:
+            if k in last_w and not (k[0] == "#" and own(last_w[k])): d.add(last_w[k])
+            d.update(readers.get(k, ()))
+        for k in rd: readers.setdefault(k, []).append(i)
+        for k in wr:
+            last_w[k] = i; readers[k] = []
+        deps.append(d)
+    line = lambda j: ops[j][0] if ops[j][4] is None else "x%d" % j
+    clock, known, waits = {}, {}, []
+    for i, (eng, fn, rd, wr, sem) in enumerate(ops):
+        kn = known.setdefault(eng, {}); w = []
+        top = {}
+        for j in deps[i]:
+            if top.get(line(j), -1) < j: top[line(j)] = j
+        for j in sorted(top.values(), reverse=True):
+            if kn.get(line(j), -1) >= j: continue
+            w.append(j)
+            for k, x in clock[j].items():
+                if kn.get(k, -1) < x: kn[k] = x
+        waits.append(w)
+        c = dict(kn); c[line(i)] = i; clock[i] = c
+    needed = set(j for w in waits for j in w)
+    count, value = {}, {}
+    for i, (eng, fn, rd, wr, sem) in enumerate(ops):
+        if sem is not None: value[i] = sem
+        elif i in needed:
+            count[eng] = count.get(eng, 0) + 1; value[i] = ("q" + eng, count[eng])
+    for i, (eng, fn, rd, wr, sem) in enumerate(ops):
+        if eng == "x": continue
+        for j in waits[i]: queue[eng].wait_ge(T.sem[value[j][0]], value[j][1])
+        if fn is None: continue
+        r = fn()
+        if sem is not None: r.then_inc(T.sem[sem[0]], sem[1])
+        elif i in needed: r.then_inc(T.sem[value[i][0]], 1)
+
+
+def rank_program(g, core, T, topo):
+    rank = T.rank_of(core)
+    if rank is None:
+        return relay_program(g, core, T, topo)
+    n = len(T.cores)
+    ops = []
+    ndma = [0]; later = []
+    rl, rrt, rt = relays(T, topo, rank)
+    eng_chip = topo.engines(core, rl); half = len(eng_chip) // 2
+    far = len(topo.engines(rl, T.cores[(rank - 1) % n]))
+    v, a, pe = g.vector, g.scalar, g.tensor
+
+    def op(eng, fn, rd, wr): ops.append((eng, fn, rd.split(), wr.split(), None))
+    def dma(eng, out, in_, rd, wr):
+        q = g.sync if eng == "s" else g.scalar
+        ops.append((eng, lambda: q.dma_start(out, in_), rd.split(), wr.split(), ("dma%d" % ndma[0], 16))); ndma[0] += 1
+    def arrival(sem, wr): ops.append(("x", None, [], [wr], (sem, far)))
+    def cp(out, in_, rd, wr): op("v", lambda: v.tensor_copy(out, in_), rd, wr)
+    def tt(out, x, y, o, rd, wr): op("v", lambda: v.tensor_tensor(out, x, y, o), rd, wr)
+    def ts(out, x, s1, o0, rd, wr): op("v", lambda: v.tensor_scalar(out, x, s1, None, o0), rd, wr)
+    def ts2(out, x, s1, o0, s2, o1, rd, wr): op("v", lambda: v.tensor_scalar(out, x, s1, s2, o0, o1), rd, wr)
+    def scan(out, x, y, init, o0, o1, rd, wr): op("v", lambda: v.tensor_tensor_scan(out, x, y, init, o0, o1), rd, wr)
+    def fill(ap, c, wr): op("v", lambda: v.memset(ap, c), "", wr)
+    def act(out, in_, rd, wr, f=AF.Identity, **kw): op("a", lambda: a.activation(out, in_, f, **kw), rd, wr)
+    def mm(out, l, r, st, sp, rd, wr): op("p", lambda: pe.matmul(out, l, r, st, sp), rd, wr)
+    def iota(out, pat, base, cm, wr, whole=False):
+        if whole: op("g", lambda: g.iota(out, pat, base, cm), "", wr)
+        else: op("g", lambda: g.iota(out, pat, base, cm, allow_small_or_imprecise_dtypes=True), "", wr)
+    def sel(out, in_, pat, o, base, cm, rd, wr, c=0.0): op("g", lambda: g.affine_select(out, in_, pat, o, c, base, cm), rd, wr)
+    P = [T["P%d" % b] for b in range(8)]
+    W = lambda k: T.WD[:, 15 - k:143 - k]
+    Dr = T.D[:, 0:JUNK]; DD = "Dl Dm Dr Dx"
+    NL = 256 - P1
+
+    dma("s", T.B2i[:, 0:256], T.b2[:, 0:256], "", "B2i0")
+    dma("a", T.B1i[:, 0:256], T.b1[:, 0:256], "", "B1i0")
+    dma("s", T.D[0:64, 0:V], T.dist[0:64, :], "", "Dl Dm Dr")
+    dma("a", T.D[64:128, 0:V], T.dist[64:128, :], "", "Dn")
+    dma("s", T.B2i[:, 256:U], T.b2[:, 256:U], "Dm Dn", "B2i1")
+    dma("s", T.B1i[:, 256:U], T.b1[:, 256:U], "", "B1i1")
+
+    iota(T.PI[:, 0:1], [[0, 1]], 0, 1, "PI", whole=True)
+    iota(T.M16[:], [[16, 8], [0, 16]], 0, 0, "M16")
+    iota(T.J16[:], [[0, 16], [1, 16]], 0, 0, "J16")
+    iota(T.R[:, 0:256], [[1, 256]], 0, 0, "R0")
+    iota(T.CR[:], [[16, 40]], 0, 0, "CR")
+    iota(T.FB[:], [[1, 2], [32, 4]], 0, 0, "FB")
+    fill(T.D[:, V:JUNK], 1e29, "Dx")
+    fill(T.UV[:], math.exp(U0 + 137 * ALPHA) / 16, "UV")
+    fill(T.QT[:], 0.25, "QT")
+    for b0, b1 in ((1, 2), (3, 5), (6, 7)):
+        fill(T.ZM[:, 16 * b0:16 * b1], 0.0, "ZM%d" % b0)
+    iota(T.ONE[:], [[0, 256]], 1, 0, "ONE")
+    iota(T.OO[:], [[0, 8]], 128, 0, "OO")
+    for f in range(3):
+        iota(T.TR0[:, f * TW_:f * TW_ + 128], [[0, 128]], NONE, 0, "TRo0%d" % f)
+    iota(T.TR0[:, 384::TW_], [[0, 3]], NONE, 0, "TRx0"); iota(T.TR1[:, 384::TW_], [[0, 3]], NONE, 0, "TRx1")
+    iota(T.BIG[:], [[0, 192]], 30, 0, "BIG")
+    iota(T.NZ[:, 64:128], [[0, 64]], 0, 0, "NZo0"); iota(T.NZ[:, 192:256], [[0, 64]], 0, 0, "NZo1")
+    iota(T.F[:, 0:16], [[0, 16]], 0, 0, "Fa Fb Fc")
+    iota(T.SSa[:, 0:1], [[0, 1]], 0, 0, "SSa0"); iota(T.SSb[:, 0:1], [[0, 1]], 0, 0, "SSb0")
+    ts(T.PJ[:, 0:1], T.PI[:, 0:1], 15, A.bitwise_and, "PI", "PJ0")
+    ts(T.PJ[:, 1:2], T.PI[:, 0:1], 112, A.bitwise_and, "PI", "PJ1")
+    cp(T.PC[:, 0:2], T.PJ[:], "PJ0 PJ1", "PC")
+    rr, gg = T.PC[:, 0:1], T.PC[:, 1:2]
+    ts2(T.PC[:, 2:3], rr, -ALPHA, A.mult, U0, A.add, "PC", "PC2")
+    ts(T.PC[:, 3:4], gg, 15.0, A.add, "PC", "PC3")
+    ts(T.BO[:], T.M16[:], gg, A.is_equal, "M16 PC", "BO")
+    ts(T.BH[:], T.M16[:], gg, A.is_equal, "M16 PC", "BH")
+    ts2(T.BT[:], T.M16[:], gg, A.is_equal, 0.390625, A.mult, "M16 PC", "BT")
+    ts(T.IM[:], T.J16[:, 0:64], rr, A.is_equal, "J16 PC", "IM")
+    ts(P[7][:, 256:256 + H], T.J16[:, 0:H], rr, A.is_equal, "J16 PC", "#7")
+    ts(T.RS[:], T.J16[:, 0:192], 0.5, A.is_gt, "J16", "RS")
+    for b in (0, 2, 5, 7):
+        ts2(T.ZM[:, 16 * b:16 * b + 16], T.J16[:, 0:16], rr, A.is_ge, float(NONE), A.mult, "J16 PC", "ZM%d" % b)
+    ts2(T.MB[:], T.J16[:], rr, A.is_equal, 4096.0, A.mult, "J16 PC", "MB")
+    ts2(T.WD[:], T.R[:, 0:144], T.PC[:, 3:4], A.is_equal, 0.0625, A.mult, "R0 PC3", "WD")
+    ts(T.CR[:], T.CR[:], rr, A.add, "CR PC", "CR")
+    ts2(T.FB[:], T.FB[:], rr, A.add, rr, A.add, "FB PC", "FB")
+    cp(T.O2[:], T.B2i[:, 0:256], "B2i0", "O2a O2b")
+    cp(T.O1[:], T.B1i[:, 0:256], "B1i0", "O1")
+    cp(P[1][:, 0:256], T.B1i[:, 0:256], "B1i0", "#1")
+    cp(P[1][:, 256:512], T.B2i[:, 0:256], "B2i0", "#1")
+    act(T.FB[:], T.FB[:], "FB", "FB", scale=40.0, bias=20.0)
+    act(T.JK[:], T.CR[:], "CR", "JK", bias=float(U))
+    act(T.J12[:], T.CR[:, 0:12], "CR", "J12", bias=float(JUNK))
+    act(T.K1[:], T.CR[:, 0:8], "CR", "K1", scale=-1.0, bias=384.0)
+    act(T.K2[:], T.CR[:, 0:8], "CR", "K2", bias=-256.0)
+    zm = " ZM0 ZM1 ZM2 ZM3 ZM5 ZM6 ZM7"
+
+    def zeros(t):
+        C, TW = T["C%d" % t], T["TW%d" % t]
+        iota(C[:, 0:H], [[0, H]], 0, 0, "C%d" % t); iota(C[:, V - H:V], [[0, H]], 0, 0, "C%d" % t)
+        iota(TW[:, 0:U], [[0, U]], 0, 0, "TW%d" % t); iota(TW[:, V - H:V], [[0, H]], 0, 0, "TW%d" % t)
+    zeros(0)
+    sel(T.TI[:], T.BO[:], [[1, 128]], A.is_ge, 0, -1, "BO", "TI")
+    sel(T.TG[:], T.BO[:], [[-1, 128]], A.is_gt, 0, 1, "BO", "TG")
+    sel(T.TX[:], T.BO[:], [[1, 128]], A.is_gt, 0, -1, "BO", "TX")
+    iota(T.IK[:], [[0, 128]], -384, 0, "IK")
+    sel(T.IK[:], T.IK[:], [[-1, 128]], A.is_equal, 0, 1, "IK", "IK")
+    iota(T.LG[:], [[1, 1024]], -512, 0, "LG")
+    iota(T.L1[:, 0:256], [[0, 256]], 1024, 0, "L1")
+    iota(T.ET[:, 0:U], [[1, U]], 0, 0, "ET"); iota(T.ET[:, U:1032], [[1, 392]], 0, 0, "ET")
+    iota(T.B1[:, 1024:1032], [[0, 8]], NONE, 0, "B1x"); iota(T.B2[:, 1024:1032], [[0, 8]], NONE, 0, "B2x")
+
+    def late_constants(t):
+        if t + 1 < RO: zeros(t + 1)
+        if t + 2 < RO: sel(T["L%d" % (t + 2)][:, 0:256], T.R[:], [[0, 256]], A.is_gt, 0, 0, "R0", "L%d" % (t + 2), code(1024))
+        if t == 2:
+            sel(T.SEL[:], T.ONE[:, 0:128], [[-1, 16], [-16, 8]], A.is_equal, 0, 1, "ONE", "SEL")
+            iota(T.SE0[:], [[0, 8]], 1, 0, "SE0")
+            sel(T.SE0[:], T.SE0[:], [[-16, 8]], A.is_equal, 0, 1, "SE0", "SE0")
+
+    lower = (rank < (rank - 1) % n, rank < (rank + 1) % n)
+    sides = ((0, "Dl", "LL"), (V - H, "Dr", "LR"))
+
+    BB1, BB2 = "B10 B11 B1m B1x", "B20 B21 B2m B2x"
+
+    def lists(first=False):
+        if first:
+            cp(T.O2[:], T.B2i[:].indirect(T.VL[:]), "B2i0 B2i1 VL", "O2a O2b")
+            cp(T.O1[:], T.B1i[:].indirect(T.VL[:]), "B1i0 B1i1 VL", "O1")
+            return
+        cp(T.O2[:, 0:64], T.B2[:].indirect(T.VL[:, 0:4]), BB2 + " VL", "O2a")
+        cp(T.O2[:, 64:256], T.B2[:].indirect(T.VL[:, 4:16]), BB2 + " VL", "O2b")
+        cp(T.O1[:], T.B1[:].indirect(T.VL[:]), BB1 + " VL", "O1")
+
+    def table(i):
+        name, h = ("B2", "B1")[i // 2], i % 2
+        cp(T[name][:, 320 * h:320 * h + 320], T[name + "i"][:, 320 * h:320 * h + 320], "%si0 %si1" % (name, name), "%s%d" % (name, h))
+
+    def own_numbers(i):
+        if i == 0:
+            ts2(T.EA[:], T.LW[:, 15::16], code(U - 0.5), A.is_gt, -float(U), A.mult, "LW", "EA")
+            ts2(T.EB[:], T.LW[:, 15::16], SLOPE, A.mult, 512.25 - SLOPE / 2, A.add, "LW", "EB")
+        if i == 1: tt(T.EB[:], T.EA[:], T.EB[:], A.add, "EA EB", "EB")
+        if i == 2: cp(T.EL[:], T.EB[:], "EB", "EL")
+
+    def fix(t):
+        C = T["C%d" % t]
+        def first(s):
+            c0, tok, land = sides[s]; his = T[land][:, t * H:(t + 1) * H]
+            if lower[s]: tt(T.D[:, c0:c0 + H], P[0][:, s * H:(s + 1) * H], his, A.add, "#0 %s%d" % (land, t), tok)
+            else: tt(P[1][:, s * H:(s + 1) * H], P[0][:, s * H:(s + 1) * H], his, A.add, "#0 %s%d" % (land, t), "#1")
+        def second(s):
+            c0, tok, land = sides[s]
+            if not lower[s]: tt(T.D[:, c0:c0 + H], P[1][:, s * H:(s + 1) * H], C[:, c0:c0 + H], A.add, "#1 C%d" % t, tok)
+        s = 0 if lower[1] else 1
+        return [lambda: first(s), lambda: first(1 - s), lambda: second(s), lambda: second(1 - s)]
+
+    for t in range(RO):
+        par = t % 2; TR, TRn = T["TR%d" % par], T["TR%d" % (1 - par)]; C, TW = T["C%d" % t], T["TW%d" % t]
+        DX = DD + (" Dn" if t == 0 else "")
+        new = lambda f, e0, e1: TR[:, f * TW_ + 128 + e0:f * TW_ + 128 + e1]
+        tri = lambda f: "TRo%d%d TRx%d TRn%d0 TRn%d1" % (par, f, par, f, f)
+
+        def g2(i):
+            act(T.G2[:, 16 * CH * i:16 * CH * (i + 1)], Dr.indirect(T.O2[:, CH * i:CH * (i + 1)]),
+                DX + (" O2a" if CH * (i + 1) <= 64 else " O2b"), "G2%d" % i)
+        def add(i):
+            e0 = CH * i
+            tt(T.S[:, 16 * e0:16 * (e0 + CH)], Dr.indirect(T.O1[:, e0:e0 + CH]), T.G2[:, 16 * e0:16 * (e0 + CH)], A.add,
+               DX + " O1 G2%d" % i, "S%d" % i)
+        n1 = P1 // CH; nc = 256 // CH
+        if t == 0: cp(P[0][:, 0:256], T.D[:, 0:256], DX, "#0")
+        if t == 1:
+            cp(T.DE[:], Dr.indirect(T.VL[:]), DX + " VL", "DE")
+            later.pop()()
+            cp(P[0][:, 0:256], T.DE[:], "DE", "#0")
+        for i in range(n1):
+            if t > 1 and i < 3: own_numbers(i)
+            g2(i); add(i)
+        if t > 1:
+            act(T.DE[:], Dr.indirect(T.EL[:]), DX + " EL", "DE")
+            act(P[0][:, 0:256], T.DE[:], "DE", "#0")
+        for i in range(n1, nc): g2(i)
+        if t > 1: later.pop()()
+        s1 = " ".join("S%d" % i for i in range(n1)); s2 = " ".join("S%d" % i for i in range(n1, nc))
+        for k in range(16):
+            tt(T.CM1[:, k * P1:(k + 1) * P1], P[0][:, 0:P1], T.S[:, k:16 * P1:16], A.is_gt, "#0 " + s1, "CM1%d" % k)
+            mm(P[2][:, 0:P1], W(k), T.CM1[:, k * P1:(k + 1) * P1], k == 0, k == 15, "WD CM1%d" % k, "#2")
+        if t == 1:
+            act(T.BF1[:], T.B1[:, 0:U].indirect(T.VL[:]), "B10 B11 VL", "BF1")
+            act(T.BF2[:], T.B2[:, 0:U].indirect(T.VL[:]), "B20 B21 VL", "BF2")
+            act(P[1][:, 0:256], T.BF1[:], "BF1", "#1")
+            act(P[1][:, 256:512], T.BF2[:], "BF2", "#1")
+        if t > 1:
+            act(T.BF1[:], T.B1[:].indirect(T.VL[:]), BB1 + " VL", "BF1")
+            act(T.BF2[:], T.B2[:].indirect(T.VL[:]), BB2 + " VL", "BF2")
+            act(P[1][:, 0:256], T.BF1[:], "BF1", "#1")
+            act(P[1][:, 256:512], T.BF2[:], "BF2", "#1")
+        late_constants(t)
+
+        def weigh(h, e0, e1, nb, sb):
+            m = e1 - e0
+            mm(P[sb][:, 0:m], T.BT[:], T.UV[:, 0:m], True, False, "BT UV", "#%d" % sb)
+            act(T.VV[:, e0:e1], P[nb][:, 0:m], "#%d PC2" % nb, "VV%d" % h, f=AF.Sigmoid, bias=T.PC[:, 2:3], scale=16 * 17 * ALPHA)
+            mm(P[sb][:, 0:m], T.BT[:], T.VV[:, e0:e1], False, True, "BT VV%d" % h, "#%d" % sb)
+        def choose(h, e0, e1, sb):
+            m = e1 - e0
+            tt(T.WIN[:, e0:e1], T.VV[:, e0:e1], P[sb][:, 0:m], A.is_gt, "VV%d #%d" % (h, sb), "WIN%d" % h)
+            mm(P[4][:, 0:m], T.BO[:], T.WIN[:, e0:e1], True, True, "BO WIN%d" % h, "#4")
+        def ranks(h, e0, e1):
+            m = e1 - e0
+            scan(T.PR[:, e0:e1], T.ONE[:, 0:m], P[4][:, 0:m], T.PR[:, e0 - 1:e0] if h else 0.0, A.mult, A.add,
+                 "ONE #4" + (" PR0" if h else ""), "PR%d" % h)
+        def pick(h, e0, e1):
+            m = e1 - e0
+            tt(T.WB[:, e0:e1], T.WIN[:, e0:e1], P[1][:, e0:e1], A.mult, "WIN%d #1" % h, "WB%d" % h)
+            tt(T.WC[:, e0:e1], T.WIN[:, e0:e1], P[1][:, 256 + e0:256 + e1], A.mult, "WIN%d #1" % h, "WC%d" % h)
+            bank = 5 if h == 0 else 3
+            mm(P[bank][:, 0:m], T.BH[:], T.WB[:, e0:e1], True, True, "BH WB%d" % h, "#%d" % bank)
+            mm(P[bank][:, 256:256 + m], T.BH[:], T.WC[:, e0:e1], True, True, "BH WC%d" % h, "#%d" % bank)
+        def count(e0, e1, col, to, rd):
+            act(T.TRASH[:, 256 * to:256 * to + e1 - e0], T.PR[:, e0:e1], rd + " FB", "ACC%d" % to, f=AF.Sigmoid, bias=T.FB[:, col:col + 1], scale=-40.0,
+                accum_out=T.ACC[:, to:to + 1])
+
+        weigh(0, 0, P1, 2, 3)
+        if t: act(new(0, 0, 256), T.ET[:].indirect(T.VL[:]), "ET VL", "TRn00 TRn01")
+        else: act(new(0, 0, 256), T.R[:, 0:256], "R0", "TRn00 TRn01")
+        add(n1)
+        choose(0, 0, P1, 3)
+        for i in range(n1 + 1, nc): add(i)
+        ranks(0, 0, P1)
+        if t == 0: act(T.LG[:], T.LG[:], "LG", "LG", scale=1.0 / 8192)
+        if t == 1:
+            act(T.B2[:, U:1024], T.B2[:, 0:384], "B20 B21", "B2m")
+            act(T.B1[:, U:1024], T.B1[:, 0:384], "B10 B11", "B1m")
+        for c in range(4): count(0, P1, 4 * par + c, 8 + c, "PR0")
+        for k in range(16):
+            tt(T.CM2[:, k * NL:(k + 1) * NL], P[0][:, P1:256], T.S[:, 16 * P1 + k::16], A.is_gt, "#0 " + s2, "CM2%d" % k)
+            mm(P[6][:, 0:NL], W(k), T.CM2[:, k * NL:(k + 1) * NL], k == 0, k == 15, "WD CM2%d" % k, "#6")
+        weigh(1, P1, 256, 6, 7)
+        pick(0, 0, P1)
+        act(new(1, 0, P1), P[5][:, 0:P1], "#5", "TRn10")
+        choose(1, P1, 256, 7)
+        tt(T.OV[:], T.OO[:, 4 * par:4 * par + 4], T.ACC[:, 8:12], A.add, "OO ACC8 ACC9 ACC10 ACC11", "OV")
+        pick(1, P1, 256)
+        ranks(1, P1, 256)
+        for c in range(4): count(P1, 256, 4 * par + c, 4 * par + c, "PR1")
+        act(new(2, 0, P1), P[5][:, 256:256 + P1], "#5", "TRn20")
+        cp(new(1, P1, 256), P[3][:, 0:NL], "#3", "TRn11")
+        cp(new(2, P1, 256), P[3][:, 256:256 + NL], "#3", "TRn21")
+        for c, (p0, p1, st) in ((0, (0, 1, 1)), (0, (5, 12, 3)), (1, (1, 8, 3)), (2, (2, 11, 4)), (3, (3, 10, 6))):
+            m = len(range(p0, p1, st)); col = 4 * par + c
+            ts2(T.SL[:, p0:p1:st], T.QT[:, 0:m], T.ACC[:, col:col + 1], A.add, T.OV[:, c:c + 1], A.add, "QT OV ACC%d" % col, "SL%d" % p0)
+        sl = " SL0 SL5 SL1 SL2 SL3"
+        for s, (c0, tok, land) in enumerate(sides):
+            if not lower[s]: act(P[0][:, s * H:(s + 1) * H], T.D[:, c0:c0 + H], tok, "#0")
+        win = lambda f: TR[:, f * TW_:f * TW_ + 385]
+        for f in range(3):
+            tt(T.XM[:, 64 * f:64 * f + 64], win(f).indirect(T.SL[:, 0:4]), T.IM[:], A.mult, tri(f) + sl + " IM", "XM%d" % f)
+        tt(T.Z[:, 0, :], win(0).indirect(T.SL[:, 4:12]), T.ZM[:], A.max, tri(0) + sl + zm, "Z0")
+        scan(T.XW[:], T.RS[:], T.XM[:], 0.0, A.mult, A.add, "RS XM0 XM1 XM2", "XW")
+        tt(T.Z[:, 1, :], win(1).indirect(T.SL[:, 4:12]), T.ZM[:], A.max, tri(1) + sl + zm, "Z1")
+        cp(T.XL[:], T.XW[:, 15::16], "XW", "XL")
+        tt(T.Z[:, 2, :], win(2).indirect(T.SL[:, 4:12]), T.ZM[:], A.max, tri(2) + sl + zm, "Z2")
+        act(T.DV[:], Dr.indirect(T.XL[:]), DX + " XL", "DV")
+        for c, (b0, b1) in ((3, (3, 7)), (2, (2, 5)), (1, (0, 2)), (0, (7, 8))):
+            E = T["E%d" % c]; m = 48 * (c + 1)
+            for f in range(3):
+                x = 64 * f + 16 * c + 15
+                ts2(E[:, f * m:(f + 1) * m], T.Z[:, :, 16 * b0:16 * b1], T.XW[:, x:x + 1], A.is_equal, 4096.0, A.mult, "Z0 Z1 Z2 XW", "E%d%d" % (c, f))
+            if c >= 2:
+                act(E[:], E[:], "E%d0 E%d1 E%d2" % (c, c, c), "CF%d E%d0 E%d1 E%d2" % (c, c, c, c), accum_out=T.CF[:, c:c + 1])
+        def red(c): op("v", lambda: v.tensor_reduce(T.CF[:, c:c + 1], T["E%d" % c][:], AX.X, A.add), "E%d0 E%d1 E%d2" % (c, c, c), "CF%d" % c)
+        def bad(c): ts(T.TB[:, c::4], T.J12[:, c::4], T.CF[:, c:c + 1], A.min, "J12 CF%d" % c, "TB%d" % c)
+        th1 = lambda: tt(T.T1[:], T.DV[:, 0:64], T.DV[:, 64:128], A.subtract, "DV", "T1")
+        th2 = lambda: tt(T.T2[:], T.T1[:], T.DV[:, 128:192], A.subtract, "T1 DV", "T2")
+        def th3():
+            if t < 2: ts(T.M[:], T.T2[:], 0.0, A.max, "T2", "M")
+            else: tt(T.M[:], T.T2[:], T.N2[:], A.max, "T2 N2", "M")
+        tb = "TB0 TB1 TB2 TB3"; co = "CO0 CO1 CO2"
+        i1 = lambda: ts2(T.I1[:], T.TB[:, 0:4], 0.5, A.is_gt, 64.0, A.mult, tb, "I1")
+        i2 = lambda: tt(T.I2[:], T.I1[:], T.CR[:, 0:4], A.add, "I1 CR", "I2")
+        sr2 = lambda: tt(T.G1[:], T.ACC[:, 4 * par:4 * par + 4], T.OV[:], A.add, "OV " + " ".join("ACC%d" % (4 * par + c) for c in range(4)), "G1")
+        urgent = t in (1, 2)
+        if urgent:
+            red(1); red(0); th1()
+        else:
+            th1(); red(1); th2(); red(0); th3()
+            for f in range(3): act(T.CO[:, 64 * f:64 * f + 64], T.M[:], "M", "CO%d" % f, scale=0.5 if f else -0.5)
+        bad(1); bad(0); bad(3); bad(2)
+        tt(T.OF[:], T.TB[:], T.XW[:, 15::16], A.max, tb + " XW", "OF")
+        cp(T.OL[:], T.OF[:], "OF", "OL")
+
+        th = 256 if t == 0 else U
+        def touches():
+            act(TW[:].indirect(T.OL[:]), T.BIG[:], "BIG OL", "TW%d" % t, f=AF.Sigmoid)
+            act(T.TH[:, 0:th], TW[:, 0:th], "TW%d" % t, "TH")
+        def send_touches():
+            tt(T.TS[:, t * H:(t + 1) * H], TW[:, V - H:V], P[7][:, 256:256 + H], A.mult, "TW%d #7" % t, "TS%d" % t)
+            rid, pid = topo.addr(rt, core)
+            op("g", lambda t=t: g.remote_dma(T.LT[:, t * H:(t + 1) * H], T.TS[:, t * H:(t + 1) * H], T.sem["at%d" % t], T.sem.ls, pid, rid,
+                                             mask_of(eng_chip[1::2])), "TS%d" % t, "")
+        nz = 128 * t
+        cand = lambda: tt(T.NZ[:, nz:nz + 64], T.NZ[:, nz + 64:nz + 128], T.CO[:, 64:128], A.subtract, "NZo%d CO1" % t, "NZc")
+        il = lambda: cp(T.IL[:], T.I2[:], "I2", "IL")
+        def corrections():
+            cp(C[:].indirect(T.OL[:]), T.CO[:], co + " OL", "C%d" % t)
+            trs = []
+            for to, c0, land, sem, en in ((rl, 0, "LR", "ar", eng_chip[1::2]), (rrt, V - H, "LL", "al", eng_chip[0::2])):
+                rid, pid = topo.addr(to, core)
+                trs.append(RemoteDMATransfer(dst_ids=[DstId(rid=rid, pnc=pid)], dma_engine_mask=mask_of(en), remote_sem=T.sem[sem + str(t)],
+                                             src=C[:, c0:c0 + H], dst=T[land][:, t * H:(t + 1) * H]))
+            op("g", lambda: g.remote_dma_fused(trs, local_sem=T.sem.ls), "C%d" % t, "")
+        if urgent:
+            touches()
+            th2(); i1(); th3(); i2()
+            for f in range(3): ts(T.CO[:, 64 * f:64 * f + 64], T.M[:], 0.5 if f else -0.5, A.mult, "M", "CO%d" % f)
+            sr2(); il(); cand(); send_touches(); corrections()
+        else:
+            corrections(); touches(); i1(); send_touches(); sr2(); i2(); cand(); il()
+        arrival("at%d" % t, "LT%d" % t); arrival("al%d" % t, "LL%d" % t); arrival("ar%d" % t, "LR%d" % t)
+        for c in range(4): count(0, 256, 4 * (1 - par) + c, 4 * (1 - par) + c, "PR0 PR1")
+        last = t == RO - 1
+        if not last:
+            for r in range(16): mm(P[2][:, 0:th // 16], W(r), T.TH[:, r:th:16], r == 0, r == 15, "WD TH", "#2")
+        tt(T.D[:].indirect(T.OL[:]), T.DV[:], T.CO[:], A.add, "DV OL " + co, DX)
+        for s, (c0, tok, land) in enumerate(sides):
+            if lower[s]: act(P[0][:, s * H:(s + 1) * H], T.D[:, c0:c0 + H], tok, "#0")
+        if last: dma("s", T.yd[:, H:V - H], T.D[:, H:V - H], "Dm", "y0")
+        s0 = 8 * (t + 1); m1 = 40 - s0; L = None if last else T["L%d" % (t + 1)]
+
+        def places(c0, c1, SS, ss, bank, minus, plus, ftok, extra, to="PL"):
+            m = c1 - c0
+            scan(SS[:, 1:1 + m], T.ONE[:, 0:m], T.F[:, c0:c1], 0.0, A.mult, A.add, "ONE " + ftok, ss)
+            mm(P[bank][:, 0:m], T.TI[:], SS[:, 1:1 + m], True, False, "TI " + ss, "#%d" % bank)
+            mm(P[bank][:, 0:m], T.TG[:], SS[:, 0:m], False, True, "TG %s %s0" % (ss, ss), "#%d" % bank)
+            if c0: mm(P[7][:, 0:1], T.BO[:], SS[:, m:m + 1], True, True, "BO " + ss, "#7")
+            ts2(T.NG[:, c0:c1], T.F[:, c0:c1], -4096.0, A.mult, minus, A.add, "NN0 " + ftok, "NG")
+            extra[0]()
+            tt(T.NF[:, c0:c1], T.NG[:, c0:c1], T.JK[:, c0:c1], A.add, "NG JK", "NF")
+            extra[1]()
+            tt(T.Q[:, c0:c1], P[bank][:, 0:m], T.NF[:, c0:c1], A.max, "#%d NF" % bank, "Q")
+            extra[2]()
+            ts(T.PL[:, c0:c1], T.Q[:, c0:c1], plus, A.add, "Q NN", to)
+        def unflag(c0, c1, plus, ftok):
+            ts2(T.KP[:, c0:c1], T.Q[:, c0:c1], plus, A.add, 255.5, A.is_gt, "Q NN", "KP")
+            return lambda: tt(T.F[:, c0:c1], T.F[:, c0:c1], T.KP[:, c0:c1], A.mult, "KP " + ftok, ftok)
+
+        def nzf():
+            ts(T.NZF[:], T.NZ[:, nz:nz + 64], 0.0, A.not_equal, "NZc", "NZF")
+            for r in range(16): mm(P[6][:, 0:4], W(r), T.NZF[:, r::16], r == 0, r == 15, "WD NZF", "#6")
+        def i3():
+            act(T.NZ[:, nz + 320:nz + 384], T.NZ[:, nz:nz + 128].indirect(T.IL[:]), "IL NZc NZo%d" % t, "NZo%d" % (t + 2))
+        q = 4 * (1 - par)
+        sr1 = lambda: tt(T.SR[:, q:q + 4], T.ACC[:, q:q + 4], T.OO[:, q:q + 4], A.add, "OO " + " ".join("ACC%d" % (q + c) for c in range(4)), "SRa")
+        go1 = lambda: tt(T.G4[:], P[6][:, 0:4], T.TB[:, 0:4], A.add, "#6 " + tb, "G4")
+        go2 = lambda: ts2(T.G3[:], T.G4[:], 0.0, A.is_equal, 384.0, A.mult, "G4", "G3")
+        go3 = lambda: tt(T.SR[:, 4 * par:4 * par + 4], T.G1[:], T.G3[:], A.max, "G1 G3", "SRb")
+        def back():
+            ts(T.WL[:], T.SR[:], 0.25, A.add, "SRa SRb", "WL")
+            for f in range(3):
+                act(TRn[:, f * TW_:f * TW_ + 128], win(f).indirect(T.WL[:]), tri(f) + " WL", "TRo%d%d" % (1 - par, f))
+        def free():
+            ts(T.FW[:], T.SR[:], 383.5, A.is_gt, "SRa SRb", "FW")
+            first = True
+            for p in range(2):
+                o = P[5][:, 4 * p:4 * p + 4]
+                mm(o, T.TI[:], T.FW[:, 0:4], True, False, "TI FW", "#5")
+                mm(o, T.TI[:] if p else T.TX[:], T.FW[:, 4:8], False, False, "TI TX FW", "#5")
+                for d in range(1, 4):
+                    for x in range(2):
+                        mm(P[5][:, 4 * p + d:4 * p + 4], T.BO[:], T.FW[:, 4 * x:4 * x + 4 - d], False, False, "BO FW", "#5")
+                mm(o, T.IK[:], T.FW[:, 4 * p:4 * p + 4], False, True, "IK FW", "#5")
+            return lambda: act(T.FB[:], P[5][:, 0:8], "#5", "FB", scale=40.0, bias=40 * 383.5)
+        o1 = lambda: tt(T.OO[:], T.FW[:], T.K1[:], A.mult, "FW K1", "OO")
+        o2 = lambda: tt(T.OO[:], T.OO[:], T.K2[:], A.add, "OO K2", "OO")
+        no = lambda: None
+
+        if not last:
+            top = 16 if t == 0 else 40
+            i3()
+            if t == 0: table(1)
+            tt(T.F[:, 0:top], P[2][:, 0:top], T.F[:, 0:top], A.max, "#2 Fa Fb Fc", "Fa Fb Fc")
+            places(s0, top, T.SSa, "SSa", 3, 1.0, -1.0, "Fa" if t else "Fc", (nzf, no, sr1))
+            if t == 0:
+                cp(L[:].indirect(T.PL[:, s0:top]), T.R[:, 16 * s0:16 * top], "PL R0", "L1")
+                go1()
+                act(T.NN[:, 0:1], P[7][:, 0:1], "#7", "NN", scale=-1.0, bias=256.0)
+                act(T.EB[:], T.CR[:, 0:16], "CR NN", "EB", bias=T.NN[:, 0:1])
+                go2()
+                scan(T.LW[:, 0:128], T.MB[:, 0:128], L[:, 0:128], 4096.0, A.max, A.min, "MB L1", "LW")
+                go3()
+                tt(T.EB[:, 0:8], T.EB[:, 0:8], T.LW[:, 15:128:16], A.min, "EB LW", "EB")
+                table(0)
+                cp(T.VL[:], T.EB[:], "EB", "VL")
+            else:
+                act(T.NN[:, 0:1], P[7][:, 0:1], "#7", "NN0", scale=-1.0, bias=1.0)
+                act(T.NN[:, 1:2], P[7][:, 0:1], "#7", "NN", bias=-1.0)
+                act(L[:].indirect(T.PL[:, s0:top]), T.LG[:, 16 * s0:16 * top], "PL LG", "L%d" % (t + 1), f=AF.Sigmoid)
+                fa = unflag(s0, 40, -1.0, "Fa")
+                later.append(fa)
+            if t >= 1: act(T.N2[:], T.NZ[:, nz + 192:nz + 256], "NZo%d" % (t + 1), "N2", scale=2.0)
+            def his(mid, t=t):
+                scan(T.XM[:, 0:H], T.RS[:, 0:H], T.LT[:, t * H:(t + 1) * H], 0.0, A.mult, A.add, "RS LT%d" % t, "XM0 XM1")
+                mid()
+                tt(T.F[:, 0:8], T.XM[:, 15:H:16], T.F[:, 0:8], A.max, "XM0 Fb", "Fb")
+            def wrap():
+                scan(T.LW[:], T.MB[:], L[:, 0:256], 4096.0, A.max, A.min, "MB L%d" % (t + 1), "LW")
+            if t == 0:
+                back(); free()()
+                lists(first=True)
+                table(2); table(3)
+                for x in fix(t): x()
+                def rest():
+                    o1()
+                    ts2(T.F[:, 16:40], T.CR[:, 16:40], T.NN[:, 0:1], A.subtract, 255.5, A.is_gt, "CR NN", "Fa")
+                    fill(T.F[:, 8:16], 0.0, "Fb Fc")
+                    his(o2)
+                later.append(rest)
+            else:
+                his(later.pop())
+                places(0, s0, T.SSb, "SSb", 2, T.NN[:, 0:1], T.NN[:, 1:2], "Fb", (go1, go2, go3), "PM")
+                act(L[:].indirect(T.PL[:, 0:s0]), T.LG[:, U:U + 16 * s0], "PM LG", "L%d" % (t + 1), f=AF.Sigmoid)
+                back(); fb = unflag(0, s0, T.NN[:, 1:2], "Fb")
+                later.append(free())
+                fb(); o1()
+                for x in fix(t): x()
+                o2()
+                wrap()
+                ts2(T.VL[:], T.LW[:, 15::16], SLOPE, A.mult, 512.25 - SLOPE / 2, A.add, "LW", "VL")
+                lists()
+        else:
+            i3(); nzf(); sr1(); go1(); go2(); go3(); back()
+            for c0, c1, bank in ((8, 40, 2), (0, 8, 3)):
+                m = 16 * (c1 - c0)
+                mm(P[bank][0:8, 0:m], T.SEL[:, 0:8], T.TH[:, 16 * c0:16 * c1], True, False, "SEL TH", "#%d" % bank)
+                for r in range(16):
+                    mm(P[bank][0:8, r:m:16], T.SEL[:, 8 * r:8 * r + 8], T.F[:, c0:c1], False, bank == 2 and r == 15, "SEL Fa Fb", "#%d" % bank)
+            ts(T.YF[0:8, H:U], P[2][0:8, :], 0.5, A.is_gt, "#2", "YFa")
+            for p in range(2):
+                act(T.YZ[:, p::2], T.NZ[:, 128 * (4 + p) + 64:128 * (5 + p)], "NZo%d" % (4 + p), "YZ%d" % p, scale=-1.0)
+            dma("s", T.yz[:], T.YZ[:], "YZ0 YZ1", "y1")
+            for f in range(3):
+                for p in range(2):
+                    mm(P[4][0:8, 128 * f + p:128 * (f + 1):2], T.SE0[:], TRn[:, f * TW_ + 64 * p:f * TW_ + 64 * p + 64], True, True,
+                       "SE0 TRo%d%d" % (1 - par, f), "#4")
+            ts2(T.S[0:8, 0:384], P[4][0:8, 0:384], float(NONE), A.is_equal, -1.0 - NONE, A.mult, "#4", "S0")
+            tt(T.YT[0:8, :], P[4][0:8, 0:384], T.S[0:8, 0:384], A.add, "#4 S0", "YT")
+            dma("s", T.yt[:], T.YT[0:8, :], "YT", "y2")
+            for x in fix(t): x()
+            dma("s", T.yd[:, 0:H], T.D[:, 0:H], "Dl", "y3")
+            dma("a", T.yd[:, V - H:V], T.D[:, V - H:V], "Dr", "y4")
+            mm(P[3][0:8, 0:H], T.BO[:, 0::16], T.LT[:, t * H:(t + 1) * H], False, True, "BO LT%d" % t, "#3")
+            ts(T.YF[0:8, 0:H], P[3][0:8, 0:H], 0.5, A.is_gt, "#3", "YFb")
+            dma("s", T.yf[:], T.YF[0:8, :], "YFa YFb", "y5")
+            op("s", None, "y0 y1 y2 y3 y4 y5", "")
+    emit(g, T, ops)
+    g.wait_ge(T.sem.ls, 3 * half * RO)

@@ -5,10 +5,10 @@ from concourse.mybir import AluOpType as A, AxisListType as AX, ActivationFuncti
 V, U, H, RO = 1280, 640, 128, 4
 NONE = 1280
 JUNK = 1288
-DW = JUNK + 192
+DW = 1800
 TW_ = 392
 P1 = 192
-CH = 32
+PT = 64
 ALPHA = math.log(1.7)
 U0 = -6.0 - 272 * ALPHA
 SLOPE = 32776.0
@@ -21,52 +21,54 @@ def code(x):
 F32, BF, F16, I32, U16 = "float32", "bfloat16", "float16", "int32", "uint16"
 
 SCRATCH = {
-    "D": ("sbuf", [128, DW], F32), "B1i": ("sbuf", [128, U], I32), "B2i": ("sbuf", [128, U], I32),
-    "B1": ("sbuf", [128, 1032], F32), "B2": ("sbuf", [128, 1032], F32),
+    "D": ("sbuf", [128, DW], F32), "B1": ("sbuf", [128, 1032], I32), "B2": ("sbuf", [128, 1032], I32),
     "O1": ("sbuf", [128, 256], U16), "O2": ("sbuf", [128, 256], U16),
     "G2": ("sbuf", [128, 4096], F32), "S": ("sbuf", [128, 4096], F32),
-    "CM1": ("sbuf", [128, 16 * P1], BF), "CM2": ("sbuf", [128, 16 * (256 - P1)], BF), "G4": ("sbuf", [128, 4], F32),
-    "DE": ("sbuf", [128, 256], F32), "BF1": ("sbuf", [128, 256], F32), "BF2": ("sbuf", [128, 256], F32),
-    "VV": ("sbuf", [128, 256], BF), "WIN": ("sbuf", [128, 256], BF), "PR": ("sbuf", [128, 256], BF),
+    "CM": ("sbuf", [128, 4096], BF), "DE": ("sbuf", [128, 256], F32),
+    "VV": ("sbuf", [128, 256], BF), "WIN": ("sbuf", [128, 256], BF), "PR": ("sbuf", [128, 256], BF), "PF": ("sbuf", [128, 256], BF),
     "WB": ("sbuf", [128, 256], F16), "WC": ("sbuf", [128, 256], F16), "TRASH": ("sbuf", [128, 12 * 256], BF),
     "TR0": ("sbuf", [128, 3 * TW_], F32), "TR1": ("sbuf", [128, 3 * TW_], F32),
     "ACC": ("sbuf", [128, 12], F32), "OO": ("sbuf", [128, 8], F32), "LG": ("sbuf", [128, 1024], F32), "OV": ("sbuf", [128, 4], F32),
     "FB": ("sbuf", [128, 8], F32), "FW": ("sbuf", [128, 8], BF), "SL": ("sbuf", [128, 12], U16),
-    "XM": ("sbuf", [128, 192], F16), "XW": ("sbuf", [128, 192], F32), "XL": ("sbuf", [128, 12], U16),
+    "XM": ("sbuf", [128, 192], F16), "XW": ("sbuf", [128, 192], F32), "XL": ("sbuf", [128, 12], U16), "ZC": ("sbuf", [128, 192], F32),
     "Z": ("sbuf", [128, 3, 128], F16), "E0": ("sbuf", [128, 144], BF), "E1": ("sbuf", [128, 288], BF),
-    "E2": ("sbuf", [128, 432], BF), "E3": ("sbuf", [128, 576], BF), "CF": ("sbuf", [128, 4], F32),
-    "TB": ("sbuf", [128, 12], F32), "OF": ("sbuf", [128, 12], F32), "OL": ("sbuf", [128, 12], U16),
-    "DV": ("sbuf", [128, 192], F32), "T1": ("sbuf", [128, 64], F32), "T2": ("sbuf", [128, 64], F32),
-    "M": ("sbuf", [128, 64], F32), "N2": ("sbuf", [128, 64], F32), "CO": ("sbuf", [128, 192], F32),
+    "E2": ("sbuf", [128, 432], BF), "E3": ("sbuf", [128, 576], BF), "ES": ("sbuf", [128, 4 * 288], BF), "OL": ("sbuf", [128, 12], U16),
+    "DV": ("sbuf", [128, 192], F32), "DZ": ("sbuf", [128, 192], F32), "T1": ("sbuf", [128, 64], F32), "T2": ("sbuf", [128, 64], F32),
+    "CO": ("sbuf", [128, 192], F32), "TB": ("sbuf", [128, 12], F32), "OF": ("sbuf", [128, 12], F32),
     "NZ": ("sbuf", [128, 768], F32), "NZF": ("sbuf", [128, 64], BF), "I1": ("sbuf", [128, 4], F32), "I2": ("sbuf", [128, 4], F32),
     "IL": ("sbuf", [128, 4], U16), "G1": ("sbuf", [128, 4], F32), "G3": ("sbuf", [128, 4], F32),
     "SR": ("sbuf", [128, 8], F32), "WL": ("sbuf", [128, 8], U16),
-    "F": ("sbuf", [128, 40], BF), "SSa": ("sbuf", [128, 48], BF), "SSb": ("sbuf", [128, 48], BF),
-    "NF": ("sbuf", [128, 40], F32), "NG": ("sbuf", [128, 40], F32), "Q": ("sbuf", [128, 40], F32), "KP": ("sbuf", [128, 40], BF),
-    "PL": ("sbuf", [128, 40], U16), "NN": ("sbuf", [128, 2], F32), "LW": ("sbuf", [128, 256], F32),
+    "X": ("sbuf", [128, U], F32), "XS": ("sbuf", [128, H], F32), "THR": ("sbuf", [128, 40], F32), "GB": ("sbuf", [128, 8], F32),
+    "F": ("sbuf", [128, 40], BF), "FO": ("sbuf", [128, 8], BF), "FN": ("sbuf", [128, 40], BF), "FK": ("sbuf", [128, 40], BF),
+    "SSa": ("sbuf", [128, 32], BF), "SSb": ("sbuf", [128, 32], BF), "SSc": ("sbuf", [128, 16], BF),
+    "NF": ("sbuf", [128, 40], F16), "KP": ("sbuf", [128, 40], BF), "PL": ("sbuf", [128, 40], U16), "OFF": ("sbuf", [128, 16], U16),
+    "LS": ("sbuf", [128, 256], F32), "LW": ("sbuf", [128, 256], F32),
     "VL": ("sbuf", [128, 16], U16), "EA": ("sbuf", [128, 16], F32), "EB": ("sbuf", [128, 16], F32), "EL": ("sbuf", [128, 16], U16),
-    "PI": ("sbuf", [128, 2], I32), "PJ": ("sbuf", [128, 2], I32), "PC": ("sbuf", [128, 4], F32),
-    "J16": ("sbuf", [128, 256], F32), "R": ("sbuf", [128, 256], F32), "ET": ("sbuf", [128, 1032], F32),
+    "PI": ("sbuf", [128, 4], I32), "PC": ("sbuf", [128, 8], F32), "IF": ("sbuf", [128, 256], F32),
+    "J16": ("sbuf", [128, U], F32), "R": ("sbuf", [128, 256], F32), "ET": ("sbuf", [128, 1032], F32),
     "M16": ("sbuf", [128, 128], F32), "WD": ("sbuf", [128, 144], BF), "BO": ("sbuf", [128, 128], BF), "BH": ("sbuf", [128, 128], F16),
     "BT": ("sbuf", [128, 128], BF), "TI": ("sbuf", [128, 128], BF), "TG": ("sbuf", [128, 128], BF), "TX": ("sbuf", [128, 128], BF),
-    "IK": ("sbuf", [128, 128], BF), "UV": ("sbuf", [128, 192], BF), "ONE": ("sbuf", [128, 256], BF), "IM": ("sbuf", [128, 64], F32),
-    "MB": ("sbuf", [128, 256], F32), "RS": ("sbuf", [128, 192], F16), "ZM": ("sbuf", [128, 128], F32), "CR": ("sbuf", [128, 40], F32),
-    "JK": ("sbuf", [128, 40], F32), "J12": ("sbuf", [128, 12], F32), "K1": ("sbuf", [128, 8], F32), "K2": ("sbuf", [128, 8], F32),
+    "IK": ("sbuf", [128, 128], BF), "IH": ("sbuf", [128, 128], F16), "ONE": ("sbuf", [128, 256], BF), "IM": ("sbuf", [128, 256], F32),
+    "MB": ("sbuf", [128, U], F32), "RS": ("sbuf", [128, 192], F16), "ZM": ("sbuf", [128, 128], F32), "CR": ("sbuf", [128, 40], F32),
+    "JK": ("sbuf", [128, 40], F32), "J12": ("sbuf", [128, 12], F32), "K1": ("sbuf", [128, 16], F32),
+    "C1": ("sbuf", [128, 16], F32), "TH0": ("sbuf", [128, 40], F32), "THS": ("sbuf", [128, 8], F32),
     "QT": ("sbuf", [128, 4], F32), "SEL": ("sbuf", [128, 128], BF), "SE0": ("sbuf", [128, 8], F32),
-    "BIG": ("sbuf", [128, 192], F32), "TS": ("sbuf", [128, RO * H], BF), "TH": ("sbuf", [128, U], BF),
-    "YZ": ("sbuf", [128, 128], F32), "YT": ("sbuf", [128, 384], F32), "YF": ("sbuf", [128, 640], F32),
-    "LL": ("sbuf", [128, RO * H], F32), "LR": ("sbuf", [128, RO * H], F32), "LT": ("sbuf", [128, RO * H], BF),
+    "TS": ("sbuf", [128, 8 * RO], F32), "TH": ("sbuf", [128, U], BF),
+    "YF": ("sbuf", [128, 640], F32),
+    "LL": ("sbuf", [128, RO * H], F32), "LR": ("sbuf", [128, RO * H], F32), "LT": ("sbuf", [128, 8 * RO], F32),
+    "LU": ("sbuf", [128, H], F32),
 }
 for _t in range(RO):
-    SCRATCH["C%d" % _t] = ("sbuf", [128, DW], F32)
     SCRATCH["TW%d" % _t] = ("sbuf", [128, DW], F32)
 for _t in range(1, RO):
-    SCRATCH["L%d" % _t] = ("sbuf", [128, V], F32)
+    SCRATCH["L%d" % _t] = ("sbuf", [128, DW], F32)
+for _t in range(2, RO):
+    SCRATCH["M%d" % _t] = ("sbuf", [128, DW], F32)
 for _b in range(8):
     SCRATCH["P%d" % _b] = ("psum", [128, 512], F32)
 
-SEMAPHORES = (["qv", "qa", "qp", "qg", "ls"] + ["dma%d" % i for i in range(16)]
-              + [n + str(t) for t in range(RO) for n in ("al", "ar", "at")])
+SEMAPHORES = (["qv", "qa", "qp", "qg", "ls"] + ["dma%d" % i for i in range(20)]
+              + [n + str(t) for t in range(RO) for n in ("al", "ar", "at", "ld")])
 
 
 def relays(T, topo, rank):
@@ -83,6 +85,10 @@ def mask_of(engines):
     return m
 
 
+def touch_piece(T, t):
+    return T.LT[:, 8 * t:8 * t + 8] if t < RO - 1 else T.LU[:]
+
+
 def relay_program(g, core, T, topo):
     n = len(T.cores)
     for rank in range(n):
@@ -94,7 +100,7 @@ def relay_program(g, core, T, topo):
         buf, sem = (("LR", "ar"), ("LL", "al"), ("LT", "at"))[role]
         rid, pid = topo.addr(dst, core); m = topo.mask(core, dst); k = len(topo.engines(core, dst))
         for t in range(RO):
-            piece = T[buf][:, t * H:(t + 1) * H]
+            piece = T[buf][:, t * H:(t + 1) * H] if role < 2 else touch_piece(T, t)
             g.wait_ge(T.sem[sem + str(t)], len(topo.engines(T.cores[rank], core)) // 2)
             g.remote_dma(piece, piece, T.sem[sem + str(t)], T.sem.ls, pid, rid, m)
         g.wait_ge(T.sem.ls, k * RO)
@@ -107,7 +113,7 @@ def emit(g, T, ops):
         d = set()
         own = lambda j: ops[j][0] == eng and ops[j][4] is None and sem is None
         for k in rd:
-            if k in last_w: d.add(last_w[k])
+            if k.lstrip("~") in last_w: d.add(last_w[k.lstrip("~")])
             if k[0] == "#":
                 d.update(j for j in readers.get(k, ()) if not own(j))
         for k in wr:
@@ -120,7 +126,7 @@ def emit(g, T, ops):
     line = lambda j: ops[j][0] if ops[j][4] is None else "x%d" % j
     clock, known, waits = {}, {}, []
     for i, (eng, fn, rd, wr, sem) in enumerate(ops):
-        kn = known.setdefault(eng, {}); w = []
+        kn = known.setdefault(eng, {}) if eng != "x" else {}; w = []
         top = {}
         for j in deps[i]:
             if top.get(line(j), -1) < j: top[line(j)] = j
@@ -152,7 +158,7 @@ def rank_program(g, core, T, topo):
         return relay_program(g, core, T, topo)
     n = len(T.cores)
     ops = []
-    ndma = [0]; later = []
+    ndma = [0]
     rl, rrt, rt = relays(T, topo, rank)
     eng_chip = topo.engines(core, rl); half = len(eng_chip) // 2
     far = len(topo.engines(rl, T.cores[(rank - 1) % n]))
@@ -162,7 +168,7 @@ def rank_program(g, core, T, topo):
     def dma(eng, out, in_, rd, wr):
         q = g.sync if eng == "s" else g.scalar
         ops.append((eng, lambda: q.dma_start(out, in_), rd.split(), wr.split(), ("dma%d" % ndma[0], 16))); ndma[0] += 1
-    def arrival(sem, wr): ops.append(("x", None, [], [wr], (sem, far)))
+    def arrival(sem, wr, k=far): ops.append(("x", None, [], [wr], (sem, k)))
     def cp(out, in_, rd, wr): op("v", lambda: v.tensor_copy(out, in_), rd, wr)
     def tt(out, x, y, o, rd, wr): op("v", lambda: v.tensor_tensor(out, x, y, o), rd, wr)
     def ts(out, x, s1, o0, rd, wr): op("v", lambda: v.tensor_scalar(out, x, s1, None, o0), rd, wr)
@@ -175,85 +181,93 @@ def rank_program(g, core, T, topo):
         if whole: op("g", lambda: g.iota(out, pat, base, cm), "", wr)
         else: op("g", lambda: g.iota(out, pat, base, cm, allow_small_or_imprecise_dtypes=True), "", wr)
     def sel(out, in_, pat, o, base, cm, rd, wr, c=0.0): op("g", lambda: g.affine_select(out, in_, pat, o, c, base, cm), rd, wr)
+    def names(s, xs): return " ".join(s % x for x in xs)
     P = [T["P%d" % b] for b in range(8)]
     W = lambda k: T.WD[:, 15 - k:143 - k]
     Dr = T.D[:, 0:JUNK]; DD = "Dl Dm Dr Dx"
     NL = 256 - P1
 
-    dma("s", T.B2i[:, 0:256], T.b2[:, 0:256], "", "B2i0")
-    dma("a", T.B1i[:, 0:256], T.b1[:, 0:256], "", "B1i0")
+    dma("s", T.B2[:, 0:64], T.b2[:, 0:64], "", "B2a")
+    dma("a", T.B1[:, 0:64], T.b1[:, 0:64], "", "B1a")
     dma("s", T.D[0:64, 0:V], T.dist[0:64, :], "", "Dl Dm Dr")
     dma("a", T.D[64:128, 0:V], T.dist[64:128, :], "", "Dn")
-    dma("s", T.B2i[:, 256:U], T.b2[:, 256:U], "Dm Dn", "B2i1")
-    dma("s", T.B1i[:, 256:U], T.b1[:, 256:U], "", "B1i1")
+    dma("s", T.B2[:, 64:256], T.b2[:, 64:256], "", "B2b")
+    dma("s", T.B1[:, 64:256], T.b1[:, 64:256], "", "B1b")
+    dma("s", T.B2[:, 256:U], T.b2[:, 256:U], "B1b B2b", "B2c")
+    dma("s", T.B1[:, 256:U], T.b1[:, 256:U], "", "B1c")
+    dma("s", T.B2[:, U:1024], T.b2[:, 0:384], "", "B2d")
+    dma("s", T.B1[:, U:1024], T.b1[:, 0:384], "", "B1d")
+    BB1, BB2 = "B1a B1b B1c B1d B1x", "B2a B2b B2c B2d B2x"
 
     iota(T.PI[:, 0:1], [[0, 1]], 0, 1, "PI", whole=True)
-    iota(T.M16[:], [[16, 8], [0, 16]], 0, 0, "M16")
-    iota(T.J16[:], [[0, 16], [1, 16]], 0, 0, "J16")
-    iota(T.R[:, 0:256], [[1, 256]], 0, 0, "R0")
     iota(T.CR[:], [[16, 40]], 0, 0, "CR")
+    iota(T.M16[:], [[16, 8], [0, 16]], 0, 0, "M16")
+    iota(T.R[:, 0:256], [[1, 256]], 0, 0, "R0")
+    iota(T.J16[:], [[0, 40], [1, 16]], 0, 0, "J16")
     iota(T.FB[:], [[1, 2], [32, 4]], 0, 0, "FB")
-    fill(T.D[:, V:JUNK], 1e29, "Dx")
-    fill(T.UV[:], math.exp(U0 + 137 * ALPHA) / 16, "UV")
+    fill(T.D[:, V:JUNK], 1e9, "Dx")
     fill(T.QT[:], 0.25, "QT")
     for b0, b1 in ((1, 2), (3, 5), (6, 7)):
         fill(T.ZM[:, 16 * b0:16 * b1], 0.0, "ZM%d" % b0)
-    iota(T.ONE[:], [[0, 256]], 1, 0, "ONE")
-    iota(T.OO[:], [[0, 8]], 128, 0, "OO")
+    fill(T.ONE[:], 1.0, "ONE")
+    fill(T.OO[:], 128.0, "OO")
     for f in range(3):
-        iota(T.TR0[:, f * TW_:f * TW_ + 128], [[0, 128]], NONE, 0, "TRo0%d" % f)
-    iota(T.TR0[:, 384::TW_], [[0, 3]], NONE, 0, "TRx0"); iota(T.TR1[:, 384::TW_], [[0, 3]], NONE, 0, "TRx1")
-    iota(T.BIG[:], [[0, 192]], 30, 0, "BIG")
-    iota(T.NZ[:, 64:128], [[0, 64]], 0, 0, "NZo0"); iota(T.NZ[:, 192:256], [[0, 64]], 0, 0, "NZo1")
-    iota(T.F[:, 0:16], [[0, 16]], 0, 0, "Fa Fb Fc")
-    iota(T.SSa[:, 0:1], [[0, 1]], 0, 0, "SSa0"); iota(T.SSb[:, 0:1], [[0, 1]], 0, 0, "SSb0")
-    ts(T.PJ[:, 0:1], T.PI[:, 0:1], 15, A.bitwise_and, "PI", "PJ0")
-    ts(T.PJ[:, 1:2], T.PI[:, 0:1], 112, A.bitwise_and, "PI", "PJ1")
-    cp(T.PC[:, 0:2], T.PJ[:], "PJ0 PJ1", "PC")
+        fill(T.TR0[:, f * TW_:f * TW_ + 128], float(NONE), "TRo0%d" % f)
+    fill(T.TR0[:, 384::TW_], float(NONE), "TRx0"); fill(T.TR1[:, 384::TW_], float(NONE), "TRx1")
+    fill(T.NZ[:, 64:128], 0.0, "NZo0"); fill(T.NZ[:, 192:256], 0.0, "NZo1")
+    fill(T.F[:, 16:40], 1.0, "Fa"); fill(T.NF[:, 16:40], 0.0, "NFa"); fill(T.KP[:], 1.0, "KPa KPb KPc")
+    for s in "abc": fill(T["SS" + s][:, 0:1], 0.0, "SS%s0" % s)
+    ts(T.PI[:, 2:3], T.PI[:, 0:1], 15, A.bitwise_and, "PI", "PJ0")
+    ts(T.PI[:, 3:4], T.PI[:, 0:1], 112, A.bitwise_and, "PI", "PJ1")
+    cp(T.PC[:, 0:2], T.PI[:, 2:4], "PJ0 PJ1", "PC")
     rr, gg = T.PC[:, 0:1], T.PC[:, 1:2]
+    ts(T.CR[:], T.CR[:], rr, A.add, "CR PC", "CR")
     ts2(T.PC[:, 2:3], rr, -ALPHA, A.mult, U0, A.add, "PC", "PC2")
     ts(T.PC[:, 3:4], gg, 15.0, A.add, "PC", "PC3")
+    act(T.TH0[:], T.CR[:], "CR", "TH0", f=AF.Sigmoid, scale=1.0 / 8192, bias=0.5 / 8192)
+    act(T.THS[:], T.CR[:, 0:8], "CR", "THS", f=AF.Sigmoid, scale=1.0 / 8192, bias=(V - H + 0.5) / 8192)
     ts(T.BO[:], T.M16[:], gg, A.is_equal, "M16 PC", "BO")
     ts(T.BH[:], T.M16[:], gg, A.is_equal, "M16 PC", "BH")
     ts2(T.BT[:], T.M16[:], gg, A.is_equal, 0.390625, A.mult, "M16 PC", "BT")
-    ts(T.IM[:], T.J16[:, 0:64], rr, A.is_equal, "J16 PC", "IM")
-    ts(P[7][:, 256:256 + H], T.J16[:, 0:H], rr, A.is_equal, "J16 PC", "#7")
+    ts2(T.WD[:], T.R[:, 0:144], T.PC[:, 3:4], A.is_equal, 0.0625, A.mult, "R0 PC3", "WD")
+    ts2(T.IH[:], T.R[:, 0:128], gg, A.subtract, rr, A.is_equal, "R0 PC", "IH")
+    ts2(T.FB[:], T.FB[:], rr, A.add, rr, A.add, "FB PC", "FB")
+    cp(T.O2[:, 0:64], T.B2[:, 0:64], "B2a", "O20")
+    cp(T.O1[:, 0:64], T.B1[:, 0:64], "B1a", "O10")
+    ts(T.IM[:], T.J16[:, 0:256], rr, A.is_equal, "J16 PC", "IM")
+    ts2(P[0][:, 256:448], T.J16[:, 0:192], rr, A.is_equal, 8192.0, A.mult, "J16 PC", "#0")
+    ts2(T.IF[:, 0:128], T.R[:, 0:128], gg, A.subtract, rr, A.is_equal, "R0 PC", "IF")
+    act(T.IF[:, 128:256], T.IF[:, 0:128], "IF", "NI", scale=-1.0)
+    act(T.PC[:, 4:5], T.PC[:, 2:3], "PC2", "PC4", bias=8 * 17 * ALPHA)
     ts(T.RS[:], T.J16[:, 0:192], 0.5, A.is_gt, "J16", "RS")
     for b in (0, 2, 5, 7):
         ts2(T.ZM[:, 16 * b:16 * b + 16], T.J16[:, 0:16], rr, A.is_ge, float(NONE), A.mult, "J16 PC", "ZM%d" % b)
     ts2(T.MB[:], T.J16[:], rr, A.is_equal, 4096.0, A.mult, "J16 PC", "MB")
-    ts2(T.WD[:], T.R[:, 0:144], T.PC[:, 3:4], A.is_equal, 0.0625, A.mult, "R0 PC3", "WD")
-    ts(T.CR[:], T.CR[:], rr, A.add, "CR PC", "CR")
-    ts2(T.FB[:], T.FB[:], rr, A.add, rr, A.add, "FB PC", "FB")
-    cp(T.O2[:], T.B2i[:, 0:256], "B2i0", "O2a O2b")
-    cp(T.O1[:], T.B1i[:, 0:256], "B1i0", "O1")
-    cp(P[1][:, 0:256], T.B1i[:, 0:256], "B1i0", "#1")
-    cp(P[1][:, 256:512], T.B2i[:, 0:256], "B2i0", "#1")
     act(T.FB[:], T.FB[:], "FB", "FB", scale=40.0, bias=20.0)
     act(T.JK[:], T.CR[:], "CR", "JK", bias=float(U))
     act(T.J12[:], T.CR[:, 0:12], "CR", "J12", bias=float(JUNK))
-    act(T.K1[:], T.CR[:, 0:8], "CR", "K1", scale=-1.0, bias=384.0)
-    act(T.K2[:], T.CR[:, 0:8], "CR", "K2", bias=-256.0)
+    act(T.K1[:, 0:8], T.CR[:, 0:8], "CR", "K1", scale=-1.0, bias=384.0)
+    act(T.K1[:, 8:16], T.CR[:, 0:8], "CR", "K2", bias=-256.0)
+    act(T.C1[:], T.CR[:, 0:16], "CR", "C1", bias=1.0)
     zm = " ZM0 ZM1 ZM2 ZM3 ZM5 ZM6 ZM7"
 
-    def zeros(t):
-        C, TW = T["C%d" % t], T["TW%d" % t]
-        iota(C[:, 0:H], [[0, H]], 0, 0, "C%d" % t); iota(C[:, V - H:V], [[0, H]], 0, 0, "C%d" % t)
-        iota(TW[:, 0:U], [[0, U]], 0, 0, "TW%d" % t); iota(TW[:, V - H:V], [[0, H]], 0, 0, "TW%d" % t)
-    zeros(0)
+    def ones(t):
+        TW = T["TW%d" % t]; m = 256 if t == 0 else U
+        iota(TW[:, 0:m], [[0, m]], 1, 0, "TW%d" % t); iota(TW[:, V - H:V], [[0, H]], 1, 0, "TW%d" % t)
+    def blank(name, tok): sel(T[name][:, 0:264], T.J16[:, 0:264], [[0, 264]], A.is_gt, 0, 0, "J16", tok, code(1024))
+    ones(0)
     sel(T.TI[:], T.BO[:], [[1, 128]], A.is_ge, 0, -1, "BO", "TI")
     sel(T.TG[:], T.BO[:], [[-1, 128]], A.is_gt, 0, 1, "BO", "TG")
     sel(T.TX[:], T.BO[:], [[1, 128]], A.is_gt, 0, -1, "BO", "TX")
     iota(T.IK[:], [[0, 128]], -384, 0, "IK")
     sel(T.IK[:], T.IK[:], [[-1, 128]], A.is_equal, 0, 1, "IK", "IK")
     iota(T.LG[:], [[1, 1024]], -512, 0, "LG")
-    iota(T.L1[:, 0:256], [[0, 256]], 1024, 0, "L1")
     iota(T.ET[:, 0:U], [[1, U]], 0, 0, "ET"); iota(T.ET[:, U:1032], [[1, 392]], 0, 0, "ET")
-    iota(T.B1[:, 1024:1032], [[0, 8]], NONE, 0, "B1x"); iota(T.B2[:, 1024:1032], [[0, 8]], NONE, 0, "B2x")
+    iota(T.B1[:, 1024:1032], [[0, 8]], NONE, 0, "B1x", whole=True); iota(T.B2[:, 1024:1032], [[0, 8]], NONE, 0, "B2x", whole=True)
 
     def late_constants(t):
-        if t + 1 < RO: zeros(t + 1)
-        if t + 2 < RO: sel(T["L%d" % (t + 2)][:, 0:256], T.R[:], [[0, 256]], A.is_gt, 0, 0, "R0", "L%d" % (t + 2), code(1024))
+        if t + 1 < RO: ones(t + 1); blank("L%d" % (t + 1), "L%d" % (t + 1))
+        if 1 <= t < RO - 1: blank("M%d" % (t + 1), "M%d" % (t + 1))
         if t == 2:
             sel(T.SEL[:], T.ONE[:, 0:128], [[-1, 16], [-16, 8]], A.is_equal, 0, 1, "ONE", "SEL")
             iota(T.SE0[:], [[0, 8]], 1, 0, "SE0")
@@ -261,339 +275,361 @@ def rank_program(g, core, T, topo):
 
     lower = (rank < (rank - 1) % n, rank < (rank + 1) % n)
     sides = ((0, "Dl", "LL"), (V - H, "Dr", "LR"))
+    q4 = lambda e0, e1: range(e0 // 64, (e1 + 63) // 64)
 
-    BB1, BB2 = "B10 B11 B1m B1x", "B20 B21 B2m B2x"
+    def o2(e0, e1): cp(T.O2[:, e0:e1], T.B2[:].indirect(T.VL[:, e0 // 16:e1 // 16]), BB2 + " VL%d VL%d" % (e0 // H, (e1 - 1) // H), names("O2%d", q4(e0, e1)))
+    def o1(e0, e1): cp(T.O1[:, e0:e1], T.B1[:].indirect(T.VL[:, e0 // 16:e1 // 16]), BB1 + " VL%d VL%d" % (e0 // H, (e1 - 1) // H), names("O1%d", q4(e0, e1)))
+    def decode(e0, e1):
+        ts2(T.VL[:, e0 // 16:e1 // 16], T.LW[:, e0 + 15:e1:16], SLOPE, A.mult, 512.25 - SLOPE / 2, A.add, "LW", names("VL%d", range(e0 // H, e1 // H)))
+    def own_numbers(e0):
+        c = e0 // 16
+        return [lambda: ts2(T.EA[:, c:16], T.LW[:, e0 + 15::16], code(U - 0.5), A.is_gt, -U / SLOPE, A.mult, "LW", "EA"),
+                lambda: tt(T.EB[:, c:16], T.EA[:, c:16], T.LW[:, e0 + 15::16], A.add, "EA LW", "EB"),
+                lambda: ts2(T.EL[:, c:16], T.EB[:, c:16], SLOPE, A.mult, 512.25 - SLOPE / 2, A.add, "EB", "EL")]
+    def ranks_of(s, c0, c1, ftok):
+        m = c1 - c0
+        scan(T["SS" + s][:, 1:1 + m], T.ONE[:, 0:m], T.F[:, c0:c1], 0.0, A.mult, A.add, "ONE " + ftok, "SS" + s)
+    def places(s, c0, c1, ntok):
+        m = c1 - c0; SS = T["SS" + s]; o = P[5][:, c0:c1]
+        mm(o, T.TI[:], SS[:, 1:1 + m], True, False, "TI SS" + s, "#5")
+        mm(o, T.TG[:], SS[:, 0:m], False, False, "TG SS%s SS%s0" % (s, s), "#5")
+        mm(o, T.IH[:], T.NF[:, c0:c1], False, True, "IH " + ntok, "#5")
+    na, nab = P[5][:, 40:41], P[5][:, 41:42]
 
-    def lists(first=False):
-        if first:
-            cp(T.O2[:], T.B2i[:].indirect(T.VL[:]), "B2i0 B2i1 VL", "O2a O2b")
-            cp(T.O1[:], T.B1i[:].indirect(T.VL[:]), "B1i0 B1i1 VL", "O1")
-            return
-        cp(T.O2[:, 0:64], T.B2[:].indirect(T.VL[:, 0:4]), BB2 + " VL", "O2a")
-        cp(T.O2[:, 64:256], T.B2[:].indirect(T.VL[:, 4:16]), BB2 + " VL", "O2b")
-        cp(T.O1[:], T.B1[:].indirect(T.VL[:]), BB1 + " VL", "O1")
+    def piece_b(t, e0):
+        s0 = 8 * (t + 1); his = T.LT[:, 8 * t:8 * t + 8]; L, M = T["L%d" % (t + 1)], T["M%d" % (t + 1)]; c = e0 // 16
+        def s1():
+            tt(T.F[:, 0:8], his, T.FO[:], A.max, "LT%d FO" % t, "Fb")
+            tt(T.FN[:, 0:8], his, T.GB[:], A.is_lt, "LT%d GB" % t, "FNb")
+        def s2():
+            ranks_of("c", 0, 8, "Fb")
+            tt(T.NF[:, 0:8], T.FN[:, 0:8], T.JK[:, 0:8], A.mult, "FNb JK", "NFb")
+            places("c", 0, 8, "NFb")
+            mm(nab, T.BO[:], T.SSa[:, 40 - s0:41 - s0], True, False, "BO SSa", "#5")
+            mm(nab, T.BO[:], T.SSc[:, 8:9], False, True, "BO SSc", "#5")
+        def s3():
+            ts2(T.PL[:, 0:8], P[5][:, 0:8], na, A.add, -1.0, A.add, "#5", "PLb")
+            act(L[:].indirect(T.PL[:, 0:8]), T.LG[:, U:U + H], "PLb LG", "L%d" % (t + 1), f=AF.Sigmoid)
+            ts(T.OFF[:, c:16], T.C1[:, c:16], nab, A.subtract, "C1 #5", "OFF")
+        def s4(): tt(T.LS[:, e0:256], M[:, 0:264].indirect(T.OFF[:, c:16]), T.IM[:, e0:256], A.mult, "M%d OFF IM" % (t + 1), "LS")
+        def s5(): scan(T.LW[:, e0:256], T.LS[:, e0:256], L[:, e0:256], 0.0, A.max, A.min, "LS L%d" % (t + 1), "LW")
+        return [s1, s2, s3, s4, s5, lambda: decode(e0, 256)]
+    def unflag(t):
+        s0 = 8 * (t + 1)
+        if t == 0:
+            st = [lambda: tt(T.F[:, 0:8], T.LT[:, 0:8], T.FO[:], A.max, "LT0 FO", "Fb")]
+        else:
+            st = [lambda: ts2(T.KP[:, 0:8], P[5][:, 0:8], na, A.add, 256.5, A.is_gt, "#5", "KPb"),
+                  lambda: ts2(T.KP[:, 8:s0], P[5][:, 8:s0], nab, A.add, 256.5, A.is_gt, "#5", "KPc")]
+        st.append(lambda: tt(T.FK[:], T.F[:], T.KP[:], A.mult, "Fa Fb KPa KPb KPc", "FK"))
+        if t + 2 < RO: st.append(lambda: tt(T.THR[:], T.FK[:], T.TH0[:], A.max, "FK TH0", "THR"))
+        return st
+    def fix(t, s):
+        c0, tok, land = sides[s]
+        tt(T.D[:, c0:c0 + H], P[0][:, s * H:(s + 1) * H], T[land][:, t * H:(t + 1) * H], A.add, "#0 %s%d sent%d" % (land, t, t), tok)
 
-    def table(i):
-        name, h = ("B2", "B1")[i // 2], i % 2
-        cp(T[name][:, 320 * h:320 * h + 320], T[name + "i"][:, 320 * h:320 * h + 320], "%si0 %si1" % (name, name), "%s%d" % (name, h))
-
-    def own_numbers(i):
-        if i == 0:
-            ts2(T.EA[:], T.LW[:, 15::16], code(U - 0.5), A.is_gt, -float(U), A.mult, "LW", "EA")
-            ts2(T.EB[:], T.LW[:, 15::16], SLOPE, A.mult, 512.25 - SLOPE / 2, A.add, "LW", "EB")
-        if i == 1: tt(T.EB[:], T.EA[:], T.EB[:], A.add, "EA EB", "EB")
-        if i == 2: cp(T.EL[:], T.EB[:], "EB", "EL")
-
-    def fix(t):
-        C = T["C%d" % t]
-        def first(s):
-            c0, tok, land = sides[s]; his = T[land][:, t * H:(t + 1) * H]
-            if lower[s]: tt(T.D[:, c0:c0 + H], P[0][:, s * H:(s + 1) * H], his, A.add, "#0 %s%d" % (land, t), tok)
-            else: tt(P[1][:, s * H:(s + 1) * H], P[0][:, s * H:(s + 1) * H], his, A.add, "#0 %s%d" % (land, t), "#1")
-        def second(s):
-            c0, tok, land = sides[s]
-            if not lower[s]: tt(T.D[:, c0:c0 + H], P[1][:, s * H:(s + 1) * H], C[:, c0:c0 + H], A.add, "#1 C%d" % t, tok)
-        s = 0 if lower[1] else 1
-        return [lambda: first(s), lambda: first(1 - s), lambda: second(s), lambda: second(1 - s)]
+    late = []
+    def one():
+        if late: late.pop(0)()
 
     for t in range(RO):
-        par = t % 2; TR, TRn = T["TR%d" % par], T["TR%d" % (1 - par)]; C, TW = T["C%d" % t], T["TW%d" % t]
+        par = t % 2; TR, TRn = T["TR%d" % par], T["TR%d" % (1 - par)]; TW = T["TW%d" % t]
         DX = DD + (" Dn" if t == 0 else "")
+        last = t == RO - 1
         new = lambda f, e0, e1: TR[:, f * TW_ + 128 + e0:f * TW_ + 128 + e1]
         tri = lambda f: "TRo%d%d TRx%d TRn%d0 TRn%d1" % (par, f, par, f, f)
 
-        def g2(i):
-            act(T.G2[:, 16 * CH * i:16 * CH * (i + 1)], Dr.indirect(T.O2[:, CH * i:CH * (i + 1)]),
-                DX + (" O2a" if CH * (i + 1) <= 64 else " O2b"), "G2%d" % i)
-        def add(i):
-            e0 = CH * i
-            tt(T.S[:, 16 * e0:16 * (e0 + CH)], Dr.indirect(T.O1[:, e0:e0 + CH]), T.G2[:, 16 * e0:16 * (e0 + CH)], A.add,
-               DX + " O1 G2%d" % i, "S%d" % i)
-        n1 = P1 // CH; nc = 256 // CH
-        if t == 0: cp(P[0][:, 0:256], T.D[:, 0:256], DX, "#0")
+        def g2(e0, e1):
+            act(T.G2[:, 16 * e0:16 * e1], Dr.indirect(T.O2[:, e0:e1]), DX + " " + names("O2%d", q4(e0, e1)), "G2%d" % e0)
+        def add(e0, e1):
+            tt(T.S[:, 16 * e0:16 * e1], Dr.indirect(T.O1[:, e0:e1]), T.G2[:, 16 * e0:16 * e1], A.add,
+               DX + " G2%d " % e0 + names("O1%d", q4(e0, e1)), "S%d" % e0)
+        cuts = [0, 16, 40, 64, 96, 128, 160, 192, 224, 256]
+        chunks = list(zip(cuts, cuts[1:]))
+        def compare(e0, e1, bank):
+            m = e1 - e0; s = names("S%d", [x for x in cuts if e0 <= x < e1])
+            for k in range(16):
+                cm = T.CM[:, 16 * e0 + k * m:16 * e0 + (k + 1) * m]
+                tt(cm, P[0][:, e0:e1], T.S[:, 16 * e0 + k:16 * e1:16], A.is_gt, "#0 " + s, "CM%d_%d" % (e0, k))
+                mm(P[bank][:, e0 % P1:e0 % P1 + m], W(k), cm, k == 0, k == 15, "WD CM%d_%d" % (e0, k), "#%d" % bank)
+                if e0 == PT and k >= 8: sum_signs(2 * k - 16, 2 * k - 14)
+        def differ(own, tok):
+            s = names("S%d", [x for x in cuts if x < PT])
+            for k in range(16):
+                o = P[6 + k // 8][:, PT * (k % 8):PT * (k % 8 + 1)]; b = "#%d" % (6 + k // 8)
+                if own is not None: mm(o, T.IF[:, 0:128], own, k % 8 == 0, False, "IF " + tok, b)
+                else: mm(o, T.IF[:, 128:256], T.S[:, k:16 * PT:16], False, k % 8 == 7, "NI " + s, b)
+        def signs(h):
+            act(T.CM[:, 8 * PT * h:8 * PT * (h + 1)], P[6 + h][:, 0:8 * PT], "#%d" % (6 + h), "CS%d" % h, f=AF.Sign, scale=2.0 ** 60, bias=-2.0 ** -100)
+        def sum_signs(k0, k1):
+            for k in range(k0, k1):
+                mm(P[4][:, 0:PT], W(k), T.CM[:, PT * k:PT * (k + 1)], k == 0, k == 15, "WD CS%d" % (k // 8), "#4")
+        def numbers():
+            cp(P[1][:, 0:256], T.O1[:], "O10 O11 O12 O13", "#1")
+            cp(P[1][:, 256:512], T.O2[:], "O20 O21 O22 O23", "#1")
+        def de(lst, e0, e1, tok, eng):
+            x = Dr.indirect(lst[:, e0 // 16:e1 // 16])
+            (cp if eng == "v" else act)(T.DE[:, e0:e1], x, DX + " " + tok, "DE%d" % e0)
+        def de_psum(toks): act(P[0][:, 0:256], T.DE[:], toks, "#0")
+
+        first = chunks[:7]
+        if t == 0:
+            g2(*first[0]); cp(P[0][:, 0:256], T.D[:, 0:256], DX, "#0"); differ(T.D[:, 0:PT], DX)
+            for i, c in enumerate(first):
+                if i: g2(*c)
+                add(*c)
+                if i == 0: cp(T.O2[:, 64:256], T.B2[:, 64:256], "B2b", "O21 O22 O23")
+                if i == 1: cp(T.O1[:, 64:256], T.B1[:, 64:256], "B1b", "O11 O12 O13")
+                if i == 2: numbers(); differ(None, "")
         if t == 1:
-            cp(T.DE[:], Dr.indirect(T.VL[:]), DX + " VL", "DE")
-            later.pop()()
-            cp(P[0][:, 0:256], T.DE[:], "DE", "#0")
-        for i in range(n1):
-            if t > 1 and i < 3: own_numbers(i)
-            g2(i); add(i)
-        if t > 1:
-            act(T.DE[:], Dr.indirect(T.EL[:]), DX + " EL", "DE")
-            act(P[0][:, 0:256], T.DE[:], "DE", "#0")
-        for i in range(n1, nc): g2(i)
-        if t > 1: later.pop()()
-        s1 = " ".join("S%d" % i for i in range(n1)); s2 = " ".join("S%d" % i for i in range(n1, nc))
-        for k in range(16):
-            tt(T.CM1[:, k * P1:(k + 1) * P1], P[0][:, 0:P1], T.S[:, k:16 * P1:16], A.is_gt, "#0 " + s1, "CM1%d" % k)
-            mm(P[2][:, 0:P1], W(k), T.CM1[:, k * P1:(k + 1) * P1], k == 0, k == 15, "WD CM1%d" % k, "#2")
-        if t == 1:
-            act(T.BF1[:], T.B1[:, 0:U].indirect(T.VL[:]), "B10 B11 VL", "BF1")
-            act(T.BF2[:], T.B2[:, 0:U].indirect(T.VL[:]), "B20 B21 VL", "BF2")
-            act(P[1][:, 0:256], T.BF1[:], "BF1", "#1")
-            act(P[1][:, 256:512], T.BF2[:], "BF2", "#1")
-        if t > 1:
-            act(T.BF1[:], T.B1[:].indirect(T.VL[:]), BB1 + " VL", "BF1")
-            act(T.BF2[:], T.B2[:].indirect(T.VL[:]), BB2 + " VL", "BF2")
-            act(P[1][:, 0:256], T.BF1[:], "BF1", "#1")
-            act(P[1][:, 256:512], T.BF2[:], "BF2", "#1")
+            g2(*first[0]); de(T.VL, 0, 256, "VL0 VL1", "v"); differ(T.DE[:, 0:PT], "DE0")
+            for i, c in enumerate(first):
+                if i: g2(*c)
+                add(*c)
+                if i == 0: numbers()
+                if i == 2: differ(None, "")
+            de_psum("DE0")
+        if t == 2:
+            st = piece_b(1, H); own = own_numbers(H)
+            g2(*first[0]); st[0](); de(T.VL, 0, H, "VL0", "v"); st[1]()
+            differ(T.DE[:, 0:PT], "DE0")
+            add(*first[0]); g2(*first[1]); st[2](); add(*first[1]); g2(*first[2]); st[3]()
+            add(*first[2]); differ(None, ""); g2(*first[3]); st[4](); add(*first[3]); g2(*first[4]); st[5](); own[0]()
+            o2(H, 256); own[1](); o1(H, 256); own[2]()
+            add(*first[4]); g2(*first[5]); de(T.EL, H, 256, "EL", "a"); numbers(); add(*first[5]); g2(*first[6]); de_psum("DE0 DE128"); add(*first[6])
+        if t == 3:
+            own = own_numbers(0)
+            own[0](); o2(0, 64); g2(*first[0]); own[1](); o1(0, 64); own[2](); o2(64, 256)
+            for i, c in enumerate(first):
+                if i: g2(*c)
+                if i == 1: de(T.EL, 0, PT, "EL", "a"); differ(T.DE[:, 0:PT], "DE0")
+                add(*c)
+                if i == 0: o1(64, 256)
+                if i == 1: numbers()
+                if i == 2: differ(None, "")
+            de(T.EL, PT, 256, "EL", "a"); de_psum("DE0 DE%d" % PT)
+        if late and t: late.pop(0)()
+        signs(0); signs(1); g2(*chunks[7]); g2(*chunks[8])
+        compare(PT, P1, 2)
+        act(T.VV[:, 0:PT], P[4][:, 0:PT], "#4 PC4", "VVs", f=AF.Sigmoid, bias=T.PC[:, 4:5], scale=8 * 17 * ALPHA)
         late_constants(t)
 
-        def weigh(h, e0, e1, nb, sb):
-            m = e1 - e0
-            mm(P[sb][:, 0:m], T.BT[:], T.UV[:, 0:m], True, False, "BT UV", "#%d" % sb)
-            act(T.VV[:, e0:e1], P[nb][:, 0:m], "#%d PC2" % nb, "VV%d" % h, f=AF.Sigmoid, bias=T.PC[:, 2:3], scale=16 * 17 * ALPHA)
-            mm(P[sb][:, 0:m], T.BT[:], T.VV[:, e0:e1], False, True, "BT VV%d" % h, "#%d" % sb)
+        def weigh(h, e0, e1, nb, sb, mid=lambda: None):
+            m = e1 - e0; x = 0 if h else PT
+            act(T.VV[:, e0 + x:e1], P[nb][:, x:m], "#%d PC2" % nb, "VV%d" % h, f=AF.Sigmoid, bias=T.PC[:, 2:3], scale=16 * 17 * ALPHA)
+            mid()
+            mm(P[sb][:, 0:m], T.BT[:], T.VV[:, e0:e1], True, True, "BT VVs VV%d" % h, "#%d" % sb)
         def choose(h, e0, e1, sb):
             m = e1 - e0
-            tt(T.WIN[:, e0:e1], T.VV[:, e0:e1], P[sb][:, 0:m], A.is_gt, "VV%d #%d" % (h, sb), "WIN%d" % h)
-            mm(P[4][:, 0:m], T.BO[:], T.WIN[:, e0:e1], True, True, "BO WIN%d" % h, "#4")
+            ts(T.PF[:, e0:e1], P[sb][:, 0:m], 0.390625 * 0.92 * math.exp(U0 + 138 * ALPHA), A.is_gt, "#%d" % sb, "PF%d" % h)
+            tt(T.WIN[:, e0:e1], T.VV[:, e0:e1], P[sb][:, 0:m], A.is_gt, "VVs VV%d #%d" % (h, sb), "WIN%d" % h)
         def ranks(h, e0, e1):
-            m = e1 - e0
-            scan(T.PR[:, e0:e1], T.ONE[:, 0:m], P[4][:, 0:m], T.PR[:, e0 - 1:e0] if h else 0.0, A.mult, A.add,
-                 "ONE #4" + (" PR0" if h else ""), "PR%d" % h)
-        def pick(h, e0, e1):
-            m = e1 - e0
-            tt(T.WB[:, e0:e1], T.WIN[:, e0:e1], P[1][:, e0:e1], A.mult, "WIN%d #1" % h, "WB%d" % h)
-            tt(T.WC[:, e0:e1], T.WIN[:, e0:e1], P[1][:, 256 + e0:256 + e1], A.mult, "WIN%d #1" % h, "WC%d" % h)
-            bank = 5 if h == 0 else 3
-            mm(P[bank][:, 0:m], T.BH[:], T.WB[:, e0:e1], True, True, "BH WB%d" % h, "#%d" % bank)
-            mm(P[bank][:, 256:256 + m], T.BH[:], T.WC[:, e0:e1], True, True, "BH WC%d" % h, "#%d" % bank)
+            scan(T.PR[:, e0:e1], T.ONE[:, 0:e1 - e0], T.PF[:, e0:e1], T.PR[:, e0 - 1:e0] if h else 0.0, A.mult, A.add,
+                 "ONE PF%d" % h + (" PR0" if h else ""), "PR%d" % h)
+        def pick(f, h, e0, e1, bank):
+            Wf = T.WB if f == 1 else T.WC; c0 = 256 * (f - 1)
+            tt(Wf[:, e0:e1], T.WIN[:, e0:e1], P[1][:, c0 + e0:c0 + e1], A.mult, "WIN%d #1" % h, "W%d%d" % (f, h))
+            mm(P[bank][:, c0:c0 + e1 - e0], T.BH[:], Wf[:, e0:e1], True, True, "BH W%d%d" % (f, h), "#%d" % bank)
         def count(e0, e1, col, to, rd):
             act(T.TRASH[:, 256 * to:256 * to + e1 - e0], T.PR[:, e0:e1], rd + " FB", "ACC%d" % to, f=AF.Sigmoid, bias=T.FB[:, col:col + 1], scale=-40.0,
                 accum_out=T.ACC[:, to:to + 1])
 
         weigh(0, 0, P1, 2, 3)
-        if t: act(new(0, 0, 256), T.ET[:].indirect(T.VL[:]), "ET VL", "TRn00 TRn01")
+        if t: act(new(0, 0, 256), T.ET[:].indirect(T.VL[:]), "ET VL0 VL1", "TRn00 TRn01")
         else: act(new(0, 0, 256), T.R[:, 0:256], "R0", "TRn00 TRn01")
-        add(n1)
+        add(*chunks[7]); add(*chunks[8])
         choose(0, 0, P1, 3)
-        for i in range(n1 + 1, nc): add(i)
         ranks(0, 0, P1)
-        if t == 0: act(T.LG[:], T.LG[:], "LG", "LG", scale=1.0 / 8192)
-        if t == 1:
-            act(T.B2[:, U:1024], T.B2[:, 0:384], "B20 B21", "B2m")
-            act(T.B1[:, U:1024], T.B1[:, 0:384], "B10 B11", "B1m")
         for c in range(4): count(0, P1, 4 * par + c, 8 + c, "PR0")
-        for k in range(16):
-            tt(T.CM2[:, k * NL:(k + 1) * NL], P[0][:, P1:256], T.S[:, 16 * P1 + k::16], A.is_gt, "#0 " + s2, "CM2%d" % k)
-            mm(P[6][:, 0:NL], W(k), T.CM2[:, k * NL:(k + 1) * NL], k == 0, k == 15, "WD CM2%d" % k, "#6")
-        weigh(1, P1, 256, 6, 7)
-        pick(0, 0, P1)
-        act(new(1, 0, P1), P[5][:, 0:P1], "#5", "TRn10")
+        compare(P1, 256, 6)
+        weigh(1, P1, 256, 6, 7, lambda: pick(1, 0, 0, P1, 4))
+        pick(2, 0, 0, P1, 2)
+        act(new(1, 0, P1), P[4][:, 0:P1], "#4", "TRn10")
+        act(new(2, 0, P1), P[2][:, 256:256 + P1], "#2", "TRn20")
+        one(); one()
         choose(1, P1, 256, 7)
         tt(T.OV[:], T.OO[:, 4 * par:4 * par + 4], T.ACC[:, 8:12], A.add, "OO ACC8 ACC9 ACC10 ACC11", "OV")
-        pick(1, P1, 256)
         ranks(1, P1, 256)
+        pick(1, 1, P1, 256, 3); pick(2, 1, P1, 256, 3)
+        one()
         for c in range(4): count(P1, 256, 4 * par + c, 4 * par + c, "PR1")
-        act(new(2, 0, P1), P[5][:, 256:256 + P1], "#5", "TRn20")
-        cp(new(1, P1, 256), P[3][:, 0:NL], "#3", "TRn11")
-        cp(new(2, P1, 256), P[3][:, 256:256 + NL], "#3", "TRn21")
-        for c, (p0, p1, st) in ((0, (0, 1, 1)), (0, (5, 12, 3)), (1, (1, 8, 3)), (2, (2, 11, 4)), (3, (3, 10, 6))):
+        for i, (c, (p0, p1, st)) in enumerate(((0, (0, 1, 1)), (0, (5, 12, 3)), (1, (1, 8, 3)), (2, (2, 11, 4)), (3, (3, 10, 6)))):
             m = len(range(p0, p1, st)); col = 4 * par + c
             ts2(T.SL[:, p0:p1:st], T.QT[:, 0:m], T.ACC[:, col:col + 1], A.add, T.OV[:, c:c + 1], A.add, "QT OV ACC%d" % col, "SL%d" % p0)
+        act(new(1, P1, 256), P[3][:, 0:NL], "#3", "TRn11")
+        act(new(2, P1, 256), P[3][:, 256:256 + NL], "#3", "TRn21")
         sl = " SL0 SL5 SL1 SL2 SL3"
-        for s, (c0, tok, land) in enumerate(sides):
-            if not lower[s]: act(P[0][:, s * H:(s + 1) * H], T.D[:, c0:c0 + H], tok, "#0")
         win = lambda f: TR[:, f * TW_:f * TW_ + 385]
+        one()
         for f in range(3):
-            tt(T.XM[:, 64 * f:64 * f + 64], win(f).indirect(T.SL[:, 0:4]), T.IM[:], A.mult, tri(f) + sl + " IM", "XM%d" % f)
-        tt(T.Z[:, 0, :], win(0).indirect(T.SL[:, 4:12]), T.ZM[:], A.max, tri(0) + sl + zm, "Z0")
-        scan(T.XW[:], T.RS[:], T.XM[:], 0.0, A.mult, A.add, "RS XM0 XM1 XM2", "XW")
-        tt(T.Z[:, 1, :], win(1).indirect(T.SL[:, 4:12]), T.ZM[:], A.max, tri(1) + sl + zm, "Z1")
+            act(T.ZC[:, 64 * f:64 * f + 64], win(f).indirect(T.SL[:, 0:4]), tri(f) + sl, "ZC%d" % f, scale=1.0 / 8192)
+            tt(T.Z[:, f, :], win(f).indirect(T.SL[:, 4:12]), T.ZM[:], A.max, tri(f) + sl + zm, "Z%d" % f)
+        nz = 128 * t
+        if t >= 2: act(P[7][:, 128:192], T.NZ[:, nz + 64:nz + 128], "NZo%d" % t, "#7")
+        tt(T.XM[:], T.ZC[:], P[0][:, 256:448], A.mult, "ZC0 ZC1 ZC2 #0", "XM")
+        one()
+        scan(T.XW[:], T.RS[:], T.XM[:], 0.0, A.mult, A.add, "RS XM", "XW")
+        one()
         cp(T.XL[:], T.XW[:, 15::16], "XW", "XL")
-        tt(T.Z[:, 2, :], win(2).indirect(T.SL[:, 4:12]), T.ZM[:], A.max, tri(2) + sl + zm, "Z2")
         act(T.DV[:], Dr.indirect(T.XL[:]), DX + " XL", "DV")
-        for c, (b0, b1) in ((3, (3, 7)), (2, (2, 5)), (1, (0, 2)), (0, (7, 8))):
-            E = T["E%d" % c]; m = 48 * (c + 1)
+        act(P[7][:, 0:128], T.DV[:, 64:192], "DV", "#7")
+        for s, (c0, tok, land) in enumerate(sides):
+            if not lower[s]: act(T.D[:, c0:c0 + H], T.R[:, 0:H], "R0", tok, scale=0.0)
+        if all(lower): DZ, dz = T.DV, "DV"
+        else:
+            DZ, dz = T.DZ, "DZ"
+            act(T.DZ[:], Dr.indirect(T.XL[:]), DX + " XL", "DZ")
+        def equal(c):
+            b0, b1 = ((7, 8), (0, 2), (2, 5), (3, 7))[c]; m = 48 * (c + 1)
             for f in range(3):
                 x = 64 * f + 16 * c + 15
-                ts2(E[:, f * m:(f + 1) * m], T.Z[:, :, 16 * b0:16 * b1], T.XW[:, x:x + 1], A.is_equal, 4096.0, A.mult, "Z0 Z1 Z2 XW", "E%d%d" % (c, f))
-            if c >= 2:
-                act(E[:], E[:], "E%d0 E%d1 E%d2" % (c, c, c), "CF%d E%d0 E%d1 E%d2" % (c, c, c, c), accum_out=T.CF[:, c:c + 1])
-        def red(c): op("v", lambda: v.tensor_reduce(T.CF[:, c:c + 1], T["E%d" % c][:], AX.X, A.add), "E%d0 E%d1 E%d2" % (c, c, c), "CF%d" % c)
-        def bad(c): ts(T.TB[:, c::4], T.J12[:, c::4], T.CF[:, c:c + 1], A.min, "J12 CF%d" % c, "TB%d" % c)
-        th1 = lambda: tt(T.T1[:], T.DV[:, 0:64], T.DV[:, 64:128], A.subtract, "DV", "T1")
-        th2 = lambda: tt(T.T2[:], T.T1[:], T.DV[:, 128:192], A.subtract, "T1 DV", "T2")
-        def th3():
-            if t < 2: ts(T.M[:], T.T2[:], 0.0, A.max, "T2", "M")
-            else: tt(T.M[:], T.T2[:], T.N2[:], A.max, "T2 N2", "M")
-        tb = "TB0 TB1 TB2 TB3"; co = "CO0 CO1 CO2"
-        i1 = lambda: ts2(T.I1[:], T.TB[:, 0:4], 0.5, A.is_gt, 64.0, A.mult, tb, "I1")
-        i2 = lambda: tt(T.I2[:], T.I1[:], T.CR[:, 0:4], A.add, "I1 CR", "I2")
-        sr2 = lambda: tt(T.G1[:], T.ACC[:, 4 * par:4 * par + 4], T.OV[:], A.add, "OV " + " ".join("ACC%d" % (4 * par + c) for c in range(4)), "G1")
-        urgent = t in (1, 2)
-        if urgent:
-            red(1); red(0); th1()
+                ts2(T["E%d" % c][:, f * m:(f + 1) * m], T.Z[:, :, 16 * b0:16 * b1], T.XW[:, x:x + 1], A.is_equal, 4096.0, A.mult,
+                    "Z0 Z1 Z2 XW", "E%d%d" % (c, f))
+        def fold(c):
+            E = T["E%d" % c]; h = 72 * (c + 1)
+            scan(T.ES[:, 288 * (c + 1) - h:288 * (c + 1)], E[:, 0:h], E[:, h:2 * h], 0.0, A.max, A.max, "E%d0 E%d1 E%d2" % (c, c, c), "ES%d" % c)
+        def bad(c): ts(T.TB[:, c::4], T.J12[:, c::4], T.ES[:, 288 * c + 287:288 * c + 288], A.min, "J12 ES%d" % c, "TB%d" % c)
+        DL = T.CO[:, 64:128]
+        equal(3); equal(2); fold(3); equal(1); fold(2)
+        tt(T.T1[:], T.DV[:, 0:64], P[7][:, 0:64], A.subtract, "DV #7", "T1")
+        equal(0)
+        tt(T.T2[:], T.T1[:], P[7][:, 64:128], A.subtract, "T1 #7", "T2")
+        fold(1); fold(0)
+        if t < 2:
+            ts2(DL, T.T2[:], 0.5, A.mult, 0.0, A.max, "T2", "DL"); bad(3); bad(2)
         else:
-            th1(); red(1); th2(); red(0); th3()
-            for f in range(3): act(T.CO[:, 64 * f:64 * f + 64], T.M[:], "M", "CO%d" % f, scale=0.5 if f else -0.5)
-        bad(1); bad(0); bad(3); bad(2)
+            ts(T.T1[:], T.T2[:], 0.5, A.mult, "T2", "T1"); bad(3); bad(2)
+            tt(DL, T.T1[:], P[7][:, 128:192], A.max, "T1 #7", "DL")
+        act(T.CO[:, 0:64], DL, "DL", "CO0", scale=-1.0); act(T.CO[:, 128:192], DL, "DL", "CO2")
+        bad(1); bad(0)
+        tb = "TB0 TB1 TB2 TB3"; TB = T.TB[:, 0:4]
+        one()
         tt(T.OF[:], T.TB[:], T.XW[:, 15::16], A.max, tb + " XW", "OF")
+        ts2(T.I1[:], TB, 0.5, A.is_gt, 64.0, A.mult, tb, "I1")
         cp(T.OL[:], T.OF[:], "OF", "OL")
-
-        th = 256 if t == 0 else U
-        def touches():
-            act(TW[:].indirect(T.OL[:]), T.BIG[:], "BIG OL", "TW%d" % t, f=AF.Sigmoid)
-            act(T.TH[:, 0:th], TW[:, 0:th], "TW%d" % t, "TH")
-        def send_touches():
-            tt(T.TS[:, t * H:(t + 1) * H], TW[:, V - H:V], P[7][:, 256:256 + H], A.mult, "TW%d #7" % t, "TS%d" % t)
+        tt(T.NZ[:, nz:nz + 64], T.NZ[:, nz + 64:nz + 128], DL, A.subtract, "NZo%d DL" % t, "NZc")
+        tt(T.D[:].indirect(T.OL[:]), DZ[:], T.CO[:], A.add, dz + " DL CO0 CO2 OL", DX)
+        act(TW[:].indirect(T.OL[:]), T.ZC[:], "ZC0 ZC1 ZC2 OL", "TW%d" % t, f=AF.Sigmoid)
+        trs = []
+        for to, c0, land, sem, en in ((rl, 0, "LR", "ar", eng_chip[1::2]), (rrt, V - H, "LL", "al", eng_chip[0::2])):
+            rid, pid = topo.addr(to, core)
+            trs.append(RemoteDMATransfer(dst_ids=[DstId(rid=rid, pnc=pid)], dma_engine_mask=mask_of(en), remote_sem=T.sem[sem + str(t)],
+                                         src=T.D[:, c0:c0 + H], dst=T[land][:, t * H:(t + 1) * H]))
+        op("g", lambda trs=trs, t=t: g.remote_dma_fused(trs, local_sem=T.sem["ld%d" % t]), "~Dl ~Dr", "")
+        def send_touches(src, tok, t=t):
             rid, pid = topo.addr(rt, core)
-            op("g", lambda t=t: g.remote_dma(T.LT[:, t * H:(t + 1) * H], T.TS[:, t * H:(t + 1) * H], T.sem["at%d" % t], T.sem.ls, pid, rid,
-                                             mask_of(eng_chip[1::2])), "TS%d" % t, "")
-        nz = 128 * t
-        cand = lambda: tt(T.NZ[:, nz:nz + 64], T.NZ[:, nz + 64:nz + 128], T.CO[:, 64:128], A.subtract, "NZo%d CO1" % t, "NZc")
-        il = lambda: cp(T.IL[:], T.I2[:], "I2", "IL")
-        def corrections():
-            cp(C[:].indirect(T.OL[:]), T.CO[:], co + " OL", "C%d" % t)
-            trs = []
-            for to, c0, land, sem, en in ((rl, 0, "LR", "ar", eng_chip[1::2]), (rrt, V - H, "LL", "al", eng_chip[0::2])):
-                rid, pid = topo.addr(to, core)
-                trs.append(RemoteDMATransfer(dst_ids=[DstId(rid=rid, pnc=pid)], dma_engine_mask=mask_of(en), remote_sem=T.sem[sem + str(t)],
-                                             src=C[:, c0:c0 + H], dst=T[land][:, t * H:(t + 1) * H]))
-            op("g", lambda: g.remote_dma_fused(trs, local_sem=T.sem.ls), "C%d" % t, "")
-        if urgent:
-            touches()
-            th2(); i1(); th3(); i2()
-            for f in range(3): ts(T.CO[:, 64 * f:64 * f + 64], T.M[:], 0.5 if f else -0.5, A.mult, "M", "CO%d" % f)
-            sr2(); il(); cand(); send_touches(); corrections()
-        else:
-            corrections(); touches(); i1(); send_touches(); sr2(); i2(); cand(); il()
-        arrival("at%d" % t, "LT%d" % t); arrival("al%d" % t, "LL%d" % t); arrival("ar%d" % t, "LR%d" % t)
+            op("g", lambda: g.remote_dma(touch_piece(T, t), src, T.sem["at%d" % t], T.sem.ls, pid, rid, mask_of(eng_chip[1::2])), tok, "")
+        arrival("at%d" % t, "LT%d" % t); arrival("al%d" % t, "LL%d" % t); arrival("ar%d" % t, "LR%d" % t); arrival("ld%d" % t, "sent%d" % t, 2 * half)
+        tw = "TW%d" % t
+        while late: one()
+        for s, (c0, tok, land) in enumerate(sides): act(P[0][:, s * H:(s + 1) * H], T.D[:, c0:c0 + H], tok, "#0")
+        if t == 0: act(T.LG[:], T.LG[:], "LG", "LG", scale=1.0 / 8192)
         for c in range(4): count(0, 256, 4 * (1 - par) + c, 4 * (1 - par) + c, "PR0 PR1")
-        last = t == RO - 1
-        if not last:
-            for r in range(16): mm(P[2][:, 0:th // 16], W(r), T.TH[:, r:th:16], r == 0, r == 15, "WD TH", "#2")
-        tt(T.D[:].indirect(T.OL[:]), T.DV[:], T.CO[:], A.add, "DV OL " + co, DX)
-        for s, (c0, tok, land) in enumerate(sides):
-            if lower[s]: act(P[0][:, s * H:(s + 1) * H], T.D[:, c0:c0 + H], tok, "#0")
-        if last: dma("s", T.yd[:, H:V - H], T.D[:, H:V - H], "Dm", "y0")
-        s0 = 8 * (t + 1); m1 = 40 - s0; L = None if last else T["L%d" % (t + 1)]
 
-        def places(c0, c1, SS, ss, bank, minus, plus, ftok, extra, to="PL"):
-            m = c1 - c0
-            scan(SS[:, 1:1 + m], T.ONE[:, 0:m], T.F[:, c0:c1], 0.0, A.mult, A.add, "ONE " + ftok, ss)
-            mm(P[bank][:, 0:m], T.TI[:], SS[:, 1:1 + m], True, False, "TI " + ss, "#%d" % bank)
-            mm(P[bank][:, 0:m], T.TG[:], SS[:, 0:m], False, True, "TG %s %s0" % (ss, ss), "#%d" % bank)
-            if c0: mm(P[7][:, 0:1], T.BO[:], SS[:, m:m + 1], True, True, "BO " + ss, "#7")
-            ts2(T.NG[:, c0:c1], T.F[:, c0:c1], -4096.0, A.mult, minus, A.add, "NN0 " + ftok, "NG")
-            extra[0]()
-            tt(T.NF[:, c0:c1], T.NG[:, c0:c1], T.JK[:, c0:c1], A.add, "NG JK", "NF")
-            extra[1]()
-            tt(T.Q[:, c0:c1], P[bank][:, 0:m], T.NF[:, c0:c1], A.max, "#%d NF" % bank, "Q")
-            extra[2]()
-            ts(T.PL[:, c0:c1], T.Q[:, c0:c1], plus, A.add, "Q NN", to)
-        def unflag(c0, c1, plus, ftok):
-            ts2(T.KP[:, c0:c1], T.Q[:, c0:c1], plus, A.add, 255.5, A.is_gt, "Q NN", "KP")
-            return lambda: tt(T.F[:, c0:c1], T.F[:, c0:c1], T.KP[:, c0:c1], A.mult, "KP " + ftok, ftok)
-
+        q = 4 * (1 - par)
         def nzf():
             ts(T.NZF[:], T.NZ[:, nz:nz + 64], 0.0, A.not_equal, "NZc", "NZF")
             for r in range(16): mm(P[6][:, 0:4], W(r), T.NZF[:, r::16], r == 0, r == 15, "WD NZF", "#6")
-        def i3():
+        def il():
+            cp(T.IL[:], T.I2[:], "I2", "IL")
             act(T.NZ[:, nz + 320:nz + 384], T.NZ[:, nz:nz + 128].indirect(T.IL[:]), "IL NZc NZo%d" % t, "NZo%d" % (t + 2))
-        q = 4 * (1 - par)
-        sr1 = lambda: tt(T.SR[:, q:q + 4], T.ACC[:, q:q + 4], T.OO[:, q:q + 4], A.add, "OO " + " ".join("ACC%d" % (q + c) for c in range(4)), "SRa")
-        go1 = lambda: tt(T.G4[:], P[6][:, 0:4], T.TB[:, 0:4], A.add, "#6 " + tb, "G4")
-        go2 = lambda: ts2(T.G3[:], T.G4[:], 0.0, A.is_equal, 384.0, A.mult, "G4", "G3")
-        go3 = lambda: tt(T.SR[:, 4 * par:4 * par + 4], T.G1[:], T.G3[:], A.max, "G1 G3", "SRb")
         def back():
             ts(T.WL[:], T.SR[:], 0.25, A.add, "SRa SRb", "WL")
             for f in range(3):
                 act(TRn[:, f * TW_:f * TW_ + 128], win(f).indirect(T.WL[:]), tri(f) + " WL", "TRo%d%d" % (1 - par, f))
         def free():
             ts(T.FW[:], T.SR[:], 383.5, A.is_gt, "SRa SRb", "FW")
-            first = True
             for p in range(2):
-                o = P[5][:, 4 * p:4 * p + 4]
-                mm(o, T.TI[:], T.FW[:, 0:4], True, False, "TI FW", "#5")
-                mm(o, T.TI[:] if p else T.TX[:], T.FW[:, 4:8], False, False, "TI TX FW", "#5")
+                o = P[4][:, 4 * p:4 * p + 4]
+                mm(o, T.TI[:], T.FW[:, 0:4], True, False, "TI FW", "#4")
+                mm(o, T.TI[:] if p else T.TX[:], T.FW[:, 4:8], False, False, "TI TX FW", "#4")
                 for d in range(1, 4):
                     for x in range(2):
-                        mm(P[5][:, 4 * p + d:4 * p + 4], T.BO[:], T.FW[:, 4 * x:4 * x + 4 - d], False, False, "BO FW", "#5")
-                mm(o, T.IK[:], T.FW[:, 4 * p:4 * p + 4], False, True, "IK FW", "#5")
-            return lambda: act(T.FB[:], P[5][:, 0:8], "#5", "FB", scale=40.0, bias=40 * 383.5)
-        o1 = lambda: tt(T.OO[:], T.FW[:], T.K1[:], A.mult, "FW K1", "OO")
-        o2 = lambda: tt(T.OO[:], T.OO[:], T.K2[:], A.add, "OO K2", "OO")
-        no = lambda: None
+                        mm(P[4][:, 4 * p + d:4 * p + 4], T.BO[:], T.FW[:, 4 * x:4 * x + 4 - d], False, False, "BO FW", "#4")
+                mm(o, T.IK[:], T.FW[:, 4 * p:4 * p + 4], False, True, "IK FW", "#4")
+        book = [nzf,
+                lambda: tt(T.I2[:], T.I1[:], T.CR[:, 0:4], A.add, "I1 CR", "I2"),
+                lambda: tt(T.G1[:], T.ACC[:, 4 * par:4 * par + 4], T.OV[:], A.add, "OV " + names("ACC%d", range(4 * par, 4 * par + 4)), "G1"),
+                il,
+                lambda: tt(T.SR[:, q:q + 4], T.ACC[:, q:q + 4], T.OO[:, q:q + 4], A.add, "OO " + names("ACC%d", range(q, q + 4)), "SRa"),
+                lambda: tt(T.OF[:, 0:4], P[6][:, 0:4], TB, A.add, "#6 " + tb, "OF"),
+                lambda: ts2(T.G3[:], T.OF[:, 0:4], 0.0, A.is_equal, 384.0, A.mult, "OF", "G3"),
+                lambda: tt(T.SR[:, 4 * par:4 * par + 4], T.G1[:], T.G3[:], A.max, "G1 G3", "SRb"),
+                back]
+        def nxt(k=1):
+            for _ in range(k): book.pop(0)()
 
         if not last:
-            top = 16 if t == 0 else 40
-            i3()
-            if t == 0: table(1)
-            tt(T.F[:, 0:top], P[2][:, 0:top], T.F[:, 0:top], A.max, "#2 Fa Fb Fc", "Fa Fb Fc")
-            places(s0, top, T.SSa, "SSa", 3, 1.0, -1.0, "Fa" if t else "Fc", (nzf, no, sr1))
-            if t == 0:
-                cp(L[:].indirect(T.PL[:, s0:top]), T.R[:, 16 * s0:16 * top], "PL R0", "L1")
-                go1()
-                act(T.NN[:, 0:1], P[7][:, 0:1], "#7", "NN", scale=-1.0, bias=256.0)
-                act(T.EB[:], T.CR[:, 0:16], "CR NN", "EB", bias=T.NN[:, 0:1])
-                go2()
-                scan(T.LW[:, 0:128], T.MB[:, 0:128], L[:, 0:128], 4096.0, A.max, A.min, "MB L1", "LW")
-                go3()
-                tt(T.EB[:, 0:8], T.EB[:, 0:8], T.LW[:, 15:128:16], A.min, "EB LW", "EB")
-                table(0)
-                cp(T.VL[:], T.EB[:], "EB", "VL")
+            s0 = 8 * (t + 1); top = 16 if t == 0 else 40; end = 32 if t == 0 else 40
+            thr, ttok = (T.TH0, "TH0") if t == 0 else (T.THR, "THR")
+            L = T["L%d" % (t + 1)]; e1 = (256, H, 0)[t]
+            nxt()
+            scan(T.XS[:], T.MB[:, 0:H], TW[:, V - H:V], 4096.0, A.max, A.min, "MB " + tw, "XS")
+            own_touches = lambda: scan(T.X[:, 0:16 * top], T.MB[:, 0:16 * top], TW[:, 0:16 * top], 4096.0, A.max, A.min, "MB " + tw, "X")
+            if e1: own_touches()
+            nxt()
+            tt(T.TS[:, 8 * t:8 * t + 8], T.XS[:, 15::16], T.THS[:], A.is_le, "XS THS", "TS%d" % t)
+            send_touches(T.TS[:, 8 * t:8 * t + 8], "TS%d" % t)
+            if not e1: own_touches()
+            tt(T.F[:, 8:top], T.X[:, H + 15:16 * top:16], thr[:, 8:top], A.is_le, "X " + ttok, "Fa")
+            tt(T.FN[:, 8:top], T.X[:, H + 15:16 * top:16], thr[:, 8:top], A.is_gt, "X " + ttok, "FNa")
+            tt(T.FO[:], T.X[:, 15:H:16], thr[:, 0:8], A.is_le, "X " + ttok, "FO")
+            ranks_of("a", s0, end, "Fa")
+            tt(T.NF[:, 8:top], T.FN[:, 8:top], T.JK[:, 8:top], A.mult, "FNa JK", "NFa")
+            places("a", s0, end, "NFa")
+            if t:
+                ranks_of("b", 8, s0, "Fa")
+                mm(na, T.BO[:], T.SSa[:, 40 - s0:41 - s0], True, True, "BO SSa", "#5")
+                places("b", 8, s0, "NFa")
+                ts2(T.GB[:], T.FO[:], -1.0, A.mult, 0.5, A.add, "FO", "GB")
+            nxt(2)
+            ts(T.PL[:, s0:end], P[5][:, s0:end], -1.0, A.add, "#5", "PLa")
+            act(L[:].indirect(T.PL[:, s0:end]), T.LG[:, 16 * s0:16 * end], "PLa LG", "L%d" % (t + 1), f=AF.Sigmoid)
+            if t:
+                cp(T.PL[:, 8:s0], P[5][:, 8:s0], "#5", "PLc")
+                act(T["M%d" % (t + 1)][:].indirect(T.PL[:, 8:s0]), T.LG[:, U + H:U + 16 * s0], "PLc LG", "M%d" % (t + 1), f=AF.Sigmoid)
+            ts(T.KP[:, s0:end], P[5][:, s0:end], 256.5, A.is_gt, "#5", "KPa")
+            nxt(5); free()
+            oo = [lambda: tt(T.OO[:], T.FW[:], T.K1[:, 0:8], A.mult, "FW K1", "OO"), lambda: tt(T.OO[:], T.OO[:], T.K1[:, 8:16], A.add, "OO K2", "OO")]
+            if e1:
+                scan(T.LW[:, 0:e1], T.MB[:, 0:e1], L[:, 0:e1], 4096.0, A.max, A.min, "MB L%d" % (t + 1), "LW")
+                oo[0](); decode(0, e1); oo[1](); o2(0, e1); o1(0, e1)
+                fix(t, 0); fix(t, 1)
             else:
-                act(T.NN[:, 0:1], P[7][:, 0:1], "#7", "NN0", scale=-1.0, bias=1.0)
-                act(T.NN[:, 1:2], P[7][:, 0:1], "#7", "NN", bias=-1.0)
-                act(L[:].indirect(T.PL[:, s0:top]), T.LG[:, 16 * s0:16 * top], "PL LG", "L%d" % (t + 1), f=AF.Sigmoid)
-                fa = unflag(s0, 40, -1.0, "Fa")
-                later.append(fa)
-            if t >= 1: act(T.N2[:], T.NZ[:, nz + 192:nz + 256], "NZo%d" % (t + 1), "N2", scale=2.0)
-            def his(mid, t=t):
-                scan(T.XM[:, 0:H], T.RS[:, 0:H], T.LT[:, t * H:(t + 1) * H], 0.0, A.mult, A.add, "RS LT%d" % t, "XM0 XM1")
-                mid()
-                tt(T.F[:, 0:8], T.XM[:, 15:H:16], T.F[:, 0:8], A.max, "XM0 Fb", "Fb")
-            def wrap():
-                scan(T.LW[:], T.MB[:], L[:, 0:256], 4096.0, A.max, A.min, "MB L%d" % (t + 1), "LW")
-            if t == 0:
-                back(); free()()
-                lists(first=True)
-                table(2); table(3)
-                for x in fix(t): x()
-                def rest():
-                    o1()
-                    ts2(T.F[:, 16:40], T.CR[:, 16:40], T.NN[:, 0:1], A.subtract, 255.5, A.is_gt, "CR NN", "Fa")
-                    fill(T.F[:, 8:16], 0.0, "Fb Fc")
-                    his(o2)
-                later.append(rest)
-            else:
-                his(later.pop())
-                places(0, s0, T.SSb, "SSb", 2, T.NN[:, 0:1], T.NN[:, 1:2], "Fb", (go1, go2, go3), "PM")
-                act(L[:].indirect(T.PL[:, 0:s0]), T.LG[:, U:U + 16 * s0], "PM LG", "L%d" % (t + 1), f=AF.Sigmoid)
-                back(); fb = unflag(0, s0, T.NN[:, 1:2], "Fb")
-                later.append(free())
-                fb(); o1()
-                for x in fix(t): x()
-                o2()
-                wrap()
-                ts2(T.VL[:], T.LW[:, 15::16], SLOPE, A.mult, 512.25 - SLOPE / 2, A.add, "LW", "VL")
-                lists()
+                oo[0](); oo[1]()
+                st = piece_b(t, 0)
+                st[0](); st[1](); fix(t, 0); st[2](); st[3](); fix(t, 1); st[4](); st[5]()
+            late.append(lambda: act(T.FB[:], P[4][:, 0:8], "#4", "FB", scale=40.0, bias=40 * 383.5))
+            late.extend(unflag(t))
         else:
-            i3(); nzf(); sr1(); go1(); go2(); go3(); back()
-            for c0, c1, bank in ((8, 40, 2), (0, 8, 3)):
+            send_touches(TW[:, V - H:V], tw)
+            arrival("ls", "gone", half * RO)
+            dma("s", T.yd[:, H:V - H], T.D[:, H:V - H], "Dm sent%d gone" % t, "y0")
+            iota(TR[:, 384::TW_], [[0, 3]], -1, 0, "TRx%d" % par)
+            nxt()
+            ts(T.TH[:], TW[:, 0:U], 0.75, A.is_lt, tw, "TH")
+            nxt(8)
+            for c0, c1, bank in ((0, 8, 3), (8, 40, 2)):
                 m = 16 * (c1 - c0)
                 mm(P[bank][0:8, 0:m], T.SEL[:, 0:8], T.TH[:, 16 * c0:16 * c1], True, False, "SEL TH", "#%d" % bank)
                 for r in range(16):
-                    mm(P[bank][0:8, r:m:16], T.SEL[:, 8 * r:8 * r + 8], T.F[:, c0:c1], False, bank == 2 and r == 15, "SEL Fa Fb", "#%d" % bank)
+                    mm(P[bank][0:8, r:m:16], T.SEL[:, 8 * r:8 * r + 8], T.FK[:, c0:c1], False, r == 15, "SEL FK", "#%d" % bank)
+            ts(T.XS[0:8, :], P[3][0:8, 0:H], 0.75, A.add, "#3", "XS")
             ts(T.YF[0:8, H:U], P[2][0:8, :], 0.5, A.is_gt, "#2", "YFa")
             for p in range(2):
-                act(T.YZ[:, p::2], T.NZ[:, 128 * (4 + p) + 64:128 * (5 + p)], "NZo%d" % (4 + p), "YZ%d" % p, scale=-1.0)
-            dma("s", T.yz[:], T.YZ[:], "YZ0 YZ1", "y1")
+                act(T.M16[:, p::2], T.NZ[:, 128 * (4 + p) + 64:128 * (5 + p)], "NZo%d" % (4 + p), "YZ%d" % p, scale=-1.0)
+            dma("s", T.yz[:], T.M16[:], "YZ0 YZ1", "y1")
             for f in range(3):
                 for p in range(2):
                     mm(P[4][0:8, 128 * f + p:128 * (f + 1):2], T.SE0[:], TRn[:, f * TW_ + 64 * p:f * TW_ + 64 * p + 64], True, True,
                        "SE0 TRo%d%d" % (1 - par, f), "#4")
-            ts2(T.S[0:8, 0:384], P[4][0:8, 0:384], float(NONE), A.is_equal, -1.0 - NONE, A.mult, "#4", "S0")
-            tt(T.YT[0:8, :], P[4][0:8, 0:384], T.S[0:8, 0:384], A.add, "#4 S0", "YT")
-            dma("s", T.yt[:], T.YT[0:8, :], "YT", "y2")
-            for x in fix(t): x()
-            dma("s", T.yd[:, 0:H], T.D[:, 0:H], "Dl", "y3")
-            dma("a", T.yd[:, V - H:V], T.D[:, V - H:V], "Dr", "y4")
-            mm(P[3][0:8, 0:H], T.BO[:, 0::16], T.LT[:, t * H:(t + 1) * H], False, True, "BO LT%d" % t, "#3")
-            ts(T.YF[0:8, 0:H], P[3][0:8, 0:H], 0.5, A.is_gt, "#3", "YFb")
+            act(T.X[0:8, 0:384], P[4][0:8, 0:384], "#4", "X")
+            dma("a", T.yt[:], T.X[0:8, 0:384], "X", "y2")
+            fix(t, 0); dma("s", T.yd[:, 0:H], T.D[:, 0:H], "Dl", "y3")
+            fix(t, 1); dma("a", T.yd[:, V - H:V], T.D[:, V - H:V], "Dr", "y4")
+            mm(P[7][0:8, 0:H], T.SE0[:], T.LU[:], True, True, "SE0 LT%d" % t, "#7")
+            tt(T.YF[0:8, 0:H], P[7][0:8, 0:H], T.XS[0:8, :], A.is_lt, "#7 XS", "YFb")
             dma("s", T.yf[:], T.YF[0:8, :], "YFa YFb", "y5")
             op("s", None, "y0 y1 y2 y3 y4 y5", "")
     emit(g, T, ops)
-    g.wait_ge(T.sem.ls, 3 * half * RO)
+    g.wait_ge(T.sem.ls, half * RO)

@@ -7,8 +7,11 @@ NONE = 1280
 JUNK = 1288
 DW = 1800
 TW_ = 392
-P1 = 192
-PT = 64
+P1 = 128
+KT = 6
+K0, PFV, CV, SA, SB, DE3 = 6, 0, 2, 2, 2, "v"
+KB, E0 = 4, 0
+CUTS = [[0, 16, 40, 64, 96, 128, 160, 192, 224, 256]] * 4
 ALPHA = math.log(1.7)
 U0 = -6.0 - 272 * ALPHA
 SLOPE = 32776.0
@@ -28,8 +31,8 @@ SCRATCH = {
     "VV": ("sbuf", [128, 256], BF), "WIN": ("sbuf", [128, 256], BF), "PR": ("sbuf", [128, 256], BF), "PF": ("sbuf", [128, 256], BF),
     "WB": ("sbuf", [128, 256], F16), "WC": ("sbuf", [128, 256], F16), "TRASH": ("sbuf", [128, 12 * 256], BF),
     "TR0": ("sbuf", [128, 3 * TW_], F32), "TR1": ("sbuf", [128, 3 * TW_], F32),
-    "ACC": ("sbuf", [128, 12], F32), "OO": ("sbuf", [128, 8], F32), "LG": ("sbuf", [128, 1024], F32), "OV": ("sbuf", [128, 4], F32),
-    "FB": ("sbuf", [128, 8], F32), "FW": ("sbuf", [128, 8], BF), "SL": ("sbuf", [128, 12], U16),
+    "ACC": ("sbuf", [128, 12 * 64], F32), "OO": ("sbuf", [128, 8], F32), "LG": ("sbuf", [128, 1024], F32), "OV": ("sbuf", [128, 4], F32),
+    "FB": ("sbuf", [128, 8], F32), "FQ": ("sbuf", [128, 8], F32), "FW": ("sbuf", [128, 16], BF), "SL": ("sbuf", [128, 12], U16),
     "XM": ("sbuf", [128, 192], F16), "XW": ("sbuf", [128, 192], F32), "XL": ("sbuf", [128, 12], U16), "ZC": ("sbuf", [128, 192], F32),
     "Z": ("sbuf", [128, 3, 128], F16), "E0": ("sbuf", [128, 144], BF), "E1": ("sbuf", [128, 288], BF),
     "E2": ("sbuf", [128, 432], BF), "E3": ("sbuf", [128, 576], BF), "ES": ("sbuf", [128, 4 * 288], BF), "OL": ("sbuf", [128, 12], U16),
@@ -45,18 +48,18 @@ SCRATCH = {
     "LS": ("sbuf", [128, 256], F32), "LW": ("sbuf", [128, 256], F32),
     "VL": ("sbuf", [128, 16], U16), "EA": ("sbuf", [128, 16], F32), "EB": ("sbuf", [128, 16], F32), "EL": ("sbuf", [128, 16], U16),
     "PI": ("sbuf", [128, 4], I32), "PC": ("sbuf", [128, 8], F32), "IF": ("sbuf", [128, 256], F32),
-    "J16": ("sbuf", [128, U], F32), "R": ("sbuf", [128, 256], F32), "ET": ("sbuf", [128, 1032], F32),
+    "J16": ("sbuf", [128, H], F32), "R": ("sbuf", [128, 256], F32), "ET": ("sbuf", [128, 1032], F32),
     "M16": ("sbuf", [128, 128], F32), "WD": ("sbuf", [128, 144], BF), "BO": ("sbuf", [128, 128], BF), "BH": ("sbuf", [128, 128], F16),
     "BT": ("sbuf", [128, 128], BF), "TI": ("sbuf", [128, 128], BF), "TG": ("sbuf", [128, 128], BF), "TX": ("sbuf", [128, 128], BF),
     "IK": ("sbuf", [128, 128], BF), "IH": ("sbuf", [128, 128], F16), "ONE": ("sbuf", [128, 256], BF), "IM": ("sbuf", [128, 256], F32),
-    "MB": ("sbuf", [128, U], F32), "RS": ("sbuf", [128, 192], F16), "ZM": ("sbuf", [128, 128], F32), "CR": ("sbuf", [128, 40], F32),
+    "MB": ("sbuf", [128, U], F32), "RS": ("sbuf", [128, 192], BF), "ZM": ("sbuf", [128, 128], F32), "CR": ("sbuf", [128, 40], F32),
     "JK": ("sbuf", [128, 40], F32), "J12": ("sbuf", [128, 12], F32), "K1": ("sbuf", [128, 16], F32),
     "C1": ("sbuf", [128, 16], F32), "TH0": ("sbuf", [128, 40], F32), "THS": ("sbuf", [128, 8], F32),
-    "QT": ("sbuf", [128, 4], F32), "SEL": ("sbuf", [128, 128], BF), "SE0": ("sbuf", [128, 8], F32),
-    "TS": ("sbuf", [128, 8 * RO], F32), "TH": ("sbuf", [128, U], BF),
+    "QT": ("sbuf", [128, 4], F32), "SEL": ("sbuf", [128, 144], BF), "CT": ("sbuf", [128, 400], F32),
+    "TS": ("sbuf", [128, 8 * RO], F32),
     "YF": ("sbuf", [128, 640], F32),
     "LL": ("sbuf", [128, RO * H], F32), "LR": ("sbuf", [128, RO * H], F32), "LT": ("sbuf", [128, 8 * RO], F32),
-    "LU": ("sbuf", [128, H], F32),
+    "LU": ("sbuf", [128, H], BF),
 }
 for _t in range(RO):
     SCRATCH["TW%d" % _t] = ("sbuf", [128, DW], F32)
@@ -85,6 +88,12 @@ def mask_of(engines):
     return m
 
 
+def first_hop(engines, t):
+    h = len(engines) // 2
+    if t == 0 and E0: return engines[1:h:2], engines[0:h:2], engines[h:]
+    return engines[1::2], engines[0::2], engines[1::2]
+
+
 def touch_piece(T, t):
     return T.LT[:, 8 * t:8 * t + 8] if t < RO - 1 else T.LU[:]
 
@@ -101,7 +110,7 @@ def relay_program(g, core, T, topo):
         rid, pid = topo.addr(dst, core); m = topo.mask(core, dst); k = len(topo.engines(core, dst))
         for t in range(RO):
             piece = T[buf][:, t * H:(t + 1) * H] if role < 2 else touch_piece(T, t)
-            g.wait_ge(T.sem[sem + str(t)], len(topo.engines(T.cores[rank], core)) // 2)
+            g.wait_ge(T.sem[sem + str(t)], len(first_hop(topo.engines(T.cores[rank], core), t)[role]))
             g.remote_dma(piece, piece, T.sem[sem + str(t)], T.sem.ls, pid, rid, m)
         g.wait_ge(T.sem.ls, k * RO)
 
@@ -186,92 +195,103 @@ def rank_program(g, core, T, topo):
     W = lambda k: T.WD[:, 15 - k:143 - k]
     Dr = T.D[:, 0:JUNK]; DD = "Dl Dm Dr Dx"
     NL = 256 - P1
+    acc = lambda j0, j1: T.ACC[:, 64 * j0 + 63:64 * j1:64]
 
-    dma("s", T.B2[:, 0:64], T.b2[:, 0:64], "", "B2a")
-    dma("a", T.B1[:, 0:64], T.b1[:, 0:64], "", "B1a")
+    dma("s", T.B2[:, 0:256], T.b2[:, 0:256], "", "B2a")
+    dma("a", T.B1[:, 0:256], T.b1[:, 0:256], "", "B1a")
     dma("s", T.D[0:64, 0:V], T.dist[0:64, :], "", "Dl Dm Dr")
     dma("a", T.D[64:128, 0:V], T.dist[64:128, :], "", "Dn")
-    dma("s", T.B2[:, 64:256], T.b2[:, 64:256], "", "B2b")
-    dma("s", T.B1[:, 64:256], T.b1[:, 64:256], "", "B1b")
-    dma("s", T.B2[:, 256:U], T.b2[:, 256:U], "B1b B2b", "B2c")
+    dma("s", T.B2[:, 256:U], T.b2[:, 256:U], "Dm Dn", "B2c")
     dma("s", T.B1[:, 256:U], T.b1[:, 256:U], "", "B1c")
     dma("s", T.B2[:, U:1024], T.b2[:, 0:384], "", "B2d")
     dma("s", T.B1[:, U:1024], T.b1[:, 0:384], "", "B1d")
-    BB1, BB2 = "B1a B1b B1c B1d B1x", "B2a B2b B2c B2d B2x"
+    BB1, BB2 = "B1a B1c B1d B1x", "B2a B2c B2d B2x"
 
     iota(T.PI[:, 0:1], [[0, 1]], 0, 1, "PI", whole=True)
     iota(T.CR[:], [[16, 40]], 0, 0, "CR")
-    iota(T.M16[:], [[16, 8], [0, 16]], 0, 0, "M16")
     iota(T.R[:, 0:256], [[1, 256]], 0, 0, "R0")
-    iota(T.J16[:], [[0, 40], [1, 16]], 0, 0, "J16")
-    iota(T.FB[:], [[1, 2], [32, 4]], 0, 0, "FB")
-    fill(T.D[:, V:JUNK], 1e9, "Dx")
-    fill(T.QT[:], 0.25, "QT")
-    for b0, b1 in ((1, 2), (3, 5), (6, 7)):
-        fill(T.ZM[:, 16 * b0:16 * b1], 0.0, "ZM%d" % b0)
+    iota(T.M16[:], [[16, 8], [0, 16]], 0, 0, "M16")
+    iota(T.J16[:], [[0, 8], [1, 16]], 0, 0, "J16")
+    iota(T.FQ[:], [[2, 2], [64, 4]], 1, 0, "FQ")
     fill(T.ONE[:], 1.0, "ONE")
-    fill(T.OO[:], 128.0, "OO")
-    for f in range(3):
-        fill(T.TR0[:, f * TW_:f * TW_ + 128], float(NONE), "TRo0%d" % f)
-    fill(T.TR0[:, 384::TW_], float(NONE), "TRx0"); fill(T.TR1[:, 384::TW_], float(NONE), "TRx1")
-    fill(T.NZ[:, 64:128], 0.0, "NZo0"); fill(T.NZ[:, 192:256], 0.0, "NZo1")
-    fill(T.F[:, 16:40], 1.0, "Fa"); fill(T.NF[:, 16:40], 0.0, "NFa"); fill(T.KP[:], 1.0, "KPa KPb KPc")
-    for s in "abc": fill(T["SS" + s][:, 0:1], 0.0, "SS%s0" % s)
+    act(T.L1[:, 0:256], T.ONE[:], "ONE", "L1", f=AF.Sigmoid, scale=(1024 - 512) / 8192)
     ts(T.PI[:, 2:3], T.PI[:, 0:1], 15, A.bitwise_and, "PI", "PJ0")
     ts(T.PI[:, 3:4], T.PI[:, 0:1], 112, A.bitwise_and, "PI", "PJ1")
+    fill(T.D[:, V:JUNK], 1e9, "Dx")
     cp(T.PC[:, 0:2], T.PI[:, 2:4], "PJ0 PJ1", "PC")
+    fill(T.NF[:, 16:40], 0.0, "NFa")
     rr, gg = T.PC[:, 0:1], T.PC[:, 1:2]
     ts(T.CR[:], T.CR[:], rr, A.add, "CR PC", "CR")
     ts2(T.PC[:, 2:3], rr, -ALPHA, A.mult, U0, A.add, "PC", "PC2")
     ts(T.PC[:, 3:4], gg, 15.0, A.add, "PC", "PC3")
-    act(T.TH0[:], T.CR[:], "CR", "TH0", f=AF.Sigmoid, scale=1.0 / 8192, bias=0.5 / 8192)
-    act(T.THS[:], T.CR[:, 0:8], "CR", "THS", f=AF.Sigmoid, scale=1.0 / 8192, bias=(V - H + 0.5) / 8192)
-    ts(T.BO[:], T.M16[:], gg, A.is_equal, "M16 PC", "BO")
-    ts(T.BH[:], T.M16[:], gg, A.is_equal, "M16 PC", "BH")
-    ts2(T.BT[:], T.M16[:], gg, A.is_equal, 0.390625, A.mult, "M16 PC", "BT")
+    ts(T.PC[:, 7:8], rr, 4.0, A.mult, "PC", "PC7")
+    ts2(T.PC[:, 6:7], rr, 15.5 - KT, A.is_gt, 8 * 17 * ALPHA, A.mult, "PC", "PC6")
+    ts2(T.IF[:, 0:128], T.R[:, 0:128], gg, A.subtract, rr, A.is_equal, "R0 PC", "IF")
     ts2(T.WD[:], T.R[:, 0:144], T.PC[:, 3:4], A.is_equal, 0.0625, A.mult, "R0 PC3", "WD")
     ts2(T.IH[:], T.R[:, 0:128], gg, A.subtract, rr, A.is_equal, "R0 PC", "IH")
-    ts2(T.FB[:], T.FB[:], rr, A.add, rr, A.add, "FB PC", "FB")
-    cp(T.O2[:, 0:64], T.B2[:, 0:64], "B2a", "O20")
-    cp(T.O1[:, 0:64], T.B1[:, 0:64], "B1a", "O10")
-    ts(T.IM[:], T.J16[:, 0:256], rr, A.is_equal, "J16 PC", "IM")
-    ts2(P[0][:, 256:448], T.J16[:, 0:192], rr, A.is_equal, 8192.0, A.mult, "J16 PC", "#0")
-    ts2(T.IF[:, 0:128], T.R[:, 0:128], gg, A.subtract, rr, A.is_equal, "R0 PC", "IF")
-    act(T.IF[:, 128:256], T.IF[:, 0:128], "IF", "NI", scale=-1.0)
-    act(T.PC[:, 4:5], T.PC[:, 2:3], "PC2", "PC4", bias=8 * 17 * ALPHA)
-    ts(T.RS[:], T.J16[:, 0:192], 0.5, A.is_gt, "J16", "RS")
-    for b in (0, 2, 5, 7):
-        ts2(T.ZM[:, 16 * b:16 * b + 16], T.J16[:, 0:16], rr, A.is_ge, float(NONE), A.mult, "J16 PC", "ZM%d" % b)
-    ts2(T.MB[:], T.J16[:], rr, A.is_equal, 4096.0, A.mult, "J16 PC", "MB")
-    act(T.FB[:], T.FB[:], "FB", "FB", scale=40.0, bias=20.0)
-    act(T.JK[:], T.CR[:], "CR", "JK", bias=float(U))
+    ts(T.IF[:, 128:256], T.IF[:, 0:128], -1.0, A.mult, "IF", "NI")
+    ts(T.PC[:, 4:5], T.PC[:, 6:7], T.PC[:, 2:3], A.add, "PC2 PC6", "PC4")
+    ts2(T.PC[:, 5:6], T.PC[:, 6:7], -1.0, A.mult, 16 * 17 * ALPHA, A.add, "PC6", "PC5")
+    ts(T.BH[:], T.M16[:], gg, A.is_equal, "M16 PC", "BH")
+    ts2(T.BT[:], T.M16[:], gg, A.is_equal, 0.390625, A.mult, "M16 PC", "BT")
+    ts(T.BO[:], T.M16[:], gg, A.is_equal, "M16 PC", "BO")
+    ts(T.IM[:, 0:H], T.J16[:], rr, A.is_equal, "J16 PC", "IM0")
+    ts2(T.ZM[:], T.J16[:], rr, A.is_ge, float(NONE), A.mult, "J16 PC", "ZM")
+    ts(T.FQ[:], T.FQ[:], T.PC[:, 7:8], A.add, "FQ PC7", "FQ")
+    cp(T.O2[:], T.B2[:, 0:256], "B2a", "O20 O21 O22 O23")
+    cp(T.O1[:], T.B1[:, 0:256], "B1a", "O10 O11 O12 O13")
+    zm = " ZM"
+    sel(T.QT[:], T.R[:, 0:4], [[0, 4]], A.is_gt, 0, 0, "R0", "QT", 0.25)
+    iota(T.OO[:], [[0, 8]], 128, 0, "OO")
+    for f in range(3): iota(T.TR0[:, f * TW_:f * TW_ + 128], [[0, 128]], NONE, 0, "TRo0%d" % f)
+    iota(T.TR0[:, 384::TW_], [[0, 3]], NONE, 0, "TRx0"); iota(T.TR1[:, 384::TW_], [[0, 3]], NONE, 0, "TRx1")
+    for b0, b1 in ((1, 2), (3, 5), (6, 7)): iota(T.ZM[:, 16 * b0:16 * b1], [[0, 16 * (b1 - b0)]], 0, 0, "ZM")
+    iota(T.NZ[:, 64:128], [[0, 64]], 0, 0, "NZo0"); iota(T.NZ[:, 192:256], [[0, 64]], 0, 0, "NZo1")
+    iota(T.F[:, 16:40], [[0, 24]], 1, 0, "Fa"); iota(T.KP[:], [[0, 40]], 1, 0, "KPa KPb KPc")
+    for s in "abc": iota(T["SS" + s][:, 0:1], [[0, 1]], 0, 0, "SS%s0" % s)
+
+    iota(T.TR0[:, 128:384], [[1, 256]], 0, 0, "TRn00 TRn01")
     act(T.J12[:], T.CR[:, 0:12], "CR", "J12", bias=float(JUNK))
-    act(T.K1[:, 0:8], T.CR[:, 0:8], "CR", "K1", scale=-1.0, bias=384.0)
-    act(T.K1[:, 8:16], T.CR[:, 0:8], "CR", "K2", bias=-256.0)
-    act(T.C1[:], T.CR[:, 0:16], "CR", "C1", bias=1.0)
-    zm = " ZM0 ZM1 ZM2 ZM3 ZM5 ZM6 ZM7"
+    for c0, m in ((0, H), (H, 64)):
+        act(T.RS[:, c0:c0 + m], T.J16[:, 0:m], "J16", "RS%d" % c0, f=AF.Sign)
+        act(P[0][:, 256 + c0:256 + c0 + m], T.IM[:, 0:m], "IM0", "#0", scale=8192.0)
+    act(T.FB[:], T.FQ[:], "FQ", "FB", scale=20.0)
+    def ring_constants():
+        act(T.TH0[:], T.CR[:], "CR", "TH0", f=AF.Sigmoid, scale=1.0 / 8192, bias=0.5 / 8192)
+        act(T.THS[:], T.CR[:, 0:8], "CR", "THS", f=AF.Sigmoid, scale=1.0 / 8192, bias=(V - H + 0.5) / 8192)
+        for c0 in (0, H): act(T.MB[:, c0:c0 + H], T.IM[:, 0:H], "IM0", "MB%d" % c0, scale=4096.0)
+        act(T.JK[:], T.CR[:], "CR", "JK", bias=float(U))
+        act(T.LG[:, H:256], T.R[:, H:256], "R0", "LGa", scale=1.0 / 8192, bias=-512.0 / 8192)
+        act(T.C1[:], T.CR[:, 0:16], "CR", "C1", bias=1.0)
+    def list_constants():
+        act(T.IM[:, H:256], T.IM[:, 0:H], "IM0", "IM")
+        act(T.CT[:, 0:265:264], T.ONE[:, 0:2], "ONE", "CT0", f=AF.Sigmoid, scale=(1024 - 512) / 8192)
+        act(T.CT[:, 265:393], T.ET[:, 512:U], "ET", "CT1", f=AF.Sigmoid, scale=1.0 / 8192, bias=-512.0 / 8192)
+        act(T.CT[:, 1:257], T.ET[:, 256:512], "ET CT0 CT1", "CT", f=AF.Sigmoid, scale=1.0 / 8192, bias=-512.0 / 8192)
+        act(T.K1[:, 0:8], T.CR[:, 0:8], "CR", "K1", scale=-1.0, bias=384.0)
+        act(T.K1[:, 8:16], T.CR[:, 0:8], "CR", "K2", bias=-256.0)
+        act(T.MB[:, 256:384], T.IM[:, 0:H], "IM0", "MB256", scale=4096.0)
 
     def ones(t):
         TW = T["TW%d" % t]; m = 256 if t == 0 else U
         iota(TW[:, 0:m], [[0, m]], 1, 0, "TW%d" % t); iota(TW[:, V - H:V], [[0, H]], 1, 0, "TW%d" % t)
-    def blank(name, tok): sel(T[name][:, 0:264], T.J16[:, 0:264], [[0, 264]], A.is_gt, 0, 0, "J16", tok, code(1024))
+    def blank(name, tok): sel(T[name][:, 0:264], T.ET[:, 0:264], [[0, 264]], A.is_gt, 0, 0, "ET", tok, code(1024))
     ones(0)
     sel(T.TI[:], T.BO[:], [[1, 128]], A.is_ge, 0, -1, "BO", "TI")
     sel(T.TG[:], T.BO[:], [[-1, 128]], A.is_gt, 0, 1, "BO", "TG")
-    sel(T.TX[:], T.BO[:], [[1, 128]], A.is_gt, 0, -1, "BO", "TX")
+    iota(T.TX[:], [[0, 128]], -1, 0, "TX"); iota(T.FW[:, 8:9], [[0, 1]], 0, 0, "FS0")
+    sel(T.TX[:], T.TX[:], [[-1, 128]], A.is_equal, 0, 1, "TX", "TX")
     iota(T.IK[:], [[0, 128]], -384, 0, "IK")
     sel(T.IK[:], T.IK[:], [[-1, 128]], A.is_equal, 0, 1, "IK", "IK")
-    iota(T.LG[:], [[1, 1024]], -512, 0, "LG")
     iota(T.ET[:, 0:U], [[1, U]], 0, 0, "ET"); iota(T.ET[:, U:1032], [[1, 392]], 0, 0, "ET")
+    iota(T.LG[:, 256:1024], [[1, 768]], -256, 0, "LG")
     iota(T.B1[:, 1024:1032], [[0, 8]], NONE, 0, "B1x", whole=True); iota(T.B2[:, 1024:1032], [[0, 8]], NONE, 0, "B2x", whole=True)
 
     def late_constants(t):
-        if t + 1 < RO: ones(t + 1); blank("L%d" % (t + 1), "L%d" % (t + 1))
-        if 1 <= t < RO - 1: blank("M%d" % (t + 1), "M%d" % (t + 1))
+        if t + 1 < RO: ones(t + 1)
+        if 1 <= t < RO - 1: blank("L%d" % (t + 1), "L%d" % (t + 1)); blank("M%d" % (t + 1), "M%d" % (t + 1))
         if t == 2:
-            sel(T.SEL[:], T.ONE[:, 0:128], [[-1, 16], [-16, 8]], A.is_equal, 0, 1, "ONE", "SEL")
-            iota(T.SE0[:], [[0, 8]], 1, 0, "SE0")
-            sel(T.SE0[:], T.SE0[:], [[-16, 8]], A.is_equal, 0, 1, "SE0", "SE0")
+            sel(T.SEL[:], T.ONE[:, 0:144], [[-1, 144]], A.is_equal, 0, 1, "ONE", "SEL")
 
     lower = (rank < (rank - 1) % n, rank < (rank + 1) % n)
     sides = ((0, "Dl", "LL"), (V - H, "Dr", "LR"))
@@ -279,6 +299,9 @@ def rank_program(g, core, T, topo):
 
     def o2(e0, e1): cp(T.O2[:, e0:e1], T.B2[:].indirect(T.VL[:, e0 // 16:e1 // 16]), BB2 + " VL%d VL%d" % (e0 // H, (e1 - 1) // H), names("O2%d", q4(e0, e1)))
     def o1(e0, e1): cp(T.O1[:, e0:e1], T.B1[:].indirect(T.VL[:, e0 // 16:e1 // 16]), BB1 + " VL%d VL%d" % (e0 // H, (e1 - 1) // H), names("O1%d", q4(e0, e1)))
+    def numbers(e0=0, e1=256):
+        cp(P[1][:, e0:e1], T.O1[:, e0:e1], names("O1%d", q4(e0, e1)), "#1")
+        cp(P[1][:, 256 + e0:256 + e1], T.O2[:, e0:e1], names("O2%d", q4(e0, e1)), "#1")
     def decode(e0, e1):
         ts2(T.VL[:, e0 // 16:e1 // 16], T.LW[:, e0 + 15:e1:16], SLOPE, A.mult, 512.25 - SLOPE / 2, A.add, "LW", names("VL%d", range(e0 // H, e1 // H)))
     def own_numbers(e0):
@@ -294,7 +317,7 @@ def rank_program(g, core, T, topo):
         mm(o, T.TI[:], SS[:, 1:1 + m], True, False, "TI SS" + s, "#5")
         mm(o, T.TG[:], SS[:, 0:m], False, False, "TG SS%s SS%s0" % (s, s), "#5")
         mm(o, T.IH[:], T.NF[:, c0:c1], False, True, "IH " + ntok, "#5")
-    na, nab = P[5][:, 40:41], P[5][:, 41:42]
+    na, nab = P[5][:, 40:41], P[3][:, 508:509]
 
     def piece_b(t, e0):
         s0 = 8 * (t + 1); his = T.LT[:, 8 * t:8 * t + 8]; L, M = T["L%d" % (t + 1)], T["M%d" % (t + 1)]; c = e0 // 16
@@ -305,13 +328,13 @@ def rank_program(g, core, T, topo):
             ranks_of("c", 0, 8, "Fb")
             tt(T.NF[:, 0:8], T.FN[:, 0:8], T.JK[:, 0:8], A.mult, "FNb JK", "NFb")
             places("c", 0, 8, "NFb")
-            mm(nab, T.BO[:], T.SSa[:, 40 - s0:41 - s0], True, False, "BO SSa", "#5")
-            mm(nab, T.BO[:], T.SSc[:, 8:9], False, True, "BO SSc", "#5")
+            mm(nab, T.BO[:], T.SSa[:, 40 - s0:41 - s0], True, False, "BO SSa", "#3")
+            mm(nab, T.BO[:], T.SSc[:, 8:9], False, True, "BO SSc", "#3")
         def s3():
             ts2(T.PL[:, 0:8], P[5][:, 0:8], na, A.add, -1.0, A.add, "#5", "PLb")
             act(L[:].indirect(T.PL[:, 0:8]), T.LG[:, U:U + H], "PLb LG", "L%d" % (t + 1), f=AF.Sigmoid)
-            ts(T.OFF[:, c:16], T.C1[:, c:16], nab, A.subtract, "C1 #5", "OFF")
-        def s4(): tt(T.LS[:, e0:256], M[:, 0:264].indirect(T.OFF[:, c:16]), T.IM[:, e0:256], A.mult, "M%d OFF IM" % (t + 1), "LS")
+            ts(T.OFF[:, c:16], T.C1[:, c:16], nab, A.subtract, "C1 #3", "OFF")
+        def s4(): tt(T.LS[:, e0:256], M[:, 0:264].indirect(T.OFF[:, c:16]), T.IM[:, e0:256], A.mult, "M%d OFF IM0 IM" % (t + 1), "LS")
         def s5(): scan(T.LW[:, e0:256], T.LS[:, e0:256], L[:, e0:256], 0.0, A.max, A.min, "LS L%d" % (t + 1), "LW")
         return [s1, s2, s3, s4, s5, lambda: decode(e0, 256)]
     def unflag(t):
@@ -320,15 +343,17 @@ def rank_program(g, core, T, topo):
             st = [lambda: tt(T.F[:, 0:8], T.LT[:, 0:8], T.FO[:], A.max, "LT0 FO", "Fb")]
         else:
             st = [lambda: ts2(T.KP[:, 0:8], P[5][:, 0:8], na, A.add, 256.5, A.is_gt, "#5", "KPb"),
-                  lambda: ts2(T.KP[:, 8:s0], P[5][:, 8:s0], nab, A.add, 256.5, A.is_gt, "#5", "KPc")]
-        st.append(lambda: tt(T.FK[:], T.F[:], T.KP[:], A.mult, "Fa Fb KPa KPb KPc", "FK"))
+                  lambda: ts2(T.KP[:, 8:s0], P[5][:, 8:s0], nab, A.add, 256.5, A.is_gt, "#5 #3", "KPc")]
+        st.append(lambda: tt(T.FK[:], T.F[:], T.KP[:], A.mult, "Fa Fb Fc KPa KPb KPc", "FK"))
         if t + 2 < RO: st.append(lambda: tt(T.THR[:], T.FK[:], T.TH0[:], A.max, "FK TH0", "THR"))
+        else: st.append(lambda: ts(T.KP[:], T.FK[:], 0.75, A.add, "FK", "KPa KPb KPc"))
         return st
     def fix(t, s):
         c0, tok, land = sides[s]
         tt(T.D[:, c0:c0 + H], P[0][:, s * H:(s + 1) * H], T[land][:, t * H:(t + 1) * H], A.add, "#0 %s%d sent%d" % (land, t, t), tok)
 
     late = []
+    spare = []
     def one():
         if late: late.pop(0)()
 
@@ -337,142 +362,185 @@ def rank_program(g, core, T, topo):
         DX = DD + (" Dn" if t == 0 else "")
         last = t == RO - 1
         new = lambda f, e0, e1: TR[:, f * TW_ + 128 + e0:f * TW_ + 128 + e1]
-        tri = lambda f: "TRo%d%d TRx%d TRn%d0 TRn%d1" % (par, f, par, f, f)
+        tri = lambda f, par=par: "TRo%d%d TRx%d TRn%d0 TRn%d1" % (par, f, par, f, f)
 
-        def g2(e0, e1):
-            act(T.G2[:, 16 * e0:16 * e1], Dr.indirect(T.O2[:, e0:e1]), DX + " " + names("O2%d", q4(e0, e1)), "G2%d" % e0)
+        def g2(e0, e1, eng="a"):
+            (cp if eng == "v" else act)(T.G2[:, 16 * e0:16 * e1], Dr.indirect(T.O2[:, e0:e1]), DX + " " + names("O2%d", q4(e0, e1)), "G2%d" % e0)
         def add(e0, e1):
             tt(T.S[:, 16 * e0:16 * e1], Dr.indirect(T.O1[:, e0:e1]), T.G2[:, 16 * e0:16 * e1], A.add,
                DX + " G2%d " % e0 + names("O1%d", q4(e0, e1)), "S%d" % e0)
-        cuts = [0, 16, 40, 64, 96, 128, 160, 192, 224, 256]
+        cuts = CUTS[t]
         chunks = list(zip(cuts, cuts[1:]))
-        def compare(e0, e1, bank):
-            m = e1 - e0; s = names("S%d", [x for x in cuts if e0 <= x < e1])
+        def compare(e0, e1, bank, mid={}):
+            c0 = 16 * e0
             for k in range(16):
-                cm = T.CM[:, 16 * e0 + k * m:16 * e0 + (k + 1) * m]
-                tt(cm, P[0][:, e0:e1], T.S[:, 16 * e0 + k:16 * e1:16], A.is_gt, "#0 " + s, "CM%d_%d" % (e0, k))
-                mm(P[bank][:, e0 % P1:e0 % P1 + m], W(k), cm, k == 0, k == 15, "WD CM%d_%d" % (e0, k), "#%d" % bank)
-                if e0 == PT and k >= 8: sum_signs(2 * k - 16, 2 * k - 14)
-        def differ(own, tok):
-            s = names("S%d", [x for x in cuts if x < PT])
-            for k in range(16):
-                o = P[6 + k // 8][:, PT * (k % 8):PT * (k % 8 + 1)]; b = "#%d" % (6 + k // 8)
-                if own is not None: mm(o, T.IF[:, 0:128], own, k % 8 == 0, False, "IF " + tok, b)
-                else: mm(o, T.IF[:, 128:256], T.S[:, k:16 * PT:16], False, k % 8 == 7, "NI " + s, b)
+                if k in mid: mid[k]()
+                x = H if e0 == 0 and k >= 16 - KT else e0; m = e1 - x
+                if x > e0 and k == 16 - KT: c0 += H * KT
+                cm = T.CM[:, c0:c0 + m]; tok = "CM%d_%d" % (e0, k); c0 += m
+                js = [] if e0 else at[k]; n_mm[0] += 1 if m else 0; total = 16 + (KT if e0 == 0 and P1 > H else 0)
+                if k == 0: n_mm[0] = 1
+                if m:
+                    tt(cm, P[0][:, x:e1], T.S[:, 16 * x + k:16 * e1:16], A.is_gt, "#0 " + names("S%d", [y for y in cuts if x <= y < e1]), tok)
+                    mm(P[bank][:, x - e0:e1 - e0], W(k), cm, k == 0, n_mm[0] == total, "WD " + tok, "#%d" % bank)
+                for j in js:
+                    n_mm[0] += 1
+                    mm(P[bank][:, 0:H], W(16 - KT + j), T.CM[:, sg + H * j:sg + H * (j + 1)], False, n_mm[0] == total,
+                       "WD CS%d" % (j // 4), "#%d" % bank)
+            if 16 in mid: mid[16]()
+        n_mm = [0]
+        at = [[j for j in range(KT) if min(15, K0 + j) == k] for k in range(16)]
+        banks = (6, 7, 4); sg = P1 * (16 - KT)
+        def owns(src, tok):
+            for j in range(KT):
+                b = banks[j // 4]; c0 = H * (j % 4)
+                mm(P[b][:, c0:c0 + H], T.IF[:, 0:128], src[:, 0:H], j % 4 == 0, False, "IF " + tok, "#%d" % b)
+        def sums(e0, e1):
+            s = names("S%d", [x for x in cuts if e0 <= x < e1])
+            for j in range(KT):
+                b = banks[j // 4]; c0 = H * (j % 4); k = 16 - KT + j
+                mm(P[b][:, c0 + e0:c0 + e1], T.IF[:, 128:256], T.S[:, 16 * e0 + k:16 * e1:16], False,
+                   e1 == H and (j % 4 == 3 or j == KT - 1), "NI " + s, "#%d" % b)
         def signs(h):
-            act(T.CM[:, 8 * PT * h:8 * PT * (h + 1)], P[6 + h][:, 0:8 * PT], "#%d" % (6 + h), "CS%d" % h, f=AF.Sign, scale=2.0 ** 60, bias=-2.0 ** -100)
-        def sum_signs(k0, k1):
-            for k in range(k0, k1):
-                mm(P[4][:, 0:PT], W(k), T.CM[:, PT * k:PT * (k + 1)], k == 0, k == 15, "WD CS%d" % (k // 8), "#4")
-        def numbers():
-            cp(P[1][:, 0:256], T.O1[:], "O10 O11 O12 O13", "#1")
-            cp(P[1][:, 256:512], T.O2[:], "O20 O21 O22 O23", "#1")
+            m = H * min(4, KT - 4 * h)
+            act(T.CM[:, sg + 4 * H * h:sg + 4 * H * h + m], P[banks[h]][:, 0:m], "#%d" % banks[h], "CS%d" % h, f=AF.Sign, scale=2.0 ** 60, bias=-2.0 ** -100)
         def de(lst, e0, e1, tok, eng):
             x = Dr.indirect(lst[:, e0 // 16:e1 // 16])
             (cp if eng == "v" else act)(T.DE[:, e0:e1], x, DX + " " + tok, "DE%d" % e0)
         def de_psum(toks): act(P[0][:, 0:256], T.DE[:], toks, "#0")
 
-        first = chunks[:7]
+        first = [c for c in chunks if c[0] < P1]; second = chunks[len(first):]
+        def added(c):
+            add(*c)
+            if c[1] == 64: sums(0, 64)
+            if c[1] == H: sums(64, H)
         if t == 0:
-            g2(*first[0]); cp(P[0][:, 0:256], T.D[:, 0:256], DX, "#0"); differ(T.D[:, 0:PT], DX)
+            numbers(); g2(*first[0], "v"); owns(T.D, DX); cp(P[0][:, 0:H], T.D[:, 0:H], DX, "#0")
             for i, c in enumerate(first):
                 if i: g2(*c)
-                add(*c)
-                if i == 0: cp(T.O2[:, 64:256], T.B2[:, 64:256], "B2b", "O21 O22 O23")
-                if i == 1: cp(T.O1[:, 64:256], T.B1[:, 64:256], "B1b", "O11 O12 O13")
-                if i == 2: numbers(); differ(None, "")
+                added(c)
         if t == 1:
-            g2(*first[0]); de(T.VL, 0, 256, "VL0 VL1", "v"); differ(T.DE[:, 0:PT], "DE0")
+            g2(*first[0], "v"); de(T.VL, 0, H, "VL0", "v"); owns(T.DE, "DE0")
             for i, c in enumerate(first):
                 if i: g2(*c)
-                add(*c)
-                if i == 0: numbers()
-                if i == 2: differ(None, "")
-            de_psum("DE0")
+                added(c)
+                if i == 0: cp(P[0][:, 0:H], T.DE[:, 0:H], "DE0", "#0")
         if t == 2:
             st = piece_b(1, H); own = own_numbers(H)
             g2(*first[0]); st[0](); de(T.VL, 0, H, "VL0", "v"); st[1]()
-            differ(T.DE[:, 0:PT], "DE0")
-            add(*first[0]); g2(*first[1]); st[2](); add(*first[1]); g2(*first[2]); st[3]()
-            add(*first[2]); differ(None, ""); g2(*first[3]); st[4](); add(*first[3]); g2(*first[4]); st[5](); own[0]()
-            o2(H, 256); own[1](); o1(H, 256); own[2]()
-            add(*first[4]); g2(*first[5]); de(T.EL, H, 256, "EL", "a"); numbers(); add(*first[5]); g2(*first[6]); de_psum("DE0 DE128"); add(*first[6])
+            owns(T.DE, "DE0"); o1(0, H)
+            g2(*first[1]); add(*first[0]); st[2](); st[3](); add(*first[1]); g2(*first[2]); st[4](); g2(*first[3])
+            added(first[2]); st[5](); own[0](); o2(H, 256); own[1](); o1(H, 256); own[2]()
+            add(*first[3]); g2(*first[4])
+            added(first[4])
         if t == 3:
             own = own_numbers(0)
             own[0](); o2(0, 64); g2(*first[0]); own[1](); o1(0, 64); own[2](); o2(64, 256)
             for i, c in enumerate(first):
                 if i: g2(*c)
-                if i == 1: de(T.EL, 0, PT, "EL", "a"); differ(T.DE[:, 0:PT], "DE0")
-                add(*c)
+                if i == 1: de(T.EL, 0, H, "EL", DE3); owns(T.DE, "DE0")
+                added(c)
                 if i == 0: o1(64, 256)
-                if i == 1: numbers()
-                if i == 2: differ(None, "")
-            de(T.EL, PT, 256, "EL", "a"); de_psum("DE0 DE%d" % PT)
-        if late and t: late.pop(0)()
-        signs(0); signs(1); g2(*chunks[7]); g2(*chunks[8])
-        compare(PT, P1, 2)
-        act(T.VV[:, 0:PT], P[4][:, 0:PT], "#4 PC4", "VVs", f=AF.Sigmoid, bias=T.PC[:, 4:5], scale=8 * 17 * ALPHA)
+        def own_psum(h):
+            e0 = H * h
+            if t == 0: return act(P[0][:, e0:e0 + H], T.D[:, e0:e0 + H], DX, "#0")
+            if h: de(T.VL if t == 1 else T.EL, H, 256, "VL1" if t == 1 else "EL", "a")
+            act(P[0][:, e0:e0 + H], T.DE[:, e0:e0 + H], "DE%d" % e0, "#0")
         late_constants(t)
 
         def weigh(h, e0, e1, nb, sb, mid=lambda: None):
-            m = e1 - e0; x = 0 if h else PT
-            act(T.VV[:, e0 + x:e1], P[nb][:, x:m], "#%d PC2" % nb, "VV%d" % h, f=AF.Sigmoid, bias=T.PC[:, 2:3], scale=16 * 17 * ALPHA)
+            m = e1 - e0
+            if h: act(T.VV[:, e0:e1], P[nb][:, 0:m], "#%d PC2" % nb, "VV1", f=AF.Sigmoid, bias=T.PC[:, 2:3], scale=16 * 17 * ALPHA)
+            else:
+                act(T.VV[:, 0:H], P[nb][:, 0:H], "#%d PC4 PC5" % nb, "VVs", f=AF.Sigmoid, bias=T.PC[:, 4:5], scale=T.PC[:, 5:6])
+                if m > H: act(T.VV[:, H:m], P[nb][:, H:m], "#%d PC2" % nb, "VV0", f=AF.Sigmoid, bias=T.PC[:, 2:3], scale=16 * 17 * ALPHA)
             mid()
             mm(P[sb][:, 0:m], T.BT[:], T.VV[:, e0:e1], True, True, "BT VVs VV%d" % h, "#%d" % sb)
         def choose(h, e0, e1, sb):
             m = e1 - e0
-            ts(T.PF[:, e0:e1], P[sb][:, 0:m], 0.390625 * 0.92 * math.exp(U0 + 138 * ALPHA), A.is_gt, "#%d" % sb, "PF%d" % h)
-            tt(T.WIN[:, e0:e1], T.VV[:, e0:e1], P[sb][:, 0:m], A.is_gt, "VVs VV%d #%d" % (h, sb), "WIN%d" % h)
+            need = 0.390625 * 0.92 * math.exp(U0 + 138 * ALPHA)
+            if h or PFV: ts2(T.PF[:, e0:e1], P[sb][:, 0:m], need, A.is_gt, 2.0, A.mult, "#%d" % sb, "PF%d" % h)
+            else:
+                mm(P[4][:, 0:m], T.BT[:], T.VV[:, e0:e1], True, True, "BT VVs VV0", "#4")
+                act(T.PF[:, e0:e1], P[4][:, 0:m], "#4", "PF0", f=AF.Sign, bias=-need)
+        def winner(h, e0, e1, sb):
+            tt(T.WIN[:, e0:e1], T.VV[:, e0:e1], P[sb][:, 0:e1 - e0], A.is_gt, "VVs VV%d #%d" % (h, sb), "WIN%d" % h)
         def ranks(h, e0, e1):
-            scan(T.PR[:, e0:e1], T.ONE[:, 0:e1 - e0], T.PF[:, e0:e1], T.PR[:, e0 - 1:e0] if h else 0.0, A.mult, A.add,
+            scan(T.PR[:, e0:e1], T.ONE[:, 0:e1 - e0], T.PF[:, e0:e1], T.PR[:, e0 - 1:e0] if h else 0.0, A.mult if h or PFV else A.add, A.add,
                  "ONE PF%d" % h + (" PR0" if h else ""), "PR%d" % h)
         def pick(f, h, e0, e1, bank):
             Wf = T.WB if f == 1 else T.WC; c0 = 256 * (f - 1)
             tt(Wf[:, e0:e1], T.WIN[:, e0:e1], P[1][:, c0 + e0:c0 + e1], A.mult, "WIN%d #1" % h, "W%d%d" % (f, h))
-            mm(P[bank][:, c0:c0 + e1 - e0], T.BH[:], Wf[:, e0:e1], True, True, "BH W%d%d" % (f, h), "#%d" % bank)
+            mm(P[bank][:, c0 + e0:c0 + e1], T.BH[:], Wf[:, e0:e1], True, True, "BH W%d%d" % (f, h), "#%d" % bank)
         def count(e0, e1, col, to, rd):
-            act(T.TRASH[:, 256 * to:256 * to + e1 - e0], T.PR[:, e0:e1], rd + " FB", "ACC%d" % to, f=AF.Sigmoid, bias=T.FB[:, col:col + 1], scale=-40.0,
-                accum_out=T.ACC[:, to:to + 1])
+            act(T.TRASH[:, 256 * to:256 * to + e1 - e0], T.PR[:, e0:e1], rd + " FB", "ACC%d" % to, f=AF.Sigmoid, bias=T.FB[:, col:col + 1], scale=-20.0,
+                accum_out=acc(to, to + 1))
 
+        for i, c in enumerate(second):
+            if i == 0 and t >= 2: own_psum(0)
+            g2(*c)
+            if i == SA:
+                for h in range((KT + 3) // 4): signs(h)
+            if i == SB: compare(0, P1, 2)
+            add(*c)
+        own_psum(1)
         weigh(0, 0, P1, 2, 3)
-        if t: act(new(0, 0, 256), T.ET[:].indirect(T.VL[:]), "ET VL0 VL1", "TRn00 TRn01")
-        else: act(new(0, 0, 256), T.R[:, 0:256], "R0", "TRn00 TRn01")
-        add(*chunks[7]); add(*chunks[8])
+        def first_ranks():
+            ranks(0, 0, P1)
+            for c in range(4): count(0, P1, 4 * par + c, 8 + c, "PR0")
+        if spare: spare.pop(0)(); spare.pop(0)()
         choose(0, 0, P1, 3)
-        ranks(0, 0, P1)
-        for c in range(4): count(0, P1, 4 * par + c, 8 + c, "PR0")
-        compare(P1, 256, 6)
-        weigh(1, P1, 256, 6, 7, lambda: pick(1, 0, 0, P1, 4))
-        pick(2, 0, 0, P1, 2)
+        if t: act(new(0, 0, 256), T.ET[:].indirect(T.VL[:]), "ET VL0 VL1", "TRn00 TRn01")
+        compare(P1, 256, 6, {KB: first_ranks})
+        if spare: spare.pop(0)()
+        weigh(1, P1, 256, 6, 7)
+        if t >= 2: numbers(0, P1)
+        winner(0, 0, P1, 3)
+        one()
+        pick(1, 0, 0, P1, 4); pick(2, 0, 0, P1, 2)
         act(new(1, 0, P1), P[4][:, 0:P1], "#4", "TRn10")
         act(new(2, 0, P1), P[2][:, 256:256 + P1], "#2", "TRn20")
-        one(); one()
-        choose(1, P1, 256, 7)
-        tt(T.OV[:], T.OO[:, 4 * par:4 * par + 4], T.ACC[:, 8:12], A.add, "OO ACC8 ACC9 ACC10 ACC11", "OV")
+        one()
+        if t >= 2: numbers(P1, 256)
+        choose(1, P1, 256, 7); winner(1, P1, 256, 7)
+        tt(T.OV[:], T.OO[:, 4 * par:4 * par + 4], acc(8, 12), A.add, "OO ACC8 ACC9 ACC10 ACC11", "OV")
         ranks(1, P1, 256)
-        pick(1, 1, P1, 256, 3); pick(2, 1, P1, 256, 3)
+        for c in range(4 - CV): count(P1, 256, 4 * par + c, 4 * par + c, "PR1")
+        pick(1, 1, P1, 256, 4)
+        for c in range(4 - CV, 4):
+            ts(T.E3[:, NL * c:NL * c + NL], T.PR[:, P1:256], T.FQ[:, 4 * par + c:4 * par + c + 1], A.is_lt, "PR1 FQ", "E3%d" % (c % 3))
+        pick(2, 1, P1, 256, 2)
+        for c in range(4 - CV, 4):
+            j = 4 * par + c
+            scan(T.ACC[:, 64 * j:64 * j + 64], T.E3[:, NL * c:NL * c + 64], T.E3[:, NL * c + 64:NL * c + NL], 0.0, A.add, A.add,
+                 "E3%d" % (c % 3), "ACC%d" % j)
         one()
-        for c in range(4): count(P1, 256, 4 * par + c, 4 * par + c, "PR1")
-        for i, (c, (p0, p1, st)) in enumerate(((0, (0, 1, 1)), (0, (5, 12, 3)), (1, (1, 8, 3)), (2, (2, 11, 4)), (3, (3, 10, 6)))):
+        for i, (c, (p0, p1, st)) in enumerate(((0, (0, 1, 1)), (0, (5, 12, 3)), (2, (2, 11, 4)), (3, (3, 10, 6)), (1, (1, 8, 3)))):
             m = len(range(p0, p1, st)); col = 4 * par + c
-            ts2(T.SL[:, p0:p1:st], T.QT[:, 0:m], T.ACC[:, col:col + 1], A.add, T.OV[:, c:c + 1], A.add, "QT OV ACC%d" % col, "SL%d" % p0)
-        act(new(1, P1, 256), P[3][:, 0:NL], "#3", "TRn11")
-        act(new(2, P1, 256), P[3][:, 256:256 + NL], "#3", "TRn21")
-        sl = " SL0 SL5 SL1 SL2 SL3"
-        win = lambda f: TR[:, f * TW_:f * TW_ + 385]
+            ts2(T.SL[:, p0:p1:st], T.QT[:, 0:m], acc(col, col + 1), A.add, T.OV[:, c:c + 1], A.add, "QT OV ACC%d" % col, "SL%d" % p0)
+        act(new(1, P1, 256), P[4][:, P1:256], "#4", "TRn11")
+        act(new(2, P1, 256), P[2][:, 256 + P1:512], "#2", "TRn21")
         one()
+        if last:
+            for c0, c1, bank in ((0, 8, 3), (8, 40, 2)):
+                for r in range(16):
+                    mm(P[bank][:, r:16 * (c1 - c0):16], T.SEL[:, r:r + 128], T.KP[:, c0:c1], r == 0, r == 15, "SEL KPa", "#%d" % bank)
+        sl = " SL0 SL5 SL1 SL2 SL3"
+        win = lambda f, TR=TR: TR[:, f * TW_:f * TW_ + 385]
         for f in range(3):
             act(T.ZC[:, 64 * f:64 * f + 64], win(f).indirect(T.SL[:, 0:4]), tri(f) + sl, "ZC%d" % f, scale=1.0 / 8192)
             tt(T.Z[:, f, :], win(f).indirect(T.SL[:, 4:12]), T.ZM[:], A.max, tri(f) + sl + zm, "Z%d" % f)
         nz = 128 * t
         if t >= 2: act(P[7][:, 128:192], T.NZ[:, nz + 64:nz + 128], "NZo%d" % t, "#7")
+        if t == 0: ring_constants()
+        while spare: spare.pop(0)()
         tt(T.XM[:], T.ZC[:], P[0][:, 256:448], A.mult, "ZC0 ZC1 ZC2 #0", "XM")
         one()
-        scan(T.XW[:], T.RS[:], T.XM[:], 0.0, A.mult, A.add, "RS XM", "XW")
+        scan(T.XW[:], T.RS[:], T.XM[:], 0.0, A.mult, A.add, "RS0 RS128 XM", "XW")
         one()
         cp(T.XL[:], T.XW[:, 15::16], "XW", "XL")
         act(T.DV[:], Dr.indirect(T.XL[:]), DX + " XL", "DV")
-        act(P[7][:, 0:128], T.DV[:, 64:192], "DV", "#7")
+        act(P[7][:, 64:128], T.DV[:, 128:192], "DV", "#7")
         for s, (c0, tok, land) in enumerate(sides):
             if not lower[s]: act(T.D[:, c0:c0 + H], T.R[:, 0:H], "R0", tok, scale=0.0)
         if all(lower): DZ, dz = T.DV, "DV"
@@ -491,7 +559,7 @@ def rank_program(g, core, T, topo):
         def bad(c): ts(T.TB[:, c::4], T.J12[:, c::4], T.ES[:, 288 * c + 287:288 * c + 288], A.min, "J12 ES%d" % c, "TB%d" % c)
         DL = T.CO[:, 64:128]
         equal(3); equal(2); fold(3); equal(1); fold(2)
-        tt(T.T1[:], T.DV[:, 0:64], P[7][:, 0:64], A.subtract, "DV #7", "T1")
+        tt(T.T1[:], T.DV[:, 0:64], T.DV[:, 64:128], A.subtract, "DV", "T1")
         equal(0)
         tt(T.T2[:], T.T1[:], P[7][:, 64:128], A.subtract, "T1 #7", "T2")
         fold(1); fold(0)
@@ -503,133 +571,148 @@ def rank_program(g, core, T, topo):
         act(T.CO[:, 0:64], DL, "DL", "CO0", scale=-1.0); act(T.CO[:, 128:192], DL, "DL", "CO2")
         bad(1); bad(0)
         tb = "TB0 TB1 TB2 TB3"; TB = T.TB[:, 0:4]
+        if t < 2: act(T.NZ[:, nz:nz + 64], DL, "DL", "NZc", scale=-1.0)
+        else: tt(T.NZ[:, nz:nz + 64], P[7][:, 128:192], DL, A.subtract, "#7 DL", "NZc")
         one()
         tt(T.OF[:], T.TB[:], T.XW[:, 15::16], A.max, tb + " XW", "OF")
         ts2(T.I1[:], TB, 0.5, A.is_gt, 64.0, A.mult, tb, "I1")
         cp(T.OL[:], T.OF[:], "OF", "OL")
-        tt(T.NZ[:, nz:nz + 64], T.NZ[:, nz + 64:nz + 128], DL, A.subtract, "NZo%d DL" % t, "NZc")
+        if t < 2: ts(T.NZF[:], DL, 0.0, A.not_equal, "DL", "NZF")
+        else: ts(T.NZF[:], T.NZ[:, nz:nz + 64], 0.0, A.not_equal, "NZc", "NZF")
+        mm(P[6][:, 0:64], T.BO[:], T.NZF[:], True, True, "BO NZF", "#6")
         tt(T.D[:].indirect(T.OL[:]), DZ[:], T.CO[:], A.add, dz + " DL CO0 CO2 OL", DX)
         act(TW[:].indirect(T.OL[:]), T.ZC[:], "ZC0 ZC1 ZC2 OL", "TW%d" % t, f=AF.Sigmoid)
         trs = []
-        for to, c0, land, sem, en in ((rl, 0, "LR", "ar", eng_chip[1::2]), (rrt, V - H, "LL", "al", eng_chip[0::2])):
+        mine = first_hop(eng_chip, t)
+        for to, c0, land, sem, en in ((rl, 0, "LR", "ar", mine[0]), (rrt, V - H, "LL", "al", mine[1])):
             rid, pid = topo.addr(to, core)
             trs.append(RemoteDMATransfer(dst_ids=[DstId(rid=rid, pnc=pid)], dma_engine_mask=mask_of(en), remote_sem=T.sem[sem + str(t)],
                                          src=T.D[:, c0:c0 + H], dst=T[land][:, t * H:(t + 1) * H]))
         op("g", lambda trs=trs, t=t: g.remote_dma_fused(trs, local_sem=T.sem["ld%d" % t]), "~Dl ~Dr", "")
-        def send_touches(src, tok, t=t):
+        def send_touches(src, tok, t=t, mine=mine):
             rid, pid = topo.addr(rt, core)
-            op("g", lambda: g.remote_dma(touch_piece(T, t), src, T.sem["at%d" % t], T.sem.ls, pid, rid, mask_of(eng_chip[1::2])), tok, "")
-        arrival("at%d" % t, "LT%d" % t); arrival("al%d" % t, "LL%d" % t); arrival("ar%d" % t, "LR%d" % t); arrival("ld%d" % t, "sent%d" % t, 2 * half)
+            op("g", lambda: g.remote_dma(touch_piece(T, t), src, T.sem["at%d" % t], T.sem.ls, pid, rid, mask_of(mine[2])), tok, "")
+        arrival("at%d" % t, "LT%d" % t); arrival("al%d" % t, "LL%d" % t); arrival("ar%d" % t, "LR%d" % t); arrival("ld%d" % t, "sent%d" % t, len(mine[0]) + len(mine[1]))
         tw = "TW%d" % t
         while late: one()
         for s, (c0, tok, land) in enumerate(sides): act(P[0][:, s * H:(s + 1) * H], T.D[:, c0:c0 + H], tok, "#0")
-        if t == 0: act(T.LG[:], T.LG[:], "LG", "LG", scale=1.0 / 8192)
+        if t == 0: list_constants()
         for c in range(4): count(0, 256, 4 * (1 - par) + c, 4 * (1 - par) + c, "PR0 PR1")
 
         q = 4 * (1 - par)
-        def nzf():
-            ts(T.NZF[:], T.NZ[:, nz:nz + 64], 0.0, A.not_equal, "NZc", "NZF")
-            for r in range(16): mm(P[6][:, 0:4], W(r), T.NZF[:, r::16], r == 0, r == 15, "WD NZF", "#6")
-        def il():
-            cp(T.IL[:], T.I2[:], "I2", "IL")
+        def keep(t=t, nz=nz):
             act(T.NZ[:, nz + 320:nz + 384], T.NZ[:, nz:nz + 128].indirect(T.IL[:]), "IL NZc NZo%d" % t, "NZo%d" % (t + 2))
-        def back():
-            ts(T.WL[:], T.SR[:], 0.25, A.add, "SRa SRb", "WL")
-            for f in range(3):
+        def back(fields=range(3), TRn=TRn, win=win, tri=tri, par=par):
+            for f in fields:
                 act(TRn[:, f * TW_:f * TW_ + 128], win(f).indirect(T.WL[:]), tri(f) + " WL", "TRo%d%d" % (1 - par, f))
         def free():
-            ts(T.FW[:], T.SR[:], 383.5, A.is_gt, "SRa SRb", "FW")
+            scan(T.FW[:, 9:13], T.FW[:, 0:4], T.FW[:, 4:8], 0.0, A.add, A.add, "FW", "FS")
             for p in range(2):
                 o = P[4][:, 4 * p:4 * p + 4]
-                mm(o, T.TI[:], T.FW[:, 0:4], True, False, "TI FW", "#4")
-                mm(o, T.TI[:] if p else T.TX[:], T.FW[:, 4:8], False, False, "TI TX FW", "#4")
-                for d in range(1, 4):
-                    for x in range(2):
-                        mm(P[4][:, 4 * p + d:4 * p + 4], T.BO[:], T.FW[:, 4 * x:4 * x + 4 - d], False, False, "BO FW", "#4")
+                mm(o, T.TI[:], T.FW[:, 9:13], True, False, "TI FS", "#4")
+                mm(o, T.TG[:], T.FW[:, 8:12], False, False, "TG FS FS0", "#4")
+                if p == 0: mm(o, T.TX[:], T.FW[:, 4:8], False, False, "TX FW", "#4")
                 mm(o, T.IK[:], T.FW[:, 4 * p:4 * p + 4], False, True, "IK FW", "#4")
-        book = [nzf,
+        book = [lambda: tt(T.XM[:, 0:64], P[6][:, 0:64], T.IM[:, 0:64], A.mult, "#6 IM0", "XM"),
                 lambda: tt(T.I2[:], T.I1[:], T.CR[:, 0:4], A.add, "I1 CR", "I2"),
-                lambda: tt(T.G1[:], T.ACC[:, 4 * par:4 * par + 4], T.OV[:], A.add, "OV " + names("ACC%d", range(4 * par, 4 * par + 4)), "G1"),
-                il,
-                lambda: tt(T.SR[:, q:q + 4], T.ACC[:, q:q + 4], T.OO[:, q:q + 4], A.add, "OO " + names("ACC%d", range(q, q + 4)), "SRa"),
-                lambda: tt(T.OF[:, 0:4], P[6][:, 0:4], TB, A.add, "#6 " + tb, "OF"),
+                lambda: None,
+                lambda: scan(T.T1[:], T.RS[:, 0:64], T.XM[:, 0:64], 0.0, A.mult, A.add, "RS0 XM", "T1"),
+                lambda: cp(T.IL[:], T.I2[:], "I2", "IL"),
+                lambda: tt(T.OF[:, 0:4], T.T1[:, 15::16], TB, A.add, "T1 " + tb, "OF"),
+                lambda: tt(T.G1[:], acc(4 * par, 4 * par + 4), T.OV[:], A.add, "OV " + names("ACC%d", range(4 * par, 4 * par + 4)), "G1"),
                 lambda: ts2(T.G3[:], T.OF[:, 0:4], 0.0, A.is_equal, 384.0, A.mult, "OF", "G3"),
+                lambda: tt(T.SR[:, q:q + 4], acc(q, q + 4), T.OO[:, q:q + 4], A.add, "OO " + names("ACC%d", range(q, q + 4)), "SRa"),
                 lambda: tt(T.SR[:, 4 * par:4 * par + 4], T.G1[:], T.G3[:], A.max, "G1 G3", "SRb"),
-                back]
+                lambda: ts(T.WL[:], T.SR[:], 0.25, A.add, "SRa SRb", "WL"),
+                lambda: ts(T.FW[:, 0:8], T.SR[:], 383.5, A.is_gt, "SRa SRb", "FW"),
+                free,
+                lambda: tt(T.OO[:], T.FW[:, 0:8], T.K1[:, 0:8], A.mult, "FW K1", "OO"),
+                lambda: tt(T.OO[:], T.OO[:], T.K1[:, 8:16], A.add, "OO K2", "OO")]
+        def bounds():
+            ts2(T.FQ[:], P[4][:, 0:8], 2.0, A.mult, 767.0, A.add, "#4", "FQ")
         def nxt(k=1):
             for _ in range(k): book.pop(0)()
 
         if not last:
-            s0 = 8 * (t + 1); top = 16 if t == 0 else 40; end = 32 if t == 0 else 40
+            s0 = 8 * (t + 1); top = (16, 32, 40)[t]; end = (16, 40, 40)[t]; e1 = (256, H, 0)[t]
             thr, ttok = (T.TH0, "TH0") if t == 0 else (T.THR, "THR")
-            L = T["L%d" % (t + 1)]; e1 = (256, H, 0)[t]
-            nxt()
-            scan(T.XS[:], T.MB[:, 0:H], TW[:, V - H:V], 4096.0, A.max, A.min, "MB " + tw, "XS")
-            own_touches = lambda: scan(T.X[:, 0:16 * top], T.MB[:, 0:16 * top], TW[:, 0:16 * top], 4096.0, A.max, A.min, "MB " + tw, "X")
-            if e1: own_touches()
-            nxt()
-            tt(T.TS[:, 8 * t:8 * t + 8], T.XS[:, 15::16], T.THS[:], A.is_le, "XS THS", "TS%d" % t)
-            send_touches(T.TS[:, 8 * t:8 * t + 8], "TS%d" % t)
-            if not e1: own_touches()
-            tt(T.F[:, 8:top], T.X[:, H + 15:16 * top:16], thr[:, 8:top], A.is_le, "X " + ttok, "Fa")
-            tt(T.FN[:, 8:top], T.X[:, H + 15:16 * top:16], thr[:, 8:top], A.is_gt, "X " + ttok, "FNa")
-            tt(T.FO[:], T.X[:, 15:H:16], thr[:, 0:8], A.is_le, "X " + ttok, "FO")
+            L = T["L%d" % (t + 1)]; ltok = "L%d" % (t + 1); lg = "LGa" if t == 0 else "LG"
+            def touched(x, c0, c1):
+                scan(T.X[:, 16 * c0:16 * c1], T.MB[:, 0:16 * (c1 - c0)], TW[:, 16 * c0:16 * c1], 4096.0, A.max, A.min,
+                     ("MB0 MB128 MB256 " if t else "MB0 ") + tw, "X" + x)
+            def flags(x, y, c0, c1):
+                tt(T.F[:, c0:c1], T.X[:, 16 * c0 + 15:16 * c1:16], thr[:, c0:c1], A.is_le, "X%s %s" % (x, ttok), "F" + y)
+                tt(T.FN[:, c0:c1], T.X[:, 16 * c0 + 15:16 * c1:16], thr[:, c0:c1], A.is_gt, "X%s %s" % (x, ttok), "FN" + y)
+            def far_touches(): scan(T.XS[:], T.MB[:, 0:H], TW[:, V - H:V], 4096.0, A.max, A.min, "MB0 " + tw, "XS")
+            def send():
+                tt(T.TS[:, 8 * t:8 * t + 8], T.XS[:, 15::16], T.THS[:], A.is_le, "XS THS", "TS%d" % t)
+                send_touches(T.TS[:, 8 * t:8 * t + 8], "TS%d" % t)
+            if e1: nxt(); touched("a", s0, top); far_touches(); flags("a", "a", s0, top); send(); nxt()
+            else: far_touches(); nxt(); send(); touched("a", s0, top); nxt(); flags("a", "a", s0, top)
             ranks_of("a", s0, end, "Fa")
-            tt(T.NF[:, 8:top], T.FN[:, 8:top], T.JK[:, 8:top], A.mult, "FNa JK", "NFa")
+            tt(T.NF[:, s0:top], T.FN[:, s0:top], T.JK[:, s0:top], A.mult, "FNa JK", "NFa")
             places("a", s0, end, "NFa")
-            if t:
-                ranks_of("b", 8, s0, "Fa")
-                mm(na, T.BO[:], T.SSa[:, 40 - s0:41 - s0], True, True, "BO SSa", "#5")
-                places("b", 8, s0, "NFa")
-                ts2(T.GB[:], T.FO[:], -1.0, A.mult, 0.5, A.add, "FO", "GB")
-            nxt(2)
+            mm(na, T.BO[:], T.SSa[:, end - s0:end - s0 + 1], True, True, "BO SSa", "#5")
+            nxt(2); touched("b", 0, s0); nxt(2)
             ts(T.PL[:, s0:end], P[5][:, s0:end], -1.0, A.add, "#5", "PLa")
-            act(L[:].indirect(T.PL[:, s0:end]), T.LG[:, 16 * s0:16 * end], "PLa LG", "L%d" % (t + 1), f=AF.Sigmoid)
-            if t:
-                cp(T.PL[:, 8:s0], P[5][:, 8:s0], "#5", "PLc")
-                act(T["M%d" % (t + 1)][:].indirect(T.PL[:, 8:s0]), T.LG[:, U + H:U + 16 * s0], "PLc LG", "M%d" % (t + 1), f=AF.Sigmoid)
-            ts(T.KP[:, s0:end], P[5][:, s0:end], 256.5, A.is_gt, "#5", "KPa")
-            nxt(5); free()
-            oo = [lambda: tt(T.OO[:], T.FW[:], T.K1[:, 0:8], A.mult, "FW K1", "OO"), lambda: tt(T.OO[:], T.OO[:], T.K1[:, 8:16], A.add, "OO K2", "OO")]
+            act(L[:].indirect(T.PL[:, s0:top]), T.LG[:, 16 * s0:16 * top], "PLa " + lg, ltok, f=AF.Sigmoid)
             if e1:
-                scan(T.LW[:, 0:e1], T.MB[:, 0:e1], L[:, 0:e1], 4096.0, A.max, A.min, "MB L%d" % (t + 1), "LW")
-                oo[0](); decode(0, e1); oo[1](); o2(0, e1); o1(0, e1)
+                c = e1 // 16; tab = T.CT[:, 0:257] if t == 0 else T.CT[:, 264:393]
+                ts2(T.OFF[:, 0:c], T.C1[:, 0:c], na, A.subtract, 16.0 * (end - top), A.add, "C1 #5", "OFF")
+            ts(T.KP[:, s0:end], P[5][:, s0:end], 256.5, A.is_gt, "#5", "KPa")
+            if t == 0: ts2(T.KP[:, 16:32], T.CR[:, 16:32], na, A.add, 511.5, A.is_gt, "CR #5", "KPc")
+            else: flags("b", "c", 8, s0)
+            nxt(2)
+            tt(T.FO[:], T.X[:, 15:H:16], thr[:, 0:8], A.is_le, "Xb " + ttok, "FO")
+            if t:
+                ranks_of("b", 8, s0, "Fc")
+                tt(T.NF[:, 8:s0], T.FN[:, 8:s0], T.JK[:, 8:s0], A.mult, "FNc JK", "NFc")
+                places("b", 8, s0, "NFc")
+            nxt(2)
+            if e1: tt(T.LS[:, 0:e1], tab.indirect(T.OFF[:, 0:c]), T.IM[:, 0:e1], A.mult, "CT OFF IM0 IM", "LS")
+            if t: ts2(T.GB[:], T.FO[:], -1.0, A.mult, 0.5, A.add, "FO", "GB")
+            nxt(2)
+            if t: cp(T.PL[:, 8:s0], P[5][:, 8:s0], "#5", "PLc")
+            def rest():
+                if t: act(T["M%d" % (t + 1)][:].indirect(T.PL[:, 8:s0]), T.LG[:, U + H:U + 16 * s0], "PLc LG", "M%d" % (t + 1), f=AF.Sigmoid)
+                if top < end: act(L[:].indirect(T.PL[:, top:end]), T.LG[:, 16 * top:16 * end], "PLa LG", ltok, f=AF.Sigmoid)
+            if e1:
+                scan(T.LW[:, 0:e1], T.LS[:, 0:e1], L[:, 0:e1], 0.0, A.max, A.min, "LS " + ltok, "LW")
+                rest(); nxt(2); decode(0, e1); nxt(); o2(0, e1)
+                bounds()
+                if t == 0: o1(0, e1); numbers(0, e1)
+                act(T.FB[:], T.FQ[:], "FQ", "FB", scale=20.0)
+                spare.extend([lambda f=f, back=back: back([f]) for f in range(3)] + [keep])
+                if t == 0:
+                    while spare: spare.pop(0)()
+                    act(T.LG[:, 256:1024], T.LG[:, 256:1024], "LG", "LG", scale=1.0 / 8192)
                 fix(t, 0); fix(t, 1)
             else:
-                oo[0](); oo[1]()
+                rest(); nxt(3); keep(); bounds()
                 st = piece_b(t, 0)
-                st[0](); st[1](); fix(t, 0); st[2](); st[3](); fix(t, 1); st[4](); st[5]()
-            late.append(lambda: act(T.FB[:], P[4][:, 0:8], "#4", "FB", scale=40.0, bias=40 * 383.5))
+                st[0](); st[1](); fix(t, 0); st[2](); back(); act(T.FB[:], T.FQ[:], "FQ", "FB", scale=20.0)
+                st[3](); fix(t, 1); st[4](); st[5]()
             late.extend(unflag(t))
         else:
-            send_touches(TW[:, V - H:V], tw)
-            arrival("ls", "gone", half * RO)
-            dma("s", T.yd[:, H:V - H], T.D[:, H:V - H], "Dm sent%d gone" % t, "y0")
-            iota(TR[:, 384::TW_], [[0, 3]], -1, 0, "TRx%d" % par)
             nxt()
-            ts(T.TH[:], TW[:, 0:U], 0.75, A.is_lt, tw, "TH")
-            nxt(8)
-            for c0, c1, bank in ((0, 8, 3), (8, 40, 2)):
-                m = 16 * (c1 - c0)
-                mm(P[bank][0:8, 0:m], T.SEL[:, 0:8], T.TH[:, 16 * c0:16 * c1], True, False, "SEL TH", "#%d" % bank)
-                for r in range(16):
-                    mm(P[bank][0:8, r:m:16], T.SEL[:, 8 * r:8 * r + 8], T.FK[:, c0:c1], False, r == 15, "SEL FK", "#%d" % bank)
-            ts(T.XS[0:8, :], P[3][0:8, 0:H], 0.75, A.add, "#3", "XS")
-            ts(T.YF[0:8, H:U], P[2][0:8, :], 0.5, A.is_gt, "#2", "YFa")
+            ts(T.WIN[:, 0:H], TW[:, V - H:V], 0.75, A.is_lt, tw, "WIN0")
+            send_touches(T.WIN[:, 0:H], "WIN0")
+            dma("s", T.yd[:, H:V - H], T.D[:, H:V - H], "Dm sent%d" % t, "y0")
+            iota(TR[:, 384::TW_], [[0, 3]], -1, 0, "TRx%d" % par)
+            nxt(10); keep()
+            tt(P[7][:, 0:H], TW[:, 0:H], P[3][:, 0:H], A.is_lt, tw + " #3", "#7")
+            tt(T.YF[:, H:U], TW[:, H:U], P[2][:], A.is_lt, tw + " #2", "YFa")
+            for f in range(3):
+                for p in range(2):
+                    act(T.X[:, 128 * f + p:128 * (f + 1):2], win(f).indirect(T.WL[:, 4 * p:4 * p + 4]), tri(f) + " WL", "YT%d%d" % (f, p))
+            dma("s", T.yt[:], T.X[0::16, 0:384], "YT00 YT01 YT10 YT11 YT20 YT21", "y2")
             for p in range(2):
                 act(T.M16[:, p::2], T.NZ[:, 128 * (4 + p) + 64:128 * (5 + p)], "NZo%d" % (4 + p), "YZ%d" % p, scale=-1.0)
             dma("s", T.yz[:], T.M16[:], "YZ0 YZ1", "y1")
-            for f in range(3):
-                for p in range(2):
-                    mm(P[4][0:8, 128 * f + p:128 * (f + 1):2], T.SE0[:], TRn[:, f * TW_ + 64 * p:f * TW_ + 64 * p + 64], True, True,
-                       "SE0 TRo%d%d" % (1 - par, f), "#4")
-            act(T.X[0:8, 0:384], P[4][0:8, 0:384], "#4", "X")
-            dma("a", T.yt[:], T.X[0:8, 0:384], "X", "y2")
             fix(t, 0); dma("s", T.yd[:, 0:H], T.D[:, 0:H], "Dl", "y3")
             fix(t, 1); dma("a", T.yd[:, V - H:V], T.D[:, V - H:V], "Dr", "y4")
-            mm(P[7][0:8, 0:H], T.SE0[:], T.LU[:], True, True, "SE0 LT%d" % t, "#7")
-            tt(T.YF[0:8, 0:H], P[7][0:8, 0:H], T.XS[0:8, :], A.is_lt, "#7 XS", "YFb")
-            dma("s", T.yf[:], T.YF[0:8, :], "YFa YFb", "y5")
+            tt(T.YF[:, 0:H], T.LU[:], P[7][:, 0:H], A.max, "#7 LT%d" % t, "YFb")
+            dma("s", T.yf[:], T.YF[0::16, :], "YFa YFb", "y5")
             op("s", None, "y0 y1 y2 y3 y4 y5", "")
     emit(g, T, ops)
     g.wait_ge(T.sem.ls, half * RO)

import math
from concourse.bass import DstId, RemoteDMATransfer
from concourse.mybir import AluOpType as A, AxisListType as AX, ActivationFunctionType as AF

V, U, H, RO = 1280, 640, 128, 4
NONE = 1280
JUNK = 1288
DW = 1800
TW_ = 392
P1 = 128
KT = 6
K0, PFV, CV, SA, SB, DE3 = 6, 0, 2, 2, 2, "v"
KB, E0 = 4, 0
CUTS = [[0, 16, 40, 64, 96, 128, 160, 192, 224, 256]] * 4
ALPHA = math.log(1.7)
U0 = -6.0 - 272 * ALPHA
SLOPE = 32776.0


def code(x):
    return 1 / (1 + math.exp(-(x - 512) / 8192))


F32, BF, F16, I32, U16 = "float32", "bfloat16", "float16", "int32", "uint16"

SCRATCH = {
    "D": ("sbuf", [128, DW], F32), "B1": ("sbuf", [128, 1032], I32), "B2": ("sbuf", [128, 1032], I32),
    "O1": ("sbuf", [128, 256], U16), "O2": ("sbuf", [128, 256], U16),
    "G2": ("sbuf", [128, 4096], F32), "S": ("sbuf", [128, 4096], F32),
    "CM": ("sbuf", [128, 4096], BF), "DE": ("sbuf", [128, 256], F32),
    "VV": ("sbuf", [128, 256], BF), "WIN": ("sbuf", [128, 256], BF), "PR": ("sbuf", [128, 256], BF), "PF": ("sbuf", [128, 256], BF),
    "WB": ("sbuf", [128, 256], F16), "WC": ("sbuf", [128, 256], F16), "TRASH": ("sbuf", [128, 12 * 256], BF),
    "TR0": ("sbuf", [128, 3 * TW_], F32), "TR1": ("sbuf", [128, 3 * TW_], F32),
    "ACC": ("sbuf", [128, 12 * 64], F32), "OO": ("sbuf", [128, 8], F32), "LG": ("sbuf", [128, 1024], F32), "OV": ("sbuf", [128, 4], F32),
    "FB": ("sbuf", [128, 8], F32), "FQ": ("sbuf", [128, 8], F32), "FW": ("sbuf", [128, 16], BF), "SL": ("sbuf", [128, 12], U16),
    "XM": ("sbuf", [128, 192], F16), "XW": ("sbuf", [128, 192], F32), "XL": ("sbuf", [128, 12], U16), "ZC": ("sbuf", [128, 192], F32),
    "Z": ("sbuf", [128, 3, 128], F16), "E0": ("sbuf", [128, 144], BF), "E1": ("sbuf", [128, 288], BF),
    "E2": ("sbuf", [128, 432], BF), "E3": ("sbuf", [128, 576], BF), "ES": ("sbuf", [128, 4 * 288], BF), "OL": ("sbuf", [128, 12], U16),
    "DV": ("sbuf", [128, 192], F32), "DZ": ("sbuf", [128, 192], F32), "T1": ("sbuf", [128, 64], F32), "T2": ("sbuf", [128, 64], F32),
    "CO": ("sbuf", [128, 192], F32), "TB": ("sbuf", [128, 12], F32), "OF": ("sbuf", [128, 12], F32),
    "NZ": ("sbuf", [128, 768], F32), "NZF": ("sbuf", [128, 64], BF), "I1": ("sbuf", [128, 4], F32), "I2": ("sbuf", [128, 4], F32),
    "IL": ("sbuf", [128, 4], U16), "G1": ("sbuf", [128, 4], F32), "G3": ("sbuf", [128, 4], F32),
    "SR": ("sbuf", [128, 8], F32), "WL": ("sbuf", [128, 8], U16),
    "X": ("sbuf", [128, U], F32), "XS": ("sbuf", [128, H], F32), "THR": ("sbuf", [128, 40], F32), "GB": ("sbuf", [128, 8], F32),
    "F": ("sbuf", [128, 40], BF), "FO": ("sbuf", [128, 8], BF), "FN": ("sbuf", [128, 40], BF), "FK": ("sbuf", [128, 40], BF),
    "SSa": ("sbuf", [128, 32], BF), "SSb": ("sbuf", [128, 32], BF), "SSc": ("sbuf", [128, 16], BF),
    "NF": ("sbuf", [128, 40], F16), "KP": ("sbuf", [128, 40], BF), "PL": ("sbuf", [128, 40], U16), "OFF": ("sbuf", [128, 16], U16),
    "LS": ("sbuf", [128, 256], F32), "LW": ("sbuf", [128, 256], F32),
    "VL": ("sbuf", [128, 16], U16), "EA": ("sbuf", [128, 16], F32), "EB": ("sbuf", [128, 16], F32), "EL": ("sbuf", [128, 16], U16),
    "PI": ("sbuf", [128, 4], I32), "PC": ("sbuf", [128, 8], F32), "IF": ("sbuf", [128, 256], F32),
    "J16": ("sbuf", [128, H], F32), "R": ("sbuf", [128, 256], F32), "ET": ("sbuf", [128, 1032], F32),
    "M16": ("sbuf", [128, 128], F32), "WD": ("sbuf", [128, 144], BF), "BO": ("sbuf", [128, 128], BF), "BH": ("sbuf", [128, 128], F16),
    "BT": ("sbuf", [128, 128], BF), "TI": ("sbuf", [128, 128], BF), "TG": ("sbuf", [128, 128], BF), "TX": ("sbuf", [128, 128], BF),
    "IK": ("sbuf", [128, 128], BF), "IH": ("sbuf", [128, 128], F16), "ONE": ("sbuf", [128, 256], BF), "IM": ("sbuf", [128, 256], F32),
    "MB": ("sbuf", [128, U], F32), "RS": ("sbuf", [128, 192], BF), "ZM": ("sbuf", [128, 128], F32), "CR": ("sbuf", [128, 40], F32),
    "JK": ("sbuf", [128, 40], F32), "J12": ("sbuf", [128, 12], F32), "K1": ("sbuf", [128, 16], F32),
    "C1": ("sbuf", [128, 16], F32), "TH0": ("sbuf", [128, 40], F32), "THS": ("sbuf", [128, 8], F32),
    "QT": ("sbuf", [128, 4], F32), "SEL": ("sbuf", [128, 144], BF), "CT": ("sbuf", [128, 400], F32),
    "TS": ("sbuf", [128, 8 * RO], F32),
    "YF": ("sbuf", [128, 640], F32),
    "LL": ("sbuf", [128, RO * H], F32), "LR": ("sbuf", [128, RO * H], F32), "LT": ("sbuf", [128, 8 * RO], F32),
    "LU": ("sbuf", [128, H], BF),
}
for _t in range(RO):
    SCRATCH["TW%d" % _t] = ("sbuf", [128, DW], F32)
for _t in range(1, RO):
    SCRATCH["L%d" % _t] = ("sbuf", [128, DW], F32)
for _t in range(2, RO):
    SCRATCH["M%d" % _t] = ("sbuf", [128, DW], F32)
for _b in range(8):
    SCRATCH["P%d" % _b] = ("psum", [128, 512], F32)

SEMAPHORES = (["qv", "qa", "qp", "qg", "ls"] + ["dma%d" % i for i in range(20)]
              + [n + str(t) for t in range(RO) for n in ("al", "ar", "at", "ld")])


def relays(T, topo, rank):
    n = len(T.cores); me = T.cores[rank]; left, right = T.cores[(rank - 1) % n], T.cores[(rank + 1) % n]
    able = [c for c in topo.cores_of(me) if c != me and topo.may_write(c, left) and topo.may_write(c, right)]
    near = [c for c in able if topo.die(c) == topo.die(me)]; other = [c for c in able if topo.die(c) != topo.die(me)]
    return near[0], other[0], near[1]


def mask_of(engines):
    m = 0
    for e in engines:
        m |= 1 << e
    return m


def first_hop(engines, t):
    h = len(engines) // 2
    if t == 0 and E0: return engines[1:h:2], engines[0:h:2], engines[h:]
    return engines[1::2], engines[0::2], engines[1::2]


def touch_piece(T, t):
    return T.LT[:, 8 * t:8 * t + 8] if t < RO - 1 else T.LU[:]


def relay_program(g, core, T, topo):
    n = len(T.cores)
    for rank in range(n):
        roles = relays(T, topo, rank)
        if core not in roles:
            continue
        role = roles.index(core)
        dst = T.cores[(rank - 1) % n] if role == 0 else T.cores[(rank + 1) % n]
        buf, sem = (("LR", "ar"), ("LL", "al"), ("LT", "at"))[role]
        rid, pid = topo.addr(dst, core); m = topo.mask(core, dst); k = len(topo.engines(core, dst))
        for t in range(RO):
            piece = T[buf][:, t * H:(t + 1) * H] if role < 2 else touch_piece(T, t)
            g.wait_ge(T.sem[sem + str(t)], len(first_hop(topo.engines(T.cores[rank], core), t)[role]))
            g.remote_dma(piece, piece, T.sem[sem + str(t)], T.sem.ls, pid, rid, m)
        g.wait_ge(T.sem.ls, k * RO)


def emit(g, T, ops):
    queue = {"v": g.vector, "a": g.scalar, "p": g.tensor, "g": g, "s": g.sync}
    last_w, readers, deps = {}, {}, []
    for i, (eng, fn, rd, wr, sem) in enumerate(ops):
        d = set()
        own = lambda j: ops[j][0] == eng and ops[j][4] is None and sem is None
        for k in rd:
            if k.lstrip("~") in last_w: d.add(last_w[k.lstrip("~")])
            if k[0] == "#":
                d.update(j for j in readers.get(k, ()) if not own(j))
        for k in wr:
            if k in last_w and not (k[0] == "#" and own(last_w[k])): d.add(last_w[k])
            d.update(readers.get(k, ()))
        for k in rd: readers.setdefault(k, []).append(i)
        for k in wr:
            last_w[k] = i; readers[k] = []
        deps.append(d)
    line = lambda j: ops[j][0] if ops[j][4] is None else "x%d" % j
    clock, known, waits = {}, {}, []
    for i, (eng, fn, rd, wr, sem) in enumerate(ops):
        kn = known.setdefault(eng, {}) if eng != "x" else {}; w = []
        top = {}
        for j in deps[i]:
            if top.get(line(j), -1) < j: top[line(j)] = j
        for j in sorted(top.values(), reverse=True):
            if kn.get(line(j), -1) >= j: continue
            w.append(j)
            for k, x in clock[j].items():
                if kn.get(k, -1) < x: kn[k] = x
        waits.append(w)
        c = dict(kn); c[line(i)] = i; clock[i] = c
    needed = set(j for w in waits for j in w)
    count, value = {}, {}
    for i, (eng, fn, rd, wr, sem) in enumerate(ops):
        if sem is not None: value[i] = sem
        elif i in needed:
            count[eng] = count.get(eng, 0) + 1; value[i] = ("q" + eng, count[eng])
    for i, (eng, fn, rd, wr, sem) in enumerate(ops):
        if eng == "x": continue
        for j in waits[i]: queue[eng].wait_ge(T.sem[value[j][0]], value[j][1])
        if fn is None: continue
        r = fn()
        if sem is not None: r.then_inc(T.sem[sem[0]], sem[1])
        elif i in needed: r.then_inc(T.sem[value[i][0]], 1)


def rank_program(g, core, T, topo):
    rank = T.rank_of(core)
    if rank is None:
        return relay_program(g, core, T, topo)
    n = len(T.cores)
    ops = []
    ndma = [0]
    rl, rrt, rt = relays(T, topo, rank)
    eng_chip = topo.engines(core, rl); half = len(eng_chip) // 2
    far = len(topo.engines(rl, T.cores[(rank - 1) % n]))
    v, a, pe = g.vector, g.scalar, g.tensor

    def op(eng, fn, rd, wr): ops.append((eng, fn, rd.split(), wr.split(), None))
    def dma(eng, out, in_, rd, wr):
        q = g.sync if eng == "s" else g.scalar
        ops.append((eng, lambda: q.dma_start(out, in_), rd.split(), wr.split(), ("dma%d" % ndma[0], 16))); ndma[0] += 1
    def arrival(sem, wr, k=far): ops.append(("x", None, [], [wr], (sem, k)))
    def cp(out, in_, rd, wr): op("v", lambda: v.tensor_copy(out, in_), rd, wr)
    def tt(out, x, y, o, rd, wr): op("v", lambda: v.tensor_tensor(out, x, y, o), rd, wr)
    def ts(out, x, s1, o0, rd, wr): op("v", lambda: v.tensor_scalar(out, x, s1, None, o0), rd, wr)
    def ts2(out, x, s1, o0, s2, o1, rd, wr): op("v", lambda: v.tensor_scalar(out, x, s1, s2, o0, o1), rd, wr)
    def scan(out, x, y, init, o0, o1, rd, wr): op("v", lambda: v.tensor_tensor_scan(out, x, y, init, o0, o1), rd, wr)
    def fill(ap, c, wr): op("v", lambda: v.memset(ap, c), "", wr)
    def act(out, in_, rd, wr, f=AF.Identity, **kw): op("a", lambda: a.activation(out, in_, f, **kw), rd, wr)
    def mm(out, l, r, st, sp, rd, wr): op("p", lambda: pe.matmul(out, l, r, st, sp), rd, wr)
    def iota(out, pat, base, cm, wr, whole=False):
        if whole: op("g", lambda: g.iota(out, pat, base, cm), "", wr)
        else: op("g", lambda: g.iota(out, pat, base, cm, allow_small_or_imprecise_dtypes=True), "", wr)
    def sel(out, in_, pat, o, base, cm, rd, wr, c=0.0): op("g", lambda: g.affine_select(out, in_, pat, o, c, base, cm), rd, wr)
    def names(s, xs): return " ".join(s % x for x in xs)
    P = [T["P%d" % b] for b in range(8)]
    W = lambda k: T.WD[:, 15 - k:143 - k]
    Dr = T.D[:, 0:JUNK]; DD = "Dl Dm Dr Dx"
    NL = 256 - P1
    acc = lambda j0, j1: T.ACC[:, 64 * j0 + 63:64 * j1:64]

    dma("s", T.B2[:, 0:256], T.b2[:, 0:256], "", "B2a")
    dma("a", T.B1[:, 0:256], T.b1[:, 0:256], "", "B1a")
    dma("s", T.D[0:64, 0:V], T.dist[0:64, :], "", "Dl Dm Dr")
    dma("a", T.D[64:128, 0:V], T.dist[64:128, :], "", "Dn")
    dma("s", T.B2[:, 256:U], T.b2[:, 256:U], "Dm Dn", "B2c")
    dma("s", T.B1[:, 256:U], T.b1[:, 256:U], "", "B1c")
    dma("s", T.B2[:, U:1024], T.b2[:, 0:384], "", "B2d")
    dma("s", T.B1[:, U:1024], T.b1[:, 0:384], "", "B1d")
    BB1, BB2 = "B1a B1c B1d B1x", "B2a B2c B2d B2x"

    iota(T.PI[:, 0:1], [[0, 1]], 0, 1, "PI", whole=True)
    iota(T.CR[:], [[16, 40]], 0, 0, "CR")
    iota(T.R[:, 0:256], [[1, 256]], 0, 0, "R0")
    iota(T.M16[:], [[16, 8], [0, 16]], 0, 0, "M16")
    iota(T.J16[:], [[0, 8], [1, 16]], 0, 0, "J16")
    iota(T.FQ[:], [[2, 2], [64, 4]], 1, 0, "FQ")
    fill(T.ONE[:], 1.0, "ONE")
    act(T.L1[:, 0:256], T.ONE[:], "ONE", "L1", f=AF.Sigmoid, scale=(1024 - 512) / 8192)
    ts(T.PI[:, 2:3], T.PI[:, 0:1], 15, A.bitwise_and, "PI", "PJ0")
    ts(T.PI[:, 3:4], T.PI[:, 0:1], 112, A.bitwise_and, "PI", "PJ1")
    fill(T.D[:, V:JUNK], 1e9, "Dx")
    cp(T.PC[:, 0:2], T.PI[:, 2:4], "PJ0 PJ1", "PC")
    fill(T.NF[:, 16:40], 0.0, "NFa")
    rr, gg = T.PC[:, 0:1], T.PC[:, 1:2]
    ts(T.CR[:], T.CR[:], rr, A.add, "CR PC", "CR")
    ts2(T.PC[:, 2:3], rr, -ALPHA, A.mult, U0, A.add, "PC", "PC2")
    ts(T.PC[:, 3:4], gg, 15.0, A.add, "PC", "PC3")
    ts(T.PC[:, 7:8], rr, 4.0, A.mult, "PC", "PC7")
    ts2(T.PC[:, 6:7], rr, 15.5 - KT, A.is_gt, 8 * 17 * ALPHA, A.mult, "PC", "PC6")
    ts2(T.IF[:, 0:128], T.R[:, 0:128], gg, A.subtract, rr, A.is_equal, "R0 PC", "IF")
    ts2(T.WD[:], T.R[:, 0:144], T.PC[:, 3:4], A.is_equal, 0.0625, A.mult, "R0 PC3", "WD")
    ts2(T.IH[:], T.R[:, 0:128], gg, A.subtract, rr, A.is_equal, "R0 PC", "IH")
    ts(T.IF[:, 128:256], T.IF[:, 0:128], -1.0, A.mult, "IF", "NI")
    ts(T.PC[:, 4:5], T.PC[:, 6:7], T.PC[:, 2:3], A.add, "PC2 PC6", "PC4")
    ts2(T.PC[:, 5:6], T.PC[:, 6:7], -1.0, A.mult, 16 * 17 * ALPHA, A.add, "PC6", "PC5")
    ts(T.BH[:], T.M16[:], gg, A.is_equal, "M16 PC", "BH")
    ts2(T.BT[:], T.M16[:], gg, A.is_equal, 0.390625, A.mult, "M16 PC", "BT")
    ts(T.BO[:], T.M16[:], gg, A.is_equal, "M16 PC", "BO")
    ts(T.IM[:, 0:H], T.J16[:], rr, A.is_equal, "J16 PC", "IM0")
    ts2(T.ZM[:], T.J16[:], rr, A.is_ge, float(NONE), A.mult, "J16 PC", "ZM")
    ts(T.FQ[:], T.FQ[:], T.PC[:, 7:8], A.add, "FQ PC7", "FQ")
    cp(T.O2[:], T.B2[:, 0:256], "B2a", "O20 O21 O22 O23")
    cp(T.O1[:], T.B1[:, 0:256], "B1a", "O10 O11 O12 O13")
    zm = " ZM"
    sel(T.QT[:], T.R[:, 0:4], [[0, 4]], A.is_gt, 0, 0, "R0", "QT", 0.25)
    iota(T.OO[:], [[0, 8]], 128, 0, "OO")
    for f in range(3): iota(T.TR0[:, f * TW_:f * TW_ + 128], [[0, 128]], NONE, 0, "TRo0%d" % f)
    iota(T.TR0[:, 384::TW_], [[0, 3]], NONE, 0, "TRx0"); iota(T.TR1[:, 384::TW_], [[0, 3]], NONE, 0, "TRx1")
    for b0, b1 in ((1, 2), (3, 5), (6, 7)): iota(T.ZM[:, 16 * b0:16 * b1], [[0, 16 * (b1 - b0)]], 0, 0, "ZM")
    iota(T.NZ[:, 64:128], [[0, 64]], 0, 0, "NZo0"); iota(T.NZ[:, 192:256], [[0, 64]], 0, 0, "NZo1")
    iota(T.F[:, 16:40], [[0, 24]], 1, 0, "Fa"); iota(T.KP[:], [[0, 40]], 1, 0, "KPa KPb KPc")
    for s in "abc": iota(T["SS" + s][:, 0:1], [[0, 1]], 0, 0, "SS%s0" % s)

    iota(T.TR0[:, 128:384], [[1, 256]], 0, 0, "TRn00 TRn01")
    act(T.J12[:], T.CR[:, 0:12], "CR", "J12", bias=float(JUNK))
    for c0, m in ((0, H), (H, 64)):
        act(T.RS[:, c0:c0 + m], T.J16[:, 0:m], "J16", "RS%d" % c0, f=AF.Sign)
        act(P[0][:, 256 + c0:256 + c0 + m], T.IM[:, 0:m], "IM0", "#0", scale=8192.0)
    act(T.FB[:], T.FQ[:], "FQ", "FB", scale=20.0)
    def ring_constants():
        act(T.TH0[:], T.CR[:], "CR", "TH0", f=AF.Sigmoid, scale=1.0 / 8192, bias=0.5 / 8192)
        act(T.THS[:], T.CR[:, 0:8], "CR", "THS", f=AF.Sigmoid, scale=1.0 / 8192, bias=(V - H + 0.5) / 8192)
        for c0 in (0, H): act(T.MB[:, c0:c0 + H], T.IM[:, 0:H], "IM0", "MB%d" % c0, scale=4096.0)
        act(T.JK[:], T.CR[:], "CR", "JK", bias=float(U))
        act(T.LG[:, H:256], T.R[:, H:256], "R0", "LGa", scale=1.0 / 8192, bias=-512.0 / 8192)
        act(T.C1[:], T.CR[:, 0:16], "CR", "C1", bias=1.0)
    def list_constants():
        act(T.IM[:, H:256], T.IM[:, 0:H], "IM0", "IM")
        act(T.CT[:, 0:265:264], T.ONE[:, 0:2], "ONE", "CT0", f=AF.Sigmoid, scale=(1024 - 512) / 8192)
        act(T.CT[:, 265:393], T.ET[:, 512:U], "ET", "CT1", f=AF.Sigmoid, scale=1.0 / 8192, bias=-512.0 / 8192)
        act(T.CT[:, 1:257], T.ET[:, 256:512], "ET CT0 CT1", "CT", f=AF.Sigmoid, scale=1.0 / 8192, bias=-512.0 / 8192)
        act(T.K1[:, 0:8], T.CR[:, 0:8], "CR", "K1", scale=-1.0, bias=384.0)
        act(T.K1[:, 8:16], T.CR[:, 0:8], "CR", "K2", bias=-256.0)
        act(T.MB[:, 256:384], T.IM[:, 0:H], "IM0", "MB256", scale=4096.0)

    def ones(t):
        TW = T["TW%d" % t]; m = 256 if t == 0 else U
        iota(TW[:, 0:m], [[0, m]], 1, 0, "TW%d" % t); iota(TW[:, V - H:V], [[0, H]], 1, 0, "TW%d" % t)
    def blank(name, tok): sel(T[name][:, 0:264], T.ET[:, 0:264], [[0, 264]], A.is_gt, 0, 0, "ET", tok, code(1024))
    ones(0)
    sel(T.TI[:], T.BO[:], [[1, 128]], A.is_ge, 0, -1, "BO", "TI")
    sel(T.TG[:], T.BO[:], [[-1, 128]], A.is_gt, 0, 1, "BO", "TG")
    iota(T.TX[:], [[0, 128]], -1, 0, "TX"); iota(T.FW[:, 8:9], [[0, 1]], 0, 0, "FS0")
    sel(T.TX[:], T.TX[:], [[-1, 128]], A.is_equal, 0, 1, "TX", "TX")
    iota(T.IK[:], [[0, 128]], -384, 0, "IK")
    sel(T.IK[:], T.IK[:], [[-1, 128]], A.is_equal, 0, 1, "IK", "IK")
    iota(T.ET[:, 0:U], [[1, U]], 0, 0, "ET"); iota(T.ET[:, U:1032], [[1, 392]], 0, 0, "ET")
    iota(T.LG[:, 256:1024], [[1, 768]], -256, 0, "LG")
    iota(T.B1[:, 1024:1032], [[0, 8]], NONE, 0, "B1x", whole=True); iota(T.B2[:, 1024:1032], [[0, 8]], NONE, 0, "B2x", whole=True)

    def late_constants(t):
        if t + 1 < RO: ones(t + 1)
        if 1 <= t < RO - 1: blank("L%d" % (t + 1), "L%d" % (t + 1)); blank("M%d" % (t + 1), "M%d" % (t + 1))
        if t == 2:
            sel(T.SEL[:], T.ONE[:, 0:144], [[-1, 144]], A.is_equal, 0, 1, "ONE", "SEL")

    lower = (rank < (rank - 1) % n, rank < (rank + 1) % n)
    sides = ((0, "Dl", "LL"), (V - H, "Dr", "LR"))
    q4 = lambda e0, e1: range(e0 // 64, (e1 + 63) // 64)

    def o2(e0, e1): cp(T.O2[:, e0:e1], T.B2[:].indirect(T.VL[:, e0 // 16:e1 // 16]), BB2 + " VL%d VL%d" % (e0 // H, (e1 - 1) // H), names("O2%d", q4(e0, e1)))
    def o1(e0, e1): cp(T.O1[:, e0:e1], T.B1[:].indirect(T.VL[:, e0 // 16:e1 // 16]), BB1 + " VL%d VL%d" % (e0 // H, (e1 - 1) // H), names("O1%d", q4(e0, e1)))
    def numbers(e0=0, e1=256):
        cp(P[1][:, e0:e1], T.O1[:, e0:e1], names("O1%d", q4(e0, e1)), "#1")
        cp(P[1][:, 256 + e0:256 + e1], T.O2[:, e0:e1], names("O2%d", q4(e0, e1)), "#1")
    def decode(e0, e1):
        ts2(T.VL[:, e0 // 16:e1 // 16], T.LW[:, e0 + 15:e1:16], SLOPE, A.mult, 512.25 - SLOPE / 2, A.add, "LW", names("VL%d", range(e0 // H, e1 // H)))
    def own_numbers(e0):
        c = e0 // 16
        return [lambda: ts2(T.EA[:, c:16], T.LW[:, e0 + 15::16], code(U - 0.5), A.is_gt, -U / SLOPE, A.mult, "LW", "EA"),
                lambda: tt(T.EB[:, c:16], T.EA[:, c:16], T.LW[:, e0 + 15::16], A.add, "EA LW", "EB"),
                lambda: ts2(T.EL[:, c:16], T.EB[:, c:16], SLOPE, A.mult, 512.25 - SLOPE / 2, A.add, "EB", "EL")]
    def ranks_of(s, c0, c1, ftok):
        m = c1 - c0
        scan(T["SS" + s][:, 1:1 + m], T.ONE[:, 0:m], T.F[:, c0:c1], 0.0, A.mult, A.add, "ONE " + ftok, "SS" + s)
    def places(s, c0, c1, ntok):
        m = c1 - c0; SS = T["SS" + s]; o = P[5][:, c0:c1]
        mm(o, T.TI[:], SS[:, 1:1 + m], True, False, "TI SS" + s, "#5")
        mm(o, T.TG[:], SS[:, 0:m], False, False, "TG SS%s SS%s0" % (s, s), "#5")
        mm(o, T.IH[:], T.NF[:, c0:c1], False, True, "IH " + ntok, "#5")
    na, nab = P[5][:, 40:41], P[3][:, 508:509]

    def piece_b(t, e0):
        s0 = 8 * (t + 1); his = T.LT[:, 8 * t:8 * t + 8]; L, M = T["L%d" % (t + 1)], T["M%d" % (t + 1)]; c = e0 // 16
        def s1():
            tt(T.F[:, 0:8], his, T.FO[:], A.max, "LT%d FO" % t, "Fb")
            tt(T.FN[:, 0:8], his, T.GB[:], A.is_lt, "LT%d GB" % t, "FNb")
        def s2():
            ranks_of("c", 0, 8, "Fb")
            tt(T.NF[:, 0:8], T.FN[:, 0:8], T.JK[:, 0:8], A.mult, "FNb JK", "NFb")
            places("c", 0, 8, "NFb")
            mm(nab, T.BO[:], T.SSa[:, 40 - s0:41 - s0], True, False, "BO SSa", "#3")
            mm(nab, T.BO[:], T.SSc[:, 8:9], False, True, "BO SSc", "#3")
        def s3():
            ts2(T.PL[:, 0:8], P[5][:, 0:8], na, A.add, -1.0, A.add, "#5", "PLb")
            act(L[:].indirect(T.PL[:, 0:8]), T.LG[:, U:U + H], "PLb LG", "L%d" % (t + 1), f=AF.Sigmoid)
            ts(T.OFF[:, c:16], T.C1[:, c:16], nab, A.subtract, "C1 #3", "OFF")
        def s4(): tt(T.LS[:, e0:256], M[:, 0:264].indirect(T.OFF[:, c:16]), T.IM[:, e0:256], A.mult, "M%d OFF IM0 IM" % (t + 1), "LS")
        def s5(): scan(T.LW[:, e0:256], T.LS[:, e0:256], L[:, e0:256], 0.0, A.max, A.min, "LS L%d" % (t + 1), "LW")
        return [s1, s2, s3, s4, s5, lambda: decode(e0, 256)]
    def unflag(t):
        s0 = 8 * (t + 1)
        if t == 0:
            st = [lambda: tt(T.F[:, 0:8], T.LT[:, 0:8], T.FO[:], A.max, "LT0 FO", "Fb")]
        else:
            st = [lambda: ts2(T.KP[:, 0:8], P[5][:, 0:8], na, A.add, 256.5, A.is_gt, "#5", "KPb"),
                  lambda: ts2(T.KP[:, 8:s0], P[5][:, 8:s0], nab, A.add, 256.5, A.is_gt, "#5 #3", "KPc")]
        st.append(lambda: tt(T.FK[:], T.F[:], T.KP[:], A.mult, "Fa Fb Fc KPa KPb KPc", "FK"))
        if t + 2 < RO: st.append(lambda: tt(T.THR[:], T.FK[:], T.TH0[:], A.max, "FK TH0", "THR"))
        else: st.append(lambda: ts(T.KP[:], T.FK[:], 0.75, A.add, "FK", "KPa KPb KPc"))
        return st
    def fix(t, s):
        c0, tok, land = sides[s]
        tt(T.D[:, c0:c0 + H], P[0][:, s * H:(s + 1) * H], T[land][:, t * H:(t + 1) * H], A.add, "#0 %s%d sent%d" % (land, t, t), tok)

    late = []
    spare = []
    def one():
        if late: late.pop(0)()

    for t in range(RO):
        par = t % 2; TR, TRn = T["TR%d" % par], T["TR%d" % (1 - par)]; TW = T["TW%d" % t]
        DX = DD + (" Dn" if t == 0 else "")
        last = t == RO - 1
        new = lambda f, e0, e1: TR[:, f * TW_ + 128 + e0:f * TW_ + 128 + e1]
        tri = lambda f, par=par: "TRo%d%d TRx%d TRn%d0 TRn%d1" % (par, f, par, f, f)

        def g2(e0, e1, eng="a"):
            (cp if eng == "v" else act)(T.G2[:, 16 * e0:16 * e1], Dr.indirect(T.O2[:, e0:e1]), DX + " " + names("O2%d", q4(e0, e1)), "G2%d" % e0)
        def add(e0, e1):
            tt(T.S[:, 16 * e0:16 * e1], Dr.indirect(T.O1[:, e0:e1]), T.G2[:, 16 * e0:16 * e1], A.add,
               DX + " G2%d " % e0 + names("O1%d", q4(e0, e1)), "S%d" % e0)
        cuts = CUTS[t]
        chunks = list(zip(cuts, cuts[1:]))
        def compare(e0, e1, bank, mid={}):
            c0 = 16 * e0
            for k in range(16):
                if k in mid: mid[k]()
                x = H if e0 == 0 and k >= 16 - KT else e0; m = e1 - x
                if x > e0 and k == 16 - KT: c0 += H * KT
                cm = T.CM[:, c0:c0 + m]; tok = "CM%d_%d" % (e0, k); c0 += m
                js = [] if e0 else at[k]; n_mm[0] += 1 if m else 0; total = 16 + (KT if e0 == 0 and P1 > H else 0)
                if k == 0: n_mm[0] = 1
                if m:
                    tt(cm, P[0][:, x:e1], T.S[:, 16 * x + k:16 * e1:16], A.is_gt, "#0 " + names("S%d", [y for y in cuts if x <= y < e1]), tok)
                    mm(P[bank][:, x - e0:e1 - e0], W(k), cm, k == 0, n_mm[0] == total, "WD " + tok, "#%d" % bank)
                for j in js:
                    n_mm[0] += 1
                    mm(P[bank][:, 0:H], W(16 - KT + j), T.CM[:, sg + H * j:sg + H * (j + 1)], False, n_mm[0] == total,
                       "WD CS%d" % (j // 4), "#%d" % bank)
            if 16 in mid: mid[16]()
        n_mm = [0]
        at = [[j for j in range(KT) if min(15, K0 + j) == k] for k in range(16)]
        banks = (6, 7, 4); sg = P1 * (16 - KT)
        def owns(src, tok):
            for j in range(KT):
                b = banks[j // 4]; c0 = H * (j % 4)
                mm(P[b][:, c0:c0 + H], T.IF[:, 0:128], src[:, 0:H], j % 4 == 0, False, "IF " + tok, "#%d" % b)
        def sums(e0, e1):
            s = names("S%d", [x for x in cuts if e0 <= x < e1])
            for j in range(KT):
                b = banks[j // 4]; c0 = H * (j % 4); k = 16 - KT + j
                mm(P[b][:, c0 + e0:c0 + e1], T.IF[:, 128:256], T.S[:, 16 * e0 + k:16 * e1:16], False,
                   e1 == H and (j % 4 == 3 or j == KT - 1), "NI " + s, "#%d" % b)
        def signs(h):
            m = H * min(4, KT - 4 * h)
            act(T.CM[:, sg + 4 * H * h:sg + 4 * H * h + m], P[banks[h]][:, 0:m], "#%d" % banks[h], "CS%d" % h, f=AF.Sign, scale=2.0 ** 60, bias=-2.0 ** -100)
        def de(lst, e0, e1, tok, eng):
            x = Dr.indirect(lst[:, e0 // 16:e1 // 16])
            (cp if eng == "v" else act)(T.DE[:, e0:e1], x, DX + " " + tok, "DE%d" % e0)
        def de_psum(toks): act(P[0][:, 0:256], T.DE[:], toks, "#0")

        first = [c for c in chunks if c[0] < P1]; second = chunks[len(first):]
        def added(c):
            add(*c)
            if c[1] == 64: sums(0, 64)
            if c[1] == H: sums(64, H)
        if t == 0:
            numbers(); g2(*first[0], "v"); owns(T.D, DX); cp(P[0][:, 0:H], T.D[:, 0:H], DX, "#0")
            for i, c in enumerate(first):
                if i: g2(*c)
                added(c)
        if t == 1:
            g2(*first[0], "v"); de(T.VL, 0, H, "VL0", "v"); owns(T.DE, "DE0")
            for i, c in enumerate(first):
                if i: g2(*c)
                added(c)
                if i == 0: cp(P[0][:, 0:H], T.DE[:, 0:H], "DE0", "#0")
        if t == 2:
            st = piece_b(1, H); own = own_numbers(H)
            g2(*first[0]); st[0](); de(T.VL, 0, H, "VL0", "v"); st[1]()
            owns(T.DE, "DE0"); o1(0, H)
            g2(*first[1]); add(*first[0]); st[2](); st[3](); add(*first[1]); g2(*first[2]); st[4](); g2(*first[3])
            added(first[2]); st[5](); own[0](); o2(H, 256); own[1](); o1(H, 256); own[2]()
            add(*first[3]); g2(*first[4])
            added(first[4])
        if t == 3:
            own = own_numbers(0)
            own[0](); o2(0, 64); g2(*first[0]); own[1](); o1(0, 64); own[2](); o2(64, 256)
            for i, c in enumerate(first):
                if i: g2(*c)
                if i == 1: de(T.EL, 0, H, "EL", DE3); owns(T.DE, "DE0")
                added(c)
                if i == 0: o1(64, 256)
        def own_psum(h):
            e0 = H * h
            if t == 0: return act(P[0][:, e0:e0 + H], T.D[:, e0:e0 + H], DX, "#0")
            if h: de(T.VL if t == 1 else T.EL, H, 256, "VL1" if t == 1 else "EL", "a")
            act(P[0][:, e0:e0 + H], T.DE[:, e0:e0 + H], "DE%d" % e0, "#0")
        late_constants(t)

        def weigh(h, e0, e1, nb, sb, mid=lambda: None):
            m = e1 - e0
            if h: act(T.VV[:, e0:e1], P[nb][:, 0:m], "#%d PC2" % nb, "VV1", f=AF.Sigmoid, bias=T.PC[:, 2:3], scale=16 * 17 * ALPHA)
            else:
                act(T.VV[:, 0:H], P[nb][:, 0:H], "#%d PC4 PC5" % nb, "VVs", f=AF.Sigmoid, bias=T.PC[:, 4:5], scale=T.PC[:, 5:6])
                if m > H: act(T.VV[:, H:m], P[nb][:, H:m], "#%d PC2" % nb, "VV0", f=AF.Sigmoid, bias=T.PC[:, 2:3], scale=16 * 17 * ALPHA)
            mid()
            mm(P[sb][:, 0:m], T.BT[:], T.VV[:, e0:e1], True, True, "BT VVs VV%d" % h, "#%d" % sb)
        def choose(h, e0, e1, sb):
            m = e1 - e0
            need = 0.390625 * 0.92 * math.exp(U0 + 138 * ALPHA)
            if h or PFV: ts2(T.PF[:, e0:e1], P[sb][:, 0:m], need, A.is_gt, 2.0, A.mult, "#%d" % sb, "PF%d" % h)
            else:
                mm(P[4][:, 0:m], T.BT[:], T.VV[:, e0:e1], True, True, "BT VVs VV0", "#4")
                act(T.PF[:, e0:e1], P[4][:, 0:m], "#4", "PF0", f=AF.Sign, bias=-need)
        def winner(h, e0, e1, sb):
            tt(T.WIN[:, e0:e1], T.VV[:, e0:e1], P[sb][:, 0:e1 - e0], A.is_gt, "VVs VV%d #%d" % (h, sb), "WIN%d" % h)
        def ranks(h, e0, e1):
            scan(T.PR[:, e0:e1], T.ONE[:, 0:e1 - e0], T.PF[:, e0:e1], T.PR[:, e0 - 1:e0] if h else 0.0, A.mult if h or PFV else A.add, A.add,
                 "ONE PF%d" % h + (" PR0" if h else ""), "PR%d" % h)
        def pick(f, h, e0, e1, bank):
            Wf = T.WB if f == 1 else T.WC; c0 = 256 * (f - 1)
            tt(Wf[:, e0:e1], T.WIN[:, e0:e1], P[1][:, c0 + e0:c0 + e1], A.mult, "WIN%d #1" % h, "W%d%d" % (f, h))
            mm(P[bank][:, c0 + e0:c0 + e1], T.BH[:], Wf[:, e0:e1], True, True, "BH W%d%d" % (f, h), "#%d" % bank)
        def count(e0, e1, col, to, rd):
            act(T.TRASH[:, 256 * to:256 * to + e1 - e0], T.PR[:, e0:e1], rd + " FB", "ACC%d" % to, f=AF.Sigmoid, bias=T.FB[:, col:col + 1], scale=-20.0,
                accum_out=acc(to, to + 1))

        for i, c in enumerate(second):
            if i == 0 and t >= 2: own_psum(0)
            g2(*c)
            if i == SA:
                for h in range((KT + 3) // 4): signs(h)
            if i == SB: compare(0, P1, 2)
            add(*c)
        own_psum(1)
        weigh(0, 0, P1, 2, 3)
        def first_ranks():
            ranks(0, 0, P1)
            for c in range(4): count(0, P1, 4 * par + c, 8 + c, "PR0")
        if spare: spare.pop(0)(); spare.pop(0)()
        choose(0, 0, P1, 3)
        if t: act(new(0, 0, 256), T.ET[:].indirect(T.VL[:]), "ET VL0 VL1", "TRn00 TRn01")
        compare(P1, 256, 6, {KB: first_ranks})
        if spare: spare.pop(0)()
        weigh(1, P1, 256, 6, 7)
        if t >= 2: numbers(0, P1)
        winner(0, 0, P1, 3)
        one()
        pick(1, 0, 0, P1, 4); pick(2, 0, 0, P1, 2)
        act(new(1, 0, P1), P[4][:, 0:P1], "#4", "TRn10")
        act(new(2, 0, P1), P[2][:, 256:256 + P1], "#2", "TRn20")
        one()
        if t >= 2: numbers(P1, 256)
        choose(1, P1, 256, 7); winner(1, P1, 256, 7)
        tt(T.OV[:], T.OO[:, 4 * par:4 * par + 4], acc(8, 12), A.add, "OO ACC8 ACC9 ACC10 ACC11", "OV")
        ranks(1, P1, 256)
        for c in range(4 - CV): count(P1, 256, 4 * par + c, 4 * par + c, "PR1")
        pick(1, 1, P1, 256, 4)
        for c in range(4 - CV, 4):
            ts(T.E3[:, NL * c:NL * c + NL], T.PR[:, P1:256], T.FQ[:, 4 * par + c:4 * par + c + 1], A.is_lt, "PR1 FQ", "E3%d" % (c % 3))
        pick(2, 1, P1, 256, 2)
        for c in range(4 - CV, 4):
            j = 4 * par + c
            scan(T.ACC[:, 64 * j:64 * j + 64], T.E3[:, NL * c:NL * c + 64], T.E3[:, NL * c + 64:NL * c + NL], 0.0, A.add, A.add,
                 "E3%d" % (c % 3), "ACC%d" % j)
        one()
        for i, (c, (p0, p1, st)) in enumerate(((0, (0, 1, 1)), (0, (5, 12, 3)), (2, (2, 11, 4)), (3, (3, 10, 6)), (1, (1, 8, 3)))):
            m = len(range(p0, p1, st)); col = 4 * par + c
            ts2(T.SL[:, p0:p1:st], T.QT[:, 0:m], acc(col, col + 1), A.add, T.OV[:, c:c + 1], A.add, "QT OV ACC%d" % col, "SL%d" % p0)
        act(new(1, P1, 256), P[4][:, P1:256], "#4", "TRn11")
        act(new(2, P1, 256), P[2][:, 256 + P1:512], "#2", "TRn21")
        one()
        if last:
            for c0, c1, bank in ((0, 8, 3), (8, 40, 2)):
                for r in range(16):
                    mm(P[bank][:, r:16 * (c1 - c0):16], T.SEL[:, r:r + 128], T.KP[:, c0:c1], r == 0, r == 15, "SEL KPa", "#%d" % bank)
        sl = " SL0 SL5 SL1 SL2 SL3"
        win = lambda f, TR=TR: TR[:, f * TW_:f * TW_ + 385]
        for f in range(3):
            act(T.ZC[:, 64 * f:64 * f + 64], win(f).indirect(T.SL[:, 0:4]), tri(f) + sl, "ZC%d" % f, scale=1.0 / 8192)
            tt(T.Z[:, f, :], win(f).indirect(T.SL[:, 4:12]), T.ZM[:], A.max, tri(f) + sl + zm, "Z%d" % f)
        nz = 128 * t
        if t >= 2: act(P[7][:, 128:192], T.NZ[:, nz + 64:nz + 128], "NZo%d" % t, "#7")
        if t == 0: ring_constants()
        while spare: spare.pop(0)()
        tt(T.XM[:], T.ZC[:], P[0][:, 256:448], A.mult, "ZC0 ZC1 ZC2 #0", "XM")
        one()
        scan(T.XW[:], T.RS[:], T.XM[:], 0.0, A.mult, A.add, "RS0 RS128 XM", "XW")
        one()
        cp(T.XL[:], T.XW[:, 15::16], "XW", "XL")
        act(T.DV[:], Dr.indirect(T.XL[:]), DX + " XL", "DV")
        act(P[7][:, 64:128], T.DV[:, 128:192], "DV", "#7")
        for s, (c0, tok, land) in enumerate(sides):
            if not lower[s]: act(T.D[:, c0:c0 + H], T.R[:, 0:H], "R0", tok, scale=0.0)
        if all(lower): DZ, dz = T.DV, "DV"
        else:
            DZ, dz = T.DZ, "DZ"
            act(T.DZ[:], Dr.indirect(T.XL[:]), DX + " XL", "DZ")
        def equal(c):
            b0, b1 = ((7, 8), (0, 2), (2, 5), (3, 7))[c]; m = 48 * (c + 1)
            for f in range(3):
                x = 64 * f + 16 * c + 15
                ts2(T["E%d" % c][:, f * m:(f + 1) * m], T.Z[:, :, 16 * b0:16 * b1], T.XW[:, x:x + 1], A.is_equal, 4096.0, A.mult,
                    "Z0 Z1 Z2 XW", "E%d%d" % (c, f))
        def fold(c):
            E = T["E%d" % c]; h = 72 * (c + 1)
            scan(T.ES[:, 288 * (c + 1) - h:288 * (c + 1)], E[:, 0:h], E[:, h:2 * h], 0.0, A.max, A.max, "E%d0 E%d1 E%d2" % (c, c, c), "ES%d" % c)
        def bad(c): ts(T.TB[:, c::4], T.J12[:, c::4], T.ES[:, 288 * c + 287:288 * c + 288], A.min, "J12 ES%d" % c, "TB%d" % c)
        DL = T.CO[:, 64:128]
        equal(3); equal(2); fold(3); equal(1); fold(2)
        tt(T.T1[:], T.DV[:, 0:64], T.DV[:, 64:128], A.subtract, "DV", "T1")
        equal(0)
        tt(T.T2[:], T.T1[:], P[7][:, 64:128], A.subtract, "T1 #7", "T2")
        fold(1); fold(0)
        if t < 2:
            ts2(DL, T.T2[:], 0.5, A.mult, 0.0, A.max, "T2", "DL"); bad(3); bad(2)
        else:
            ts(T.T1[:], T.T2[:], 0.5, A.mult, "T2", "T1"); bad(3); bad(2)
            tt(DL, T.T1[:], P[7][:, 128:192], A.max, "T1 #7", "DL")
        act(T.CO[:, 0:64], DL, "DL", "CO0", scale=-1.0); act(T.CO[:, 128:192], DL, "DL", "CO2")
        bad(1); bad(0)
        tb = "TB0 TB1 TB2 TB3"; TB = T.TB[:, 0:4]
        if t < 2: act(T.NZ[:, nz:nz + 64], DL, "DL", "NZc", scale=-1.0)
        else: tt(T.NZ[:, nz:nz + 64], P[7][:, 128:192], DL, A.subtract, "#7 DL", "NZc")
        one()
        tt(T.OF[:], T.TB[:], T.XW[:, 15::16], A.max, tb + " XW", "OF")
        ts2(T.I1[:], TB, 0.5, A.is_gt, 64.0, A.mult, tb, "I1")
        cp(T.OL[:], T.OF[:], "OF", "OL")
        if t < 2: ts(T.NZF[:], DL, 0.0, A.not_equal, "DL", "NZF")
        else: ts(T.NZF[:], T.NZ[:, nz:nz + 64], 0.0, A.not_equal, "NZc", "NZF")
        mm(P[6][:, 0:64], T.BO[:], T.NZF[:], True, True, "BO NZF", "#6")
        tt(T.D[:].indirect(T.OL[:]), DZ[:], T.CO[:], A.add, dz + " DL CO0 CO2 OL", DX)
        act(TW[:].indirect(T.OL[:]), T.ZC[:], "ZC0 ZC1 ZC2 OL", "TW%d" % t, f=AF.Sigmoid)
        trs = []
        mine = first_hop(eng_chip, t)
        for to, c0, land, sem, en in ((rl, 0, "LR", "ar", mine[0]), (rrt, V - H, "LL", "al", mine[1])):
            rid, pid = topo.addr(to, core)
            trs.append(RemoteDMATransfer(dst_ids=[DstId(rid=rid, pnc=pid)], dma_engine_mask=mask_of(en), remote_sem=T.sem[sem + str(t)],
                                         src=T.D[:, c0:c0 + H], dst=T[land][:, t * H:(t + 1) * H]))
        op("g", lambda trs=trs, t=t: g.remote_dma_fused(trs, local_sem=T.sem["ld%d" % t]), "~Dl ~Dr", "")
        def send_touches(src, tok, t=t, mine=mine):
            rid, pid = topo.addr(rt, core)
            op("g", lambda: g.remote_dma(touch_piece(T, t), src, T.sem["at%d" % t], T.sem.ls, pid, rid, mask_of(mine[2])), tok, "")
        arrival("at%d" % t, "LT%d" % t); arrival("al%d" % t, "LL%d" % t); arrival("ar%d" % t, "LR%d" % t); arrival("ld%d" % t, "sent%d" % t, len(mine[0]) + len(mine[1]))
        tw = "TW%d" % t
        while late: one()
        for s, (c0, tok, land) in enumerate(sides): act(P[0][:, s * H:(s + 1) * H], T.D[:, c0:c0 + H], tok, "#0")
        if t == 0: list_constants()
        for c in range(4): count(0, 256, 4 * (1 - par) + c, 4 * (1 - par) + c, "PR0 PR1")

        q = 4 * (1 - par)
        def keep(t=t, nz=nz):
            act(T.NZ[:, nz + 320:nz + 384], T.NZ[:, nz:nz + 128].indirect(T.IL[:]), "IL NZc NZo%d" % t, "NZo%d" % (t + 2))
        def back(fields=range(3), TRn=TRn, win=win, tri=tri, par=par):
            for f in fields:
                act(TRn[:, f * TW_:f * TW_ + 128], win(f).indirect(T.WL[:]), tri(f) + " WL", "TRo%d%d" % (1 - par, f))
        def free():
            scan(T.FW[:, 9:13], T.FW[:, 0:4], T.FW[:, 4:8], 0.0, A.add, A.add, "FW", "FS")
            for p in range(2):
                o = P[4][:, 4 * p:4 * p + 4]
                mm(o, T.TI[:], T.FW[:, 9:13], True, False, "TI FS", "#4")
                mm(o, T.TG[:], T.FW[:, 8:12], False, False, "TG FS FS0", "#4")
                if p == 0: mm(o, T.TX[:], T.FW[:, 4:8], False, False, "TX FW", "#4")
                mm(o, T.IK[:], T.FW[:, 4 * p:4 * p + 4], False, True, "IK FW", "#4")
        book = [lambda: tt(T.XM[:, 0:64], P[6][:, 0:64], T.IM[:, 0:64], A.mult, "#6 IM0", "XM"),
                lambda: tt(T.I2[:], T.I1[:], T.CR[:, 0:4], A.add, "I1 CR", "I2"),
                lambda: None,
                lambda: scan(T.T1[:], T.RS[:, 0:64], T.XM[:, 0:64], 0.0, A.mult, A.add, "RS0 XM", "T1"),
                lambda: cp(T.IL[:], T.I2[:], "I2", "IL"),
                lambda: tt(T.OF[:, 0:4], T.T1[:, 15::16], TB, A.add, "T1 " + tb, "OF"),
                lambda: tt(T.G1[:], acc(4 * par, 4 * par + 4), T.OV[:], A.add, "OV " + names("ACC%d", range(4 * par, 4 * par + 4)), "G1"),
                lambda: ts2(T.G3[:], T.OF[:, 0:4], 0.0, A.is_equal, 384.0, A.mult, "OF", "G3"),
                lambda: tt(T.SR[:, q:q + 4], acc(q, q + 4), T.OO[:, q:q + 4], A.add, "OO " + names("ACC%d", range(q, q + 4)), "SRa"),
                lambda: tt(T.SR[:, 4 * par:4 * par + 4], T.G1[:], T.G3[:], A.max, "G1 G3", "SRb"),
                lambda: ts(T.WL[:], T.SR[:], 0.25, A.add, "SRa SRb", "WL"),
                lambda: ts(T.FW[:, 0:8], T.SR[:], 383.5, A.is_gt, "SRa SRb", "FW"),
                free,
                lambda: tt(T.OO[:], T.FW[:, 0:8], T.K1[:, 0:8], A.mult, "FW K1", "OO"),
                lambda: tt(T.OO[:], T.OO[:], T.K1[:, 8:16], A.add, "OO K2", "OO")]
        def bounds():
            ts2(T.FQ[:], P[4][:, 0:8], 2.0, A.mult, 767.0, A.add, "#4", "FQ")
        def nxt(k=1):
            for _ in range(k): book.pop(0)()

        if not last:
            s0 = 8 * (t + 1); top = (16, 32, 40)[t]; end = (16, 40, 40)[t]; e1 = (256, H, 0)[t]
            thr, ttok = (T.TH0, "TH0") if t == 0 else (T.THR, "THR")
            L = T["L%d" % (t + 1)]; ltok = "L%d" % (t + 1); lg = "LGa" if t == 0 else "LG"
            def touched(x, c0, c1):
                scan(T.X[:, 16 * c0:16 * c1], T.MB[:, 0:16 * (c1 - c0)], TW[:, 16 * c0:16 * c1], 4096.0, A.max, A.min,
                     ("MB0 MB128 MB256 " if t else "MB0 ") + tw, "X" + x)
            def flags(x, y, c0, c1):
                tt(T.F[:, c0:c1], T.X[:, 16 * c0 + 15:16 * c1:16], thr[:, c0:c1], A.is_le, "X%s %s" % (x, ttok), "F" + y)
                tt(T.FN[:, c0:c1], T.X[:, 16 * c0 + 15:16 * c1:16], thr[:, c0:c1], A.is_gt, "X%s %s" % (x, ttok), "FN" + y)
            def far_touches(): scan(T.XS[:], T.MB[:, 0:H], TW[:, V - H:V], 4096.0, A.max, A.min, "MB0 " + tw, "XS")
            def send():
                tt(T.TS[:, 8 * t:8 * t + 8], T.XS[:, 15::16], T.THS[:], A.is_le, "XS THS", "TS%d" % t)
                send_touches(T.TS[:, 8 * t:8 * t + 8], "TS%d" % t)
            if e1: nxt(); touched("a", s0, top); far_touches(); flags("a", "a", s0, top); send(); nxt()
            else: far_touches(); nxt(); send(); touched("a", s0, top); nxt(); flags("a", "a", s0, top)
            ranks_of("a", s0, end, "Fa")
            tt(T.NF[:, s0:top], T.FN[:, s0:top], T.JK[:, s0:top], A.mult, "FNa JK", "NFa")
            places("a", s0, end, "NFa")
            mm(na, T.BO[:], T.SSa[:, end - s0:end - s0 + 1], True, True, "BO SSa", "#5")
            nxt(2); touched("b", 0, s0); nxt(2)
            ts(T.PL[:, s0:end], P[5][:, s0:end], -1.0, A.add, "#5", "PLa")
            act(L[:].indirect(T.PL[:, s0:top]), T.LG[:, 16 * s0:16 * top], "PLa " + lg, ltok, f=AF.Sigmoid)
            if e1:
                c = e1 // 16; tab = T.CT[:, 0:257] if t == 0 else T.CT[:, 264:393]
                ts2(T.OFF[:, 0:c], T.C1[:, 0:c], na, A.subtract, 16.0 * (end - top), A.add, "C1 #5", "OFF")
            ts(T.KP[:, s0:end], P[5][:, s0:end], 256.5, A.is_gt, "#5", "KPa")
            if t == 0: ts2(T.KP[:, 16:32], T.CR[:, 16:32], na, A.add, 511.5, A.is_gt, "CR #5", "KPc")
            else: flags("b", "c", 8, s0)
            nxt(2)
            tt(T.FO[:], T.X[:, 15:H:16], thr[:, 0:8], A.is_le, "Xb " + ttok, "FO")
            if t:
                ranks_of("b", 8, s0, "Fc")
                tt(T.NF[:, 8:s0], T.FN[:, 8:s0], T.JK[:, 8:s0], A.mult, "FNc JK", "NFc")
                places("b", 8, s0, "NFc")
            nxt(2)
            if e1: tt(T.LS[:, 0:e1], tab.indirect(T.OFF[:, 0:c]), T.IM[:, 0:e1], A.mult, "CT OFF IM0 IM", "LS")
            if t: ts2(T.GB[:], T.FO[:], -1.0, A.mult, 0.5, A.add, "FO", "GB")
            nxt(2)
            if t: cp(T.PL[:, 8:s0], P[5][:, 8:s0], "#5", "PLc")
            def rest():
                if t: act(T["M%d" % (t + 1)][:].indirect(T.PL[:, 8:s0]), T.LG[:, U + H:U + 16 * s0], "PLc LG", "M%d" % (t + 1), f=AF.Sigmoid)
                if top < end: act(L[:].indirect(T.PL[:, top:end]), T.LG[:, 16 * top:16 * end], "PLa LG", ltok, f=AF.Sigmoid)
            if e1:
                scan(T.LW[:, 0:e1], T.LS[:, 0:e1], L[:, 0:e1], 0.0, A.max, A.min, "LS " + ltok, "LW")
                rest(); nxt(2); decode(0, e1); nxt(); o2(0, e1)
                bounds()
                if t == 0: o1(0, e1); numbers(0, e1)
                act(T.FB[:], T.FQ[:], "FQ", "FB", scale=20.0)
                spare.extend([lambda f=f, back=back: back([f]) for f in range(3)] + [keep])
                if t == 0:
                    while spare: spare.pop(0)()
                    act(T.LG[:, 256:1024], T.LG[:, 256:1024], "LG", "LG", scale=1.0 / 8192)
                fix(t, 0); fix(t, 1)
            else:
                rest(); nxt(3); keep(); bounds()
                st = piece_b(t, 0)
                st[0](); st[1](); fix(t, 0); st[2](); back(); act(T.FB[:], T.FQ[:], "FQ", "FB", scale=20.0)
                st[3](); fix(t, 1); st[4](); st[5]()
            late.extend(unflag(t))
        else:
            nxt()
            ts(T.WIN[:, 0:H], TW[:, V - H:V], 0.75, A.is_lt, tw, "WIN0")
            send_touches(T.WIN[:, 0:H], "WIN0")
            dma("s", T.yd[:, H:V - H], T.D[:, H:V - H], "Dm sent%d" % t, "y0")
            iota(TR[:, 384::TW_], [[0, 3]], -1, 0, "TRx%d" % par)
            nxt(10); keep()
            tt(P[7][:, 0:H], TW[:, 0:H], P[3][:, 0:H], A.is_lt, tw + " #3", "#7")
            tt(T.YF[:, H:U], TW[:, H:U], P[2][:], A.is_lt, tw + " #2", "YFa")
            for f in range(3):
                for p in range(2):
                    act(T.X[:, 128 * f + p:128 * (f + 1):2], win(f).indirect(T.WL[:, 4 * p:4 * p + 4]), tri(f) + " WL", "YT%d%d" % (f, p))
            dma("s", T.yt[:], T.X[0::16, 0:384], "YT00 YT01 YT10 YT11 YT20 YT21", "y2")
            for p in range(2):
                act(T.M16[:, p::2], T.NZ[:, 128 * (4 + p) + 64:128 * (5 + p)], "NZo%d" % (4 + p), "YZ%d" % p, scale=-1.0)
            dma("s", T.yz[:], T.M16[:], "YZ0 YZ1", "y1")
            fix(t, 0); dma("s", T.yd[:, 0:H], T.D[:, 0:H], "Dl", "y3")
            fix(t, 1); dma("a", T.yd[:, V - H:V], T.D[:, V - H:V], "Dr", "y4")
            tt(T.YF[:, 0:H], T.LU[:], P[7][:, 0:H], A.max, "#7 LT%d" % t, "YFb")
            dma("s", T.yf[:], T.YF[0::16, :], "YFa YFb", "y5")
            op("s", None, "y0 y1 y2 y3 y4 y5", "")
    emit(g, T, ops)
    g.wait_ge(T.sem.ls, half * RO)
